import numpy as np, ml_dtypes
CORES = [40,41,42,43,44,45,46,47]
N = 8
BF = ml_dtypes.bfloat16
V, S, Q, RO, W = 1024, 4, 256, 6, 2304
def pack(res, cap, B, T, K, wt, ka):
    w = B + 4096 * T - 65536 * K
    return {"res": np.ascontiguousarray(res).reshape(N, 128, W).astype(np.float32).astype(BF), "cap": np.ascontiguousarray(cap).reshape(N, 128, V).astype(np.float32).astype(BF),
            "br": np.ascontiguousarray(w).reshape(N, 128, V).astype(np.int32), "wt": np.ascontiguousarray(wt).reshape(N, 128, 1).astype(np.int32), "ka": np.ascontiguousarray(ka).reshape(N, 128, 1).astype(np.int32)}
def parts(rng):
    sh = (N, 8, 16, V)
    res = (rng.integers(4, 29, (N, 8, 1, W)) * rng.random((N, 8, 16, W))).astype(np.int64)
    heavy = (rng.random((N, 8, 1, W)) < 0.06) & (rng.random((N, 8, 16, W)) < 0.7)
    res = np.where(heavy, rng.integers(0, 256, res.shape), res)
    cap = rng.integers(0, 64, sh); dead = rng.choice(np.array([0.0, 0.25, 0.5]), (N, 8, 1, 1))
    B = rng.integers(0, W, sh); T = np.where(rng.random(sh) < dead, 0, rng.integers(0, 16, sh)); K = np.where(rng.random(sh) < 0.5, 0, rng.integers(0, 16, sh))
    return res, cap, B, T, K, rng.integers(0, 256, (N, 8, 16, 1)), rng.integers(0, V, (N, 8, 16, 1))
def setup_inputs(rng):
    return pack(*parts(rng))
def setup_inputs_corners(rng):
    res, cap, B, T, K, wt, ka = parts(rng)
    v = np.arange(V); t0 = v % S + 1; row = np.arange(16).reshape(16, 1)
    res[..., W - 16:] = np.where(row < np.arange(16), 200, 0)
    res[:, 5, :, 0:V:2] = 255; res[:, 6, :, 0:V:2] = 0; cap[:, 6, :, ::2] = 63
    cl = rng.integers(0, 9, (N, 8, 1, V)); one = rng.integers(0, 16, (N, 8, 1, V)); near = W - 16 + rng.integers(3, 7, (N, 8, 1, V)); same = rng.integers(0, W, (N, 8, 1, V))
    T = np.where(cl == 0, t0 - 1, T); K = np.where(cl == 0, 0, K)
    T = np.where(cl == 1, 15, T); K = np.where(cl == 1, 0, K)
    T = np.where(cl == 2, np.where(row % 2 == 0, t0, t0 - 1), T); K = np.where(cl == 2, 0, K)
    T = np.where(cl == 3, 15, T); K = np.where(cl == 3, np.where(row % 2 == 0, t0 - 1, t0), K)
    T = np.where(cl == 4, np.where(row == one, 15, 0), T); K = np.where(cl == 4, 0, K); B = np.where(cl == 4, near, B); cap = np.where(cl == 4, 63, cap)
    T = np.where(cl == 5, 15, T); K = np.where(cl == 5, 0, K); B = np.where(cl == 5, same, B)
    cap = np.where(cl == 5, np.minimum(np.take_along_axis(res, same, 3), 63), cap)
    chain = np.where(row == 0, v, np.where(row == 1, np.maximum(v - 1, 0), np.where(row == 2, W - 1, np.where(row == 3, 0, V))))
    T = np.where(cl == 6, np.where(row < 5, 15, 0), T); K = np.where(cl == 6, 0, K); B = np.where(cl == 6, chain, B)
    two = (cl == 7) & ((row == 3) | (row == 15))
    T = np.where(two, 15, T); K = np.where(two, 0, K); B = np.where(two, near, B); cap = np.where(cl == 7, 63, cap)
    q = rng.permutation(N); T[q[0], 7] = 0; T[q[1], 7] = 15; K[q[1], 7] = 0
    wt[:, 0] = 0; wt[:, 1] = 255; ka[:, 2] = 0; ka[:, 3] = V - 1; ka[:, 4] = rng.choice(np.array([0, V >> 1]), (N, 16, 1))
    return pack(res, cap, B, T, K, wt, ka)
def setup_inputs_ends(rng):
    sh = (N, 8, 16, V); lane = np.arange(16).reshape(16, 1)
    kd = rng.choice(6, (N, 8, 1, W), p=[0.38, 0.12, 0.25, 0.1, 0.08, 0.07])
    kd[:, :, 0, W - 1] = np.where(np.arange(8) % 2 == 1, 1, 2); kd[:, 7, 0, V - 1] = 5; kd[:, 7, 0, V - 2] = 4
    rot = (lane + rng.integers(0, 16, (N, 8, 1, W))) % 16; some = 255 * (rng.random((N, 8, 16, W)) < 0.2)
    res = np.where(kd == 1, 255, np.where(kd == 2, some, np.where(kd == 3, 63, np.where(kd == 4, np.where(rot < 4, 255, 63), np.where(kd == 5, np.where(rot < 5, 255, 63), 0)))))
    ck = rng.choice(3, (N, 8, 1, V), p=[0.5, 0.15, 0.35]); cap = np.where(ck == 0, 63, np.where(ck == 1, 0, 63 * rng.integers(0, 2, sh)))
    up = rng.random(sh) < rng.choice(np.array([0.0, 0.1, 0.2]), (N, 8, 1, V))
    B = np.where(up, W - 1, 0); T = np.where(up, 15, 0); K = np.where(up, 0, 15)
    fr = rng.random(sh) < rng.choice(np.array([0.0, 0.1, 0.2, 0.4]), (N, 8, 1, V)); live = rng.random(sh) < 0.8
    B = np.where(fr, np.where(rng.random(sh) < 0.7, rng.integers(0, W, sh), rng.choice(np.array([0, V - 1, V, W - 1]), sh)), B)
    T = np.where(fr, np.where(live, 15, 15 * rng.integers(0, 2, sh)), T); K = np.where(fr, np.where(live, 0, 15 * rng.integers(0, 2, sh)), K)
    for j, first, col, c in ((0, 15, V - 1, 63), (1, 15, V - 2, 63), (2, 14, W - 1, 0)):
        a = S * (Q - 1 - j)
        B[:, 7, :, a:a + S] = 0; T[:, 7, :, a:a + S] = 0; K[:, 7, :, a:a + S] = 15; cap[:, 7, :, a:a + S] = c
        B[:, 7, first:, a:a + S] = col; T[:, 7, first:, a:a + S] = 15; K[:, 7, first:, a:a + S] = 0
    wt = np.where(rng.random((N, 8, 16, 1)) < 0.8, 255 * rng.integers(0, 2, (N, 8, 16, 1)), rng.integers(0, 256, (N, 8, 16, 1))); wt[:, 7] = 255; wt[:, 0, 0] = 0
    ka = np.where(rng.random((N, 8, 16, 1)) < 0.8, (V - 1) * rng.integers(0, 2, (N, 8, 16, 1)), rng.integers(0, V, (N, 8, 16, 1)))
    ka[:, 7] = rng.integers(0, V, (N, 16, 1)); ka[:, 0, 0] = 0; ka[:, 0, 1] = V - 1; ka[:, 7, 15] = V - 1
    return pack(res, cap, B, T, K, wt, ka)
def setup_inputs_full(rng):
    res, cap, B, T, K, wt, ka = parts(rng); q = rng.permutation(N); i = np.arange(Q); lane = np.arange(16).reshape(16, 1)
    res[..., W - 16:] = np.where(lane < np.arange(16), 200, 0)
    a = q[0]; T[a, :, :, 0::S] = 0; T[a, :, :, 1::S] = 0; cap[a, :, :, 1::S] = 63
    odd = rng.permutation(8 * Q)[:2 * int(rng.integers(1, 100)) + 1]; k = rng.integers(0, 16, odd.size); g = odd // Q; v = S * (odd % Q)
    B[a, g, k, v] = W - 16 + rng.integers(6, 16, odd.size); T[a, g, k, v] = 15; K[a, g, k, v] = 0
    a = q[1]; hit = lane == rng.integers(0, 16, (8, 1, Q))
    B[a, :, :, 0::S] = np.where(hit, W - 16 + rng.integers(6, 16, (8, 1, Q)), B[a, :, :, 0::S]); T[a, :, :, 0::S] = np.where(hit, 15, T[a, :, :, 0::S]); K[a, :, :, 0::S] = np.where(hit, 0, K[a, :, :, 0::S])
    for a, s in ((q[0], 2), (q[1], 1)):
        five = rng.random((8, 1, Q)) < 0.6; hit = lane == rng.integers(0, 16, (8, 1, Q))
        B[a, :, :, s::S] = np.where(five & hit, W - 11, B[a, :, :, s::S]); K[a, :, :, s::S] = np.where(five & hit, 0, K[a, :, :, s::S])
        T[a, :, :, s::S] = np.where(five, np.where(hit, 15, 0), T[a, :, :, s::S])
    a = q[2]; T[a] = 15; K[a] = 0; B[a, 1::2] = rng.integers(V, W, (4, 16, V))
    for g in (0, 4):
        base = rng.integers(200, 249, 16); turn = (lane + rng.integers(0, 16, (1, Q - 16))) % 16
        res[a, g, :, W - Q:W - 16] = base[turn] + (lane < rng.integers(0, 8, (1, Q - 16)))
        B[a, g] = np.where(rng.random((1, V)) < 0.5, rng.integers(W - Q, W - 16, (16, V)), B[a, g])
    a = q[3]; r = (a + 1) % N; T[a, :, :, 0::S] = 0
    for g in range(8):
        x, y = rng.permutation(16)[:2]; wt[r, g] = 0; wt[r, g, x] = 16; wt[r, g, y] = 1
        if g != 3: ka[r, g] = int(ka[r, g, 0, 0])
        o = rng.permutation(4096); p = ((o * o >> 5) + int(ka[r, g, 0, 0]) * o) & (V - 1)
        first = rng.permutation(np.unique(p, return_index=True)[1]); n = (Q, 8, Q, 1, Q, 8, Q, 1)[g]
        s = (o[first[rng.permutation(Q) % n]] - 37 * i) & 4095; col = V + rng.permutation(Q); k = rng.integers(0, 16, Q)
        res[a, g, :, V:V + Q] = 0; res[a, g, x, col] = s >> 4; res[a, g, y, col] = s & 15
        B[a, g, k, S * i] = col; T[a, g, k, S * i] = 15; K[a, g, k, S * i] = 0
    return pack(res, cap, B, T, K, wt, ka)
def setup_inputs_spread(rng):
    res, cap, B, T, K, wt, ka = parts(rng)
    res = (np.exp2(8 * rng.random((N, 8, 1, W)) ** 3) * rng.random((N, 8, 16, W))).astype(np.int64)
    res = np.where(rng.random((N, 8, 1, W)) < 0.02, rng.integers(0, 256, res.shape), np.minimum(res, 255))
    cap = np.minimum((np.exp2(6 - 6 * rng.random((N, 8, 1, V)) ** 3) * rng.random(cap.shape)).astype(np.int64), 63)
    B = np.minimum((W * rng.random(B.shape) ** rng.choice(np.array([0.5, 1.0, 3.0]), (N, 8, 1, 1))).astype(np.int64), W - 1)
    wt = np.minimum(np.exp2(8 * rng.random(wt.shape)).astype(np.int64), 255)
    return pack(res, cap, B, T, K, wt, ka)
def setup_inputs_ties(rng):
    res, cap, B, T, K, wt, ka = parts(rng)
    lane = np.arange(16).reshape(16, 1); turn = (lane + rng.integers(0, 16, (N, 8, 1, W))) % 16
    res = np.where(turn < rng.integers(2, 4, (N, 8, 1, W)), 40, 0)
    cap = np.broadcast_to(rng.choice(np.array([0, 20, 20, 39, 40, 63]), (N, 8, 1, V)), cap.shape)
    live = rng.random(B.shape) < rng.choice(np.array([0.1, 0.2, 0.3]), (N, 8, 1, 1))
    T = np.where(live, 15, 0); K = np.where(live, 0, K)
    wt[:, ::2] = 1; ka[:, 1::2] = rng.choice(np.array([0, 1, V >> 1, V - 1]), (N, 4, 16, 1))
    return pack(res, cap, B, T, K, wt, ka)
def check_inputs(d):
    bad = []
    for k, lo, hi in (("res", 0, 255), ("cap", 0, 63), ("br", -983040, 63743), ("wt", 0, 255), ("ka", 0, V - 1)):
        v = np.asarray(d[k]).astype(np.float64)
        if not np.all((v >= lo) & (v <= hi) & (v == np.floor(v))): bad.append("range of " + k)
    if np.any((np.asarray(d["br"]).astype(np.int64) & 4095) >= W): bad.append("column numbers in br")
    return bad
def reference(res, cap, br, wt, ka):
    R = res.astype(np.float32).astype(np.int32).reshape(N, 8, 16, W); C = cap.astype(np.float32).astype(np.int32).reshape(N, 8, 16, V)
    b = np.array(br, dtype=np.int32).reshape(N, 8, 16, V); w = wt.astype(np.int64).reshape(N, 8, 16, 1); kf = ka.astype(np.int64).reshape(N, 8, 16, 1)
    A = [0] * N; row = np.arange(16).reshape(1, 16, 1); i = np.arange(Q)
    for t in range(1, RO + 1):
        v = S * i + (t - 1) % S; sent = []
        for r in range(N):
            x = b[r][:, :, v]; on = (((x >> 12) & 15) >= t) & (-(x >> 16) < t)
            c = C[r][:, :, v]; most = 4 + (A[r] & 1)
            pick = np.take_along_axis(R[r], (x & 4095).reshape(8, 1, 16 * Q), 2).reshape(8, 16, 16, Q) * on[:, None]
            m = np.max(pick, axis=2); fail = np.sum(m > c, axis=1) > most
            over = np.where(on, np.sum(np.maximum(pick - c[:, :, None], 0), axis=1), -1)
            gone = fail[:, None] & (row == np.argmax(over, axis=1)[:, None])
            m = np.max(pick * (~gone)[:, None], axis=2)
            m = np.where((np.sum(m > c, axis=1) > most)[:, None], 0, m)
            b[r][:, :, v] = np.where(gone, (x & 65535) - 65536 * (t + S), x)
            R[r][:, :, v] = m; A[r] = int(np.sum(fail)); sent.append(m)
        for r in range(N):
            m = sent[(r - 1 - (t - 1) % (N - 1)) % N]
            u = (np.sum(w[r] * m, axis=1) + 37 * i) & 4095
            p = ((u * u >> 5)[:, None] + kf[r] * u[:, None]) & (V - 1)
            slack = np.maximum(C[r] - R[r][:, :, :V], 0)
            sl = np.take_along_axis(slack, p.reshape(8, 1, 16 * Q), 2).reshape(8, 16, 16, Q)
            score = np.sum(np.minimum(m[:, :, None], sl), axis=1)
            par = np.take_along_axis(p, np.argmax(score, axis=1)[:, None], 1)[:, 0]
            for g in range(8):
                node, first = np.unique(par[g], return_index=True)
                b[r, g, first & 15, node] = V + Q * (t - 1) + first + 4096 * (t + 2)
            if t < RO: R[r][:, :, V + Q * (t - 1):V + Q * t] = m
    return {"yr": np.ascontiguousarray(R[..., :V]).reshape(N, 128, V).astype(np.float32).astype(BF), "yb": b.reshape(N, 128, V).astype(np.float32)}

@@ -1,0 +1,577 @@
+from concourse.mybir import AluOpType, ActivationFunctionType
+import comms_topo
+
+OP = AluOpType
+AF = ActivationFunctionType
+B16, F32, I32, U16 = "bfloat16", "float32", "int32", "uint16"
+ROUNDS, PH = 6, 4
+MV = 10
+SH = 16
+AREA0, AREAD = 13312, 4352
+RWN = AREA0 + AREAD * 4 + 256
+DDN = 4384
+
+SCRATCH = {}
+
+
+def _buf(where, dtype, *names):
+    for n in names:
+        SCRATCH[n[0]] = (where, [128, n[1]], dtype)
+
+
+_buf("sbuf", B16, ("RW", RWN), ("CAPS", 1024), ("SL", 1024), ("DD", DDN), ("E1", 4096), ("E2", 4096), ("X", 4096), ("SEG", 4096), ("TT", 256), ("FL", 256),
+     ("F2", 256), ("MN", 256), ("A1", 256), ("A2", 256), ("EX", 256), ("EXP", 256), ("JK", 256), ("MR", 1024), ("SG", 2048), ("EQ", 2176))
+_buf("sbuf", F32, ("W", 1280), ("BC", 1024), ("OFA", 256), ("OFB", 256), ("EQT", 256), ("DF", 256), ("T1", 256), ("EXD", 256), ("EXN", 256), ("PLT", 16), ("SM", 256),
+     ("PBF", 256), ("SX", 256), ("S16F", 160), ("TW", 256), ("NW", 256))
+_buf("sbuf", I32, ("BRI", 1024), ("YL", 1024), ("KI", 256), ("S16I", 224), ("UI", 256), ("PI1", 256), ("PI2", 256), ("WTI", 1), ("KAI", 1), ("I1", 8))
+_buf("sbuf", U16, ("OFFS", 256), ("IDX", 16), ("POF", 256), ("PBU", 256), ("LST", 16), ("LSD", 16), ("LID", 16), ("LLN", 16))
+_buf("sbuf", B16, ("IB", 256), ("IB15", 256), ("IB4", 256), ("MSKD", 256), ("NEGM", 256), ("BB", 128), ("BB4", 128), ("WB", 128), ("O8K", 8), ("O8S", 8), ("O8N", 8), ("O8M", 8), ("O8W", 8),
+     ("BSM", 128), ("ID", 128), ("IDN", 128), ("CK", 256), ("ONE", 128), ("C37", 128), ("ZR", 256))
+_buf("sbuf", F32, ("F1", 24), ("NMSK", 256), ("TRIM", 256), ("SEGM", 256), ("KR", 256), ("KAX", 256), ("BBF", 128), ("O8F", 8), ("CIX", 16), ("TRX", 16), ("TRD", 16), ("IDF", 128), ("O16", 128), ("NWN", 256))
+SCRATCH.update({"KRW": ("sbuf", [2, 128], I32), "KH": ("sbuf", [2, 128], I32), "KL": ("sbuf", [2, 128], I32), "KHF": ("sbuf", [2, 128], F32), "KLF": ("sbuf", [2, 128], F32), "KC": ("sbuf", [2, 256], B16)})
+_buf("psum", F32, ("pk", 512), ("pb", 512), ("pn", 512), ("pc", 512), ("pd", 2048))
+for _f in range(PH):
+    _buf("sbuf", B16, ("CX%d" % _f, 4096))
+for _r in range(1, ROUNDS + 1):
+    _buf("sbuf", B16, ("MO%d" % _r, 256), ("LD%d" % _r, 256))
+ALIAS = {n: ("F1", c, 1) for c, n in enumerate(("PIF", "LNF", "GRF", "LREV", "LN16", "OMP", "WTF", "KAF", "LIM", "FC", "SC", "H1", "H2", "LP0", "LP1", "LP2", "LP3"))}
+ALIAS.update({n: ("I1", c, 1) for c, n in enumerate(("PIX", "LNI", "GRI"))})
+ALIAS.update({n: ("S16I", 16 * c, 16) for c, n in enumerate(("TA", "TB", "U", "U2", "BS", "P2", "PL", "UT0", "UT", "UT2", "BST", "PLI", "PL3"))})
+ALIAS.update({n: ("S16F", 16 * c, 16) for c, n in enumerate(("TAF", "P1", "PLF", "L1", "L2", "L3", "L4", "PZ", "PQ"))})
+PSUM = ("pk", "pb", "pn", "pc", "pd")
+LOADS = ["lcap", "lbr", "lres", "lwt", "lka", "lk0", "lk1"]
+SEMAPHORES = ["sV", "sS", "sP", "sG", "sent", "oyr", "oyb"] + LOADS + ["arr%d" % r for r in range(1, ROUNDS + 1)]
+
+
+def scheduler(g, T):
+    eng = {"V": g.vector, "S": g.scalar, "P": g.tensor, "G": g, "Y": g.sync}
+    cnt, rec, snap = {}, {}, {}
+    clk = {q: {} for q in eng}
+
+    def ref(name, a=None, b=None, s=1, p=None):
+        if name in ALIAS:
+            name, o, w = ALIAS[name]
+            a, b = o + (a or 0), o + (w if b is None else b)
+        a = 0 if a is None else a
+        b = SCRATCH[name][1][1] if b is None else b
+        if s > 0:
+            sl = slice(a, b, s)
+        else:
+            sl = slice(b - 1, a - 1 if a else None, -1)
+        rows = slice(0, p) if p else slice(0, SCRATCH[name][1][0])
+        x = (name, a, b, max(s, 1), a % max(s, 1))
+        return {"ap": T[name][rows, sl], "r": [x], "w": [x]}
+
+    def ind(win, off):
+        return {"ap": win["ap"].indirect(off["ap"]), "r": win["r"] + off["r"], "w": win["w"], "x": off["r"]}
+
+    def overlap(q, x, y):
+        if x[0] in PSUM and q:
+            return x[1] // 512 <= (y[2] - 1) // 512 and y[1] // 512 <= (x[2] - 1) // 512
+        if x[3] == y[3] and x[4] != y[4]:
+            return False
+        return x[1] < y[2] and y[1] < x[2]
+
+    def deps(q, reads, writes):
+        need = {}
+        for isw, rs in ((False, reads), (True, writes)):
+            for x in rs:
+                for (y, w, q2, n) in rec.get(x[0], []):
+                    same = q2 == q
+                    if not overlap(not same, x, y) or (same and q == "P"):
+                        continue
+                    if not (w or isw or (x[0] in PSUM and not same)):
+                        continue
+                    if need.get(q2, 0) < n:
+                        need[q2] = n
+        for q2 in sorted(need):
+            n = need[q2]
+            if clk[q].get(q2, 0) >= n:
+                continue
+            if any(q3 != q2 and snap.get((q3, m), {}).get(q2, 0) >= n for q3, m in need.items() if clk[q].get(q3, 0) < m):
+                continue
+            eng[q].wait_ge(T.sem["s" + q2] if q2 in eng else T.sem[q2], n)
+        for q2, n in need.items():
+            if clk[q].get(q2, 0) < n:
+                clk[q][q2] = n
+                for q3, m in snap.get((q2, n), {}).items():
+                    if clk[q].get(q3, 0) < m:
+                        clk[q][q3] = m
+
+    def record(q, n, reads, writes, by):
+        s = dict(clk[by]) if by else {}
+        if q in eng:
+            s[q] = max(s.get(q, 0), n - 1)
+        snap[(q, n)] = s
+        for x in writes:
+            rec[x[0]] = [e for e in rec.get(x[0], []) if not (x[1] <= e[0][1] and e[0][2] <= x[2] and (x[3] == 1 or x[3:] == e[0][3:]))]
+        for w, rs in ((False, reads), (True, writes)):
+            for x in rs:
+                rec.setdefault(x[0], []).append((x, w, q, n))
+
+    def op(q, fn, outs, ins):
+        reads = [x for i in ins for x in i["r"]] + [x for o in outs for x in o.get("x", [])]
+        writes = [x for o in outs for x in o["w"]]
+        deps(q, reads, writes)
+        cnt[q] = cnt.get(q, 0) + 1
+        fn().then_inc(T.sem["s" + q], 1)
+        record(q, cnt[q], reads, writes, q)
+
+    def dma(q, sem, out, in_, outs, ins):
+        reads, writes = [x for i in ins for x in i["r"]], [x for o in outs for x in o["w"]]
+        deps(q, reads, writes)
+        eng[q].dma_start(out, in_).then_inc(T.sem[sem], 16)
+        record(sem, 16, reads, writes, q)
+
+    return {"ref": ref, "ind": ind, "op": op, "dma": dma, "deps": deps, "record": record, "cnt": cnt}
+
+
+def rank_program(g, core, T, topo):
+    rank = T.rank_of(core)
+    if rank is None:
+        return
+    sc = scheduler(g, T)
+    R, IND, op = sc["ref"], sc["ind"], sc["op"]
+
+    def val(x):
+        return x["ap"] if isinstance(x, dict) else x
+
+    def tt(out, a, b, o):
+        op("V", lambda: g.vector.tensor_tensor(out["ap"], a["ap"], b["ap"], o), [out], [a, b])
+
+    def ts(out, a, s1, s2, o0, o1=None):
+        ins = [a] + [s for s in (s1, s2) if isinstance(s, dict)]
+        if o1 is None:
+            op("V", lambda: g.vector.tensor_scalar(out["ap"], a["ap"], val(s1), None, o0), [out], ins)
+        else:
+            op("V", lambda: g.vector.tensor_scalar(out["ap"], a["ap"], val(s1), val(s2), o0, o1), [out], ins)
+
+    def cp(out, a):
+        op("V", lambda: g.vector.tensor_copy(out["ap"], a["ap"]), [out], [a])
+
+    def scan(out, d0, d1, o0, o1):
+        op("V", lambda: g.vector.tensor_tensor_scan(out["ap"], d0["ap"], d1["ap"], 0.0, o0, o1), [out], [d0, d1])
+
+    def ms(out, v):
+        op("V", lambda: g.vector.memset(out["ap"], v), [out], [])
+
+    def act(out, a, f, scale=1.0, bias=0.0, acc=None):
+        ins = [a] + [v for v in (scale, bias) if isinstance(v, dict)]
+        if acc:
+            op("S", lambda: g.scalar.activation(out["ap"], a["ap"], f, bias=val(bias), scale=val(scale), accum_out=acc["ap"]), [out, acc], ins)
+        else:
+            op("S", lambda: g.scalar.activation(out["ap"], a["ap"], f, bias=val(bias), scale=val(scale)), [out], ins)
+
+    def aff(out, a, scale, bias=0.0):
+        act(out, a, AF.Identity, scale, bias)
+
+    def mm(out, l, r, start, stop):
+        op("P", lambda: g.tensor.matmul(out["ap"], l["ap"], r["ap"], start, stop), [out], [l, r])
+
+    def iota(out, pattern, base, cm):
+        if SCRATCH[out["r"][0][0]][2] == I32:
+            op("G", lambda: g.iota(out["ap"], pattern, base, cm), [out], [])
+        else:
+            op("G", lambda: g.iota(out["ap"], pattern, base, cm, allow_small_or_imprecise_dtypes=True), [out], [])
+
+    def gcopy(a, b, n):
+        op("G", lambda: g.affine_select(a["ap"], b["ap"], [[0, n]], OP.is_gt, 0.0, 1, 0), [a], [b])
+
+    def widen(f, k, q, h=None):
+        if h is None:
+            a, b = R("CX%d" % f, k, 4096, 16), R("CAPS", f, 1024, 4)
+        else:
+            a, b = R("CX%d" % f, 2048 * h + k, 2048 * h + 2048, 16), R("CAPS", 512 * h + f, 512 * h + 512, 4)
+        if q == "G":
+            gcopy(a, b, 256 if h is None else 128)
+        elif q == "V":
+            cp(a, b)
+        else:
+            act(a, b, AF.Copy)
+
+    sc["dma"]("Y", "lbr", R("BRI")["ap"], T.br[:], [R("BRI")], [])
+    sc["dma"]("S", "lcap", R("CAPS")["ap"], T.cap[:], [R("CAPS")], [])
+    x = R("RW", SH, SH + 2304)
+    sc["dma"]("Y", "lres", x["ap"], T.res[:], [x], [])
+    sc["dma"]("S", "lwt", R("WTI")["ap"], T.wt[:], [R("WTI")], [])
+    sc["dma"]("S", "lka", R("KAI")["ap"], T.ka[:], [R("KAI")], [])
+    for p in (0, 1):
+        g.scalar.dma_start(T.KRW[p:p + 1, :], T.ka[:]).then_inc(T.sem["lk%d" % p], 16)
+        sc["record"]("lk%d" % p, 16, [], [("KRW", p, p + 1, 1, 0)], "S")
+
+    iota(R("PIX"), [[0, 1]], 0, 1)
+    iota(R("IB15"), [[0, 16], [1, 16]], 0, 0)
+    iota(R("IB4"), [[1, 16], [0, 16]], 0, 0)
+    iota(R("IB"), [[1, 256]], 0, 0)
+    for k in range(4):
+        widen(0, k, "G", 1)
+    iota(R("CIX"), [[256, 16]], 15, 0)
+    iota(R("TRX"), [[16, 16]], 1024, 0)
+    iota(R("TRD"), [[16, 16]], 4128, 0)
+    iota(R("NWN"), [[1, 256]], AREA0 - AREAD, 0)
+    ms(R("RW", 0, SH), 0.0)
+    ms(R("DD", 0, 16), 0.0)
+    ms(R("DD", 4112, DDN), 0.0)
+    ms(R("LIM"), 4.0)
+    ms(R("ONE"), 1.0)
+    ts(R("LNI"), R("PIX"), 15, None, OP.bitwise_and)
+    ts(R("GRI"), R("PIX"), 4, None, OP.arith_shift_right)
+    cp(R("PIF"), R("PIX"))
+    cp(R("LNF"), R("LNI"))
+    cp(R("GRF"), R("GRI"))
+    ts(R("SEG", 0, 256), R("IB15"), 0.0, 768.0, OP.is_gt, OP.mult)
+    ts(R("SEG", 0, 256), R("SEG", 0, 256), -256.0, None, OP.add)
+
+    def halves(f):
+        ts(R("YL", f, 1024, 4), R("BRI", f, 1024, 4), 65535, None, OP.bitwise_and)
+        ts(R("KI"), R("BRI", f, 1024, 4), 4095, None, OP.bitwise_and)
+        ts(R("BC", 256 * f, 256 * f + 256), R("KI"), float(SH), None, OP.add)
+
+    def code(f, t, out, q, tiles=None):
+        a, b = (R("pn", 0, 256), R("pc", 0, 256)) if q == "V" else (R(tiles[0]), R(tiles[1]))
+        ts(a, R("BRI", f, 1024, 4), float(-65536 * (t - 1)), -8192.0, OP.is_lt, OP.mult)
+        ts(b, R("YL", f, 1024, 4), float(4096 * t), -8192.0, OP.is_lt, OP.mult)
+        bc = R("BC", 256 * f, 256 * f + 256)
+        if q == "V":
+            tt(R("DF"), bc, a, OP.add)
+            tt(out, R("DF"), b, OP.add)
+        else:
+            s = R("pd", 512 * q, 512 * q + 256)
+            mm(s, R("IDF"), bc, True, False)
+            mm(s, R("ID"), a, False, False)
+            mm(s, R("ID"), b, False, True)
+            act(out, s, AF.Copy)
+    for n in (256, 512):
+        act(R("SEG", n, 2 * n), R("SEG", 0, n), AF.Copy)
+    for n in (1024, 2048):
+        gcopy(R("SEG", n, 2 * n), R("SEG", 0, n), n)
+    iota(R("C37"), [[0, 128]], 37, 0)
+    iota(R("ZR"), [[0, 256]], 0, 0)
+    iota(R("W", 1024, 1280), [[0, 256]], 0, 0)
+    cp(R("WTF"), R("WTI"))
+    cp(R("KAF"), R("KAI"))
+    for k in range(4, 16):
+        widen(0, k, "S", 1)
+    for k in range(11, 16):
+        widen(0, k, "S", 0)
+    halves(0)
+    code(0, 1, R("W", 0, 1024, 4), "V")
+    cp(R("OFFS"), R("W", 0, 1024, 4))
+    for k in range(11):
+        widen(0, k, "V", 0)
+
+    def key_constants():
+        ts(R("ID"), R("IB", 0, 128), R("PIF"), None, OP.is_equal)
+        ts(R("IDN"), R("ID"), -1.0, None, OP.mult)
+        ts(R("O8K"), R("IB", 0, 8), R("GRF"), 16.0, OP.is_equal, OP.mult)
+        ts(R("BB"), R("IB4", 0, 128), R("GRF"), None, OP.is_equal)
+        aff(R("CK"), R("IB15"), -1.0, 15.0)
+
+    def late_constants():
+        aff(R("IDF"), R("ID"), 1.0)
+        aff(R("O8M"), R("O8K"), -0.0625)
+        aff(R("LN16"), R("LNF"), 16.0)
+        aff(R("CIX"), R("CIX"), 1.0, R("LN16"))
+        aff(R("LREV"), R("LNF"), -1.0, 15.0)
+        ts(R("MSKD"), R("IB15"), R("LNF"), None, OP.is_equal)
+        cp(R("LID"), R("IB", 0, 16))
+        ts(R("SEGM"), R("IB15"), 0.0, None, OP.is_gt)
+        aff(R("NEGM"), R("MSKD"), 2097152.0, -2097152.0)
+        aff(R("O16"), R("ONE"), 0.0625)
+        aff(R("NMSK"), R("MSKD"), -1.0, 1.0)
+        aff(R("KHF"), R("CK", 0, 128, 1, 2), 1024.0)
+        aff(R("OMP"), R("PIF"), -1.0, 1.0)
+        aff(R("BB4"), R("BB"), 8192.0)
+        aff(R("WB"), R("BB"), R("WTF"))
+        aff(R("O8F"), R("O8K"), 0.0625)
+        aff(R("O8W"), R("O8F"), R("WTF"))
+        aff(R("BBF"), R("BB"), 1.0)
+        aff(R("O8S"), R("O8K"), 1024.0)
+        aff(R("O8N"), R("O8K"), -1024.0)
+
+    def score_constants():
+        ts(R("LLN"), R("IB", 0, 16), 0.0, R("LNF"), OP.mult, OP.add)
+        ts(R("BSM"), R("IB15", 0, 128), float(MV), 16384.0, OP.is_ge, OP.mult)
+        ts(R("KR"), R("IB4"), R("LNF"), R("KAF"), OP.is_equal, OP.mult)
+        mm(R("pk", 0, 256), R("BBF"), R("KR"), True, True)
+        tt(R("BSM"), R("BSM"), R("BB"), OP.mult)
+        aff(R("KAX"), R("pk", 0, 256), 1.0)
+
+    def parent_constants():
+        ts(R("KH"), R("KRW"), 768, None, OP.bitwise_and)
+        ts(R("KL"), R("KRW"), 255, None, OP.bitwise_and)
+        tt(R("KHF"), R("KHF"), R("KH"), OP.add)
+        ts(R("KLF"), R("KL"), R("PIF", 0, 1, 1, 2), None, OP.mult)
+        ts(R("KHF"), R("KHF"), R("OMP", 0, 1, 1, 2), None, OP.mult)
+        ts(R("TRIM"), R("IB15"), R("LNF"), 2097152.0, OP.is_le, OP.mult)
+        tt(R("KC", 0, 128), R("KHF"), R("KLF"), OP.add)
+        tt(R("NWN"), R("NWN"), R("NEGM"), OP.add)
+        cp(R("KC", 128, 256), R("KC", 0, 128))
+
+    def list_constants():
+        aff(R("TRX"), R("TRX"), 1.0, R("LNF"))
+        aff(R("TRD"), R("TRD"), 1.0, R("LNF"))
+        for c in range(4):
+            aff(R("LP%d" % c), R("LNF"), 1.0, 16.0 - 4 * c)
+
+    def room(f, c, rooms, res):
+        o = 1024 * (c % 2)
+        for b in (0, 512):
+            if rooms:
+                mm(R("pd", o + b, o + b + 512), R("IDN" if c else "ID"), R("CX%d" % f, 1024 * c + b, 1024 * c + b + 512), True, not c)
+        for b in (0, 512):
+            if res:
+                mm(R("pd", o + b, o + b + 512), R("ID"), R("DD", 16 + 1024 * c + b, 528 + 1024 * c + b), False, True)
+
+    word_steps = [lambda: tt(R("L1"), R("SX", 15, 256, 16), R("TRX"), OP.min),
+                  lambda: tt(R("L2"), R("L1"), R("PLF"), OP.max),
+                  lambda: cp(R("LST"), R("L2")),
+                  lambda: tt(R("TW"), IND(R("W"), R("LST")), R("NMSK"), OP.mult),
+                  lambda: tt(IND(R("W"), R("LST")), R("TW"), R("NW"), OP.add)]
+
+    sent = 0
+    for t in range(1, ROUNDS + 1):
+        f = (t - 1) % PH
+        f2 = t % PH
+        wf, capf = R("W", f, 1024, 4), R("CAPS", f, 1024, 4)
+        if t == 1:
+            win = R("RW", 0, SH + 2304)
+            for c in (0, 1):
+                cp(R("DD", 16 + 1024 * c, 1040 + 1024 * c), IND(win, R("OFFS", 64 * c, 64 * c + 64)))
+            for c in (2, 3):
+                act(R("DD", 16 + 1024 * c, 1040 + 1024 * c), IND(win, R("OFFS", 64 * c, 64 * c + 64)), AF.Copy)
+            key_constants()
+            room(0, 0, True, False)
+            room(0, 1, True, False)
+        mm(R("pk", 0, 256), R("ONE", 0, 128, 1, 1), R("CK", 0, 256, 1, 1), True, False)
+        mm(R("pc", 256, 512), R("ID"), capf, True, True)
+        room(f, 1, False, True)
+        tt(R("X", 0, 1024), R("DD", 16, 1040), R("pd", 0, 1024), OP.max)
+        mm(R("pn", 0, 256), R("ID"), R("DD", 31, 4112, 16), True, True)
+        room(f, 2, True, True)
+        act(R("X", 1024, 2048), R("pd", 1024, 2048), AF.Relu)
+        room(f, 3, True, True)
+        act(R("X", 2048, 3072), R("pd", 0, 1024), AF.Relu)
+        act(R("X", 3072, 4096), R("pd", 1024, 2048), AF.Relu)
+        scan(R("E1"), R("DD", 15, 4111), R("SEG"), OP.max, OP.min)
+        scan(R("E2", 0, 4096, -1), R("DD", 17, 4113, -1), R("SEG"), OP.max, OP.min)
+        tt(R("TT"), R("E1", 15, 4096, 16), R("pn", 0, 256), OP.max)
+        if t > 1:
+            word_steps[0]()
+        tt(R("FL"), R("TT"), R("pc", 256, 512), OP.is_gt)
+        if t > 1:
+            word_steps[1]()
+            word_steps[2]()
+        for h in (0, 1):
+            for k in range(16):
+                mm(R("pk", 128 * h + k, 128 * h + 128, 16), R("X", 2048 * h + k, 2048 * h + 2048, 16), R("O8K"), False, h == 1 and k == 15)
+            if h == 0:
+                mm(R("pb", 0, 256), R("BB"), R("FL"), True, True)
+        if t == 1:
+            late_constants()
+        mm(R("pn", 256, 272), R("IDF"), R("CIX"), True, False)
+        ts(R("pb", 0, 256), R("pb", 0, 256), R("LIM"), -512.0, OP.is_gt, OP.mult)
+        tt(R("MN"), R("TT"), R("pb", 0, 256), OP.add)
+        scan(R("KI"), R("SEGM"), R("pk", 0, 256), OP.mult, OP.max)
+        ts(R("TA"), R("KI", 15, 256, 16), 15, None, OP.bitwise_and)
+        tt(R("EX"), IND(R("TA"), R("LID")), R("MSKD"), OP.mult)
+        cp(R("TAF"), R("TA"))
+        for h in (0, 1):
+            mm(R("pn", 256 + 8 * h, 264 + 8 * h), R("EX", 128 * h, 128 * h + 128), R("O8M"), False, h == 1)
+        act(R("EXP"), IND(R("TAF"), R("LID")), AF.Copy)
+        cp(R("IDX"), R("pn", 256, 272))
+        tt(R("A1"), IND(R("E1"), R("IDX")), R("MN"), OP.max)
+        tt(R("A2"), IND(R("E2"), R("IDX")), R("A1"), OP.max)
+        tt(R("F2"), R("A2"), R("pc", 256, 512), OP.is_gt)
+        mm(R("pn", 0, 256), R("BB"), R("F2"), True, True)
+        ts(R("pn", 0, 256), R("pn", 0, 256), R("LIM"), None, OP.is_le)
+        mo, ld = R("MO%d" % t), R("LD%d" % t)
+        tt(mo, R("A2"), R("pn", 0, 256), OP.mult)
+        dst = T.cores[(rank + 1 + (t - 1) % 7) % 8]
+        ne = len(topo.engines(core, dst))
+        rid, pid, _se = topo.addr(dst)
+        sc["deps"]("G", mo["r"], [])
+        g.remote_dma(ld["ap"], mo["ap"], T.sem["arr%d" % t], T.sem["sent"], pid, rid, topo.mask(core, dst))
+        sent += ne
+        sc["record"]("arr%d" % t, ne, [], ld["w"], None)
+        if t < PH:
+            for k in range(16):
+                widen(t, k, "G")
+        if t == 1:
+            for b in (0, 512):
+                mm(R("pd", 1024 + b, 1536 + b), R("ID"), R("CAPS", b, b + 512), True, False)
+                mm(R("pd", 1024 + b, 1536 + b), R("IDN"), R("RW", SH + b, SH + b + 512), False, True)
+            act(R("SL"), R("pd", 1024, 2048), AF.Relu)
+        for h in (0, 1):
+            mm(R("pd", 128 * h, 128 * h + 128), R("EXP", 128 * h, 128 * h + 128), R("ID"), True, True)
+        mm(R("pd", 512, 768), R("ID"), capf, True, False)
+        mm(R("pd", 512, 768), R("IDN"), mo, False, True)
+        act(R("SL", f, 1024, 4), R("pd", 512, 768), AF.Relu)
+        act(R("RW", SH + f, SH + 1024, 4), mo, AF.Copy)
+        if t == 1:
+            score_constants()
+        else:
+            word_steps[3]()
+        ts(R("EQT"), R("pd", 0, 256), R("LREV"), 128.0 * (t + 4), OP.is_equal, OP.mult)
+        if t > 1:
+            word_steps[4]()
+        tg, b2, sm, bf = R("pd", 1536, 1792), R("pd", 1792, 2048), R("SM"), R("BRI", f, 1024, 4)
+        tt(tg, R("EQT"), R("pb", 0, 256), OP.mult)
+        if t < ROUNDS:
+            act(R("JK"), R("pb", 0, 256), AF.Copy, scale=-1.0 / 512, acc=R("FC"))
+            mm(R("pd", 1024, 1025), R("O16"), R("FC"), True, True)
+            aff(R("SC"), R("pd", 1024, 1025), 1.0)
+            aff(R("H1"), R("SC"), 0.5, 8388608.0)
+            aff(R("H2"), R("H1"), -2.0, 16777216.0)
+            act(R("H1"), R("SC"), AF.Abs, 1.0, R("H2"))
+            aff(R("LIM"), R("H1"), 1.0, 4.0)
+        else:
+            y = R("RW", SH, SH + 1024)
+            sc["dma"]("Y", "oyr", T.yr[:], y["ap"], [], [y])
+        if t == 1:
+            for c, tiles in ((1, ("MN", "A1")), (2, ("FL", "F2")), (3, ("A2", "EX"))):
+                halves(c)
+                code(c, c + 1, R("W", c, 1024, 4), 1 + c % 2, tiles)
+            code(0, 5, R("OFA"), 1, ("MN", "A1"))
+            code(1, 6, R("OFB"), 2, ("FL", "F2"))
+            parent_constants()
+        yf = R("YL", f, 1024, 4)
+        if t > 1:
+            if t < ROUNDS:
+                cp(R("OFFS"), R("W", f2, 1024, 4))
+            tt(b2, yf, tg, OP.add)
+            ts(sm, wf, 4096.0, None, OP.is_ge)
+            tt(b2, bf, b2, OP.min)
+            if t == 2:
+                tt(R("EQT"), R("OFB"), tg, OP.add)
+            own = [lambda: tt(R("DF"), wf, tg, OP.add), lambda: tt(tg, R("DF"), b2, OP.subtract),
+                   lambda: tt(R("DF"), sm, tg, OP.mult), lambda: tt(bf if t == 2 else wf, R("DF"), b2, OP.add)]
+            if t == 2:
+                own += [lambda: ts(sm, sm, 2097152.0, None, OP.mult), lambda: tt(yf, yf, sm, OP.max),
+                        lambda: tt(wf, R("EQT"), sm, OP.subtract)]
+        else:
+            own = [lambda: tt(b2, yf, tg, OP.add), lambda: tt(wf, R("OFA"), tg, OP.add), lambda: tt(bf, bf, b2, OP.min)]
+        mm(R("pn", 0, 256), R("ID"), R("NEGM"), True, False)
+        mm(R("pn", 0, 256), R("C37", 0, 128, 1, 1), R("IB", 0, 256, 1, 1), False, False)
+        mm(R("pk", 0, 256), R("ONE", 0, 128, 1, 1), R("ZR", 0, 256, 1, 1), True, False)
+        mm(R("pn", 0, 256), R("WB"), ld, False, True)
+        for h in (0, 1):
+            mm(R("pk", 128 * h, 128 * h + 128), R("LD%d" % t, 128 * h, 128 * h + 128), R("BSM"), False, False)
+        for k in range(4):
+            act(R("MR", 256 * k, 256 * k + 256), ld, AF.Copy)
+        if t < ROUNDS:
+            act(R("RW", SH + 1024 + 256 * (t - 1), SH + 1280 + 256 * (t - 1)), ld, AF.Copy)
+            act(R("RW", AREA0 + AREAD * (t - 1), AREA0 + AREAD * (t - 1) + 256), ld, AF.Copy)
+            if t > 2:
+                act(R("RW", AREA0 + AREAD * (t - 3), AREA0 + AREAD * (t - 3) + 256), R("ZR"), AF.Copy)
+        scan(R("UI"), R("SEGM"), R("pn", 0, 256), OP.mult, OP.max)
+        ts(R("U"), R("UI", 15, 256, 16), 4095, None, OP.bitwise_and)
+        tt(R("U2"), R("U"), R("U"), OP.mult)
+        tt(R("T1"), IND(R("U"), R("LLN")), R("KAX"), OP.mult)
+        ts(R("BS"), R("U2"), 5, None, OP.arith_shift_right)
+        tt(R("PI1"), IND(R("BS"), R("LLN")), R("T1"), OP.add)
+        ts(R("PI2"), R("PI1"), 1023, None, OP.bitwise_and)
+        cp(R("POF"), R("PI2"))
+        def pieces(a, b):
+            return [(o, min(512, b - o)) for o in range(a, b, 512)]
+        for o, n in pieces(0, 256 * (16 - MV)):
+            mm(R("pd", o, o + n), R("ID"), R("MR", 0, n), True, False)
+        for h in (0, 1):
+            mm(R("pn", 256 + 8 * h, 264 + 8 * h), R("LD%d" % t, 128 * h, 128 * h + 128), R("O8W"), True, False)
+            mm(R("pn", 256 + 8 * h, 264 + 8 * h), R("IB", 128 * h, 128 * h + 128, 1, 1), R("C37", 0, 8, 1, 1), False, True)
+
+        def keys(m0, n, r):
+            for mc in range(m0, m0 + n):
+                for h in (0, 1):
+                    mm(R("pk", 128 * h + mc, 128 * h + 128, 16), R("X", 256 * mc + 128 * h, 256 * mc + 128 * h + 128), r, False, False)
+        spl = [(m0, min(4, 16 - m0)) for m0 in range(MV, 16, 4)]
+        vpl = [(m0, min(4, MV - m0)) for m0 in range(0, MV, 4)]
+        for m0, n in spl:
+            o = 256 * (m0 - MV)
+            act(R("SG", o, o + 256 * n), IND(R("SL"), R("POF", 16 * m0, 16 * (m0 + n))), AF.Copy)
+        for e, (m0, n) in enumerate(vpl):
+            tt(R("X", 256 * m0, 256 * (m0 + n)), IND(R("SL"), R("POF", 16 * m0, 16 * (m0 + n))), R("MR", 0, 256 * n), OP.min)
+            keys(m0, n, R("O8S"))
+            if e < len(spl):
+                m1, n1 = spl[e]
+                for o, w in pieces(256 * (m1 - MV), 256 * (m1 - MV + n1)):
+                    mm(R("pd", o, o + w), R("IDN"), R("SG", o, o + w), False, True)
+                act(R("X", 256 * m1, 256 * (m1 + n1)), R("pd", 256 * (m1 - MV), 256 * (m1 - MV + n1)), AF.Relu)
+        for m0, n in spl:
+            keys(m0, n, R("O8N"))
+        mm(R("pk", 0, 256), R("ONE", 0, 128, 1, 2), R("KC"), False, True)
+        act(R("NW"), R("NWN"), AF.Relu, 1.0, float(AREAD * t))
+        if t == 1:
+            list_constants()
+        def gather(c):
+            win = R("RW", 0, AREA0 + AREAD * (t - 1) + 256)
+            act(R("DD", 16 + 1024 * c, 1040 + 1024 * c), IND(win, R("OFFS", 64 * c, 64 * c + 64)), AF.Copy)
+        if t < ROUNDS:
+            if t == 1:
+                cp(R("OFFS"), R("W", f2, 1024, 4))
+            gather(0)
+            room(f2, 0, True, False)
+        turned = [lambda: cp(R("UT0"), R("pn", 256, 272)), lambda: ts(R("UT"), R("UT0"), 4095, None, OP.bitwise_and),
+                  lambda: tt(R("UT2"), R("UT"), R("UT"), OP.mult), lambda: ts(R("BST"), R("UT2"), 5, None, OP.arith_shift_right)]
+        for e in range(4):
+            turned[e]()
+            if e < 3:
+                own[e]()
+        scan(R("KI"), R("SEGM"), R("pk", 0, 256), OP.mult, OP.max)
+        ts(R("TB"), R("KI", 15, 256, 16), 1023, None, OP.bitwise_and)
+        tt(R("P1"), R("UT"), R("TB"), OP.mult)
+        tt(R("P2"), R("P1"), R("BST"), OP.add)
+        ts(R("PL"), R("P2"), 1023, None, OP.bitwise_and)
+        cp(R("PLT"), R("PL"))
+        tt(R("EXD"), IND(R("PL"), R("LID")), R("MSKD"), OP.mult)
+        act(R("EXN"), IND(R("PLT"), R("LID")), AF.Copy)
+        if t < ROUNDS:
+            for c in (1, 2, 3):
+                gather(c)
+        for h in (0, 1):
+            mm(R("pc", 8 * h, 8 * h + 8), R("EXD", 128 * h, 128 * h + 128), R("O8F"), True, True)
+        for h in (0, 1):
+            mm(R("pb", 128 * h, 128 * h + 128), R("EXN", 128 * h, 128 * h + 128), R("IDF"), True, True)
+        mm(R("pn", 0, 256), R("ID"), R("NEGM"), True, False)
+        for e in own[3:]:
+            e()
+        if t < ROUNDS:
+            room(f2, 1, True, False)
+        cp(R("PLF"), R("pc", 0, 16))
+        if t < ROUNDS:
+            cp(R("PLI"), R("pc", 0, 16))
+            ts(R("PQ"), R("PLF"), 4.0, R("LP%d" % f2), OP.mult, OP.add)
+            ts(R("PL3"), R("PLI"), 3, None, OP.bitwise_and)
+        cp(R("PBU"), R("pb", 0, 256))
+        if t < ROUNDS:
+            ts(R("PZ"), R("PL3"), float(f2), 8192.0, OP.not_equal, OP.mult)
+        o = 0
+        for q in range(15):
+            n = 240 - 16 * q
+            if q == 1 and t < ROUNDS:
+                tt(R("PZ"), R("PQ"), R("PZ"), OP.add)
+            ts(R("EQ", o, o + n), R("PBU", 256 - n, 256), R("PLF", q, q + 1), None, OP.is_equal)
+            mm(R("pn", 256 - n, 256), R("BB4"), R("EQ", o, o + n), False, q == 14)
+            o += n
+            if q == 1:
+                tt(R("PBF"), R("pb", 0, 256), R("TRIM"), OP.add)
+                tt(R("EQ", 1920, 2176), IND(R("PLF"), R("LID")), R("PBF"), OP.is_equal)
+                mm(R("pn", 0, 256), R("BB4"), R("EQ", 1920, 2176), False, False)
+        scan(R("SX"), R("SEGM"), R("pn", 0, 256), OP.mult, OP.max)
+        if t < ROUNDS:
+            tt(R("L3"), R("SX", 15, 256, 16), R("PZ"), OP.max)
+            tt(R("L4"), R("L3"), R("TRD"), OP.min)
+            cp(R("LSD"), R("L4"))
+            out = IND(R("DD"), R("LSD"))
+            op("V", lambda: g.vector.tensor_copy(out["ap"], ld["ap"]), [out], [ld])
+    for step in word_steps:
+        step()
+    y = R("W", 0, 1024)
+    sc["dma"]("Y", "oyb", T.yb[:], y["ap"], [], [y])
+    g.sync.wait_ge(T.sem.oyb, 16)
+    g.sync.wait_ge(T.sem.oyr, 16)
+    for q in ("V", "S", "P", "G"):
+        g.wait_ge(T.sem["s" + q], sc["cnt"][q])
+    g.wait_ge(T.sem.sent, sent)
+    for s in LOADS:
+        g.wait_ge(T.sem[s], 16)

@@ -3,13 +3,15 @@ import comms_topo
 
 OP = AluOpType
 AF = ActivationFunctionType
-B16, F32, I32, U16 = "bfloat16", "float32", "int32", "uint16"
+B16, F16, F32, I32, U16 = "bfloat16", "float16", "float32", "int32", "uint16"
 ROUNDS, PH = 6, 4
 MV = 10
 SH = 16
 AREA0, AREAD = 13312, 4352
-RWN = AREA0 + AREAD * 4 + 256
+RWN = AREA0 + AREAD * 3 + 256
 DDN = 4384
+PIECES = ((0, 40), (40, 104), (104, 152), (152, 204), (204, 256))
+BIG = 2097152.0
 
 SCRATCH = {}
 
@@ -19,27 +21,30 @@ def _buf(where, dtype, *names):
         SCRATCH[n[0]] = (where, [128, n[1]], dtype)
 
 
-_buf("sbuf", B16, ("RW", RWN), ("CAPS", 1024), ("SL", 1024), ("DD", DDN), ("E1", 4096), ("E2", 4096), ("X", 4096), ("SEG", 4096), ("TT", 256), ("FL", 256),
-     ("F2", 256), ("MN", 256), ("A1", 256), ("A2", 256), ("EX", 256), ("EXP", 256), ("JK", 256), ("MR", 1024), ("SG", 2048), ("EQ", 2176))
-_buf("sbuf", F32, ("W", 1280), ("BC", 1024), ("OFA", 256), ("OFB", 256), ("EQT", 256), ("DF", 256), ("T1", 256), ("EXD", 256), ("EXN", 256), ("PLT", 16), ("SM", 256),
-     ("PBF", 256), ("SX", 256), ("S16F", 160), ("TW", 256), ("NW", 256))
-_buf("sbuf", I32, ("BRI", 1024), ("YL", 1024), ("KI", 256), ("S16I", 224), ("UI", 256), ("PI1", 256), ("PI2", 256), ("WTI", 1), ("KAI", 1), ("I1", 8))
-_buf("sbuf", U16, ("OFFS", 256), ("IDX", 16), ("POF", 256), ("PBU", 256), ("LST", 16), ("LSD", 16), ("LID", 16), ("LLN", 16))
-_buf("sbuf", B16, ("IB", 256), ("IB15", 256), ("IB4", 256), ("MSKD", 256), ("NEGM", 256), ("BB", 128), ("BB4", 128), ("WB", 128), ("O8K", 8), ("O8S", 8), ("O8N", 8), ("O8M", 8), ("O8W", 8),
-     ("BSM", 128), ("ID", 128), ("IDN", 128), ("CK", 256), ("ONE", 128), ("C37", 128), ("ZR", 256))
-_buf("sbuf", F32, ("F1", 24), ("NMSK", 256), ("TRIM", 256), ("SEGM", 256), ("KR", 256), ("KAX", 256), ("BBF", 128), ("O8F", 8), ("CIX", 16), ("TRX", 16), ("TRD", 16), ("IDF", 128), ("O16", 128), ("NWN", 256))
-SCRATCH.update({"KRW": ("sbuf", [2, 128], I32), "KH": ("sbuf", [2, 128], I32), "KL": ("sbuf", [2, 128], I32), "KHF": ("sbuf", [2, 128], F32), "KLF": ("sbuf", [2, 128], F32), "KC": ("sbuf", [2, 256], B16)})
+_buf("sbuf", B16, ("RW", RWN), ("CAPS", 1024), ("SL", 1024), ("DD", DDN), ("E1", 4096), ("E2", 4096), ("X", 4096), ("SEG", 4096), ("TABD", 4096), ("TT", 256),
+     ("FL", 256), ("F2", 256), ("MN", 256), ("A1", 256), ("A2", 256), ("EX", 256), ("JK", 256), ("TG", 256), ("SN", 256), ("SN2", 256), ("NN", 256), ("POS", 256),
+     ("SG", 2048), ("EQ", 2176), ("C2", 2048), ("AB", 2560))
+_buf("sbuf", F16, ("PB", 256), ("EXD", 256), ("O8H", 8), ("IDH", 128), ("ONH", 128), ("KC", 128))
+_buf("sbuf", F32, ("W", 1280), ("BRE", 1024), ("YLE", 1024), ("DF", 256), ("T1", 256), ("SX", 256), ("S16F", 96), ("TW", 256), ("NW", 256), ("UZ", 32))
+_buf("sbuf", I32, ("BRI", 1024), ("YL", 1024), ("KB", 1024), ("KI", 256), ("S16I", 112), ("UI", 256), ("PI1", 256), ("PI2", 256), ("PR", 32), ("WTI", 1), ("KAI", 1), ("I1", 8),
+     ("KRW", 128))
+_buf("sbuf", U16, ("OFFS", 256), ("IDX", 16), ("POF", 256), ("PLU", 16), ("LST", 16), ("LSD", 16), ("LID", 16), ("LLN", 16))
+_buf("sbuf", B16, ("IB", 256), ("IB15", 256), ("IB4", 256), ("MSKD", 256), ("MSK4", 256), ("NEGM", 256), ("NEG2", 256), ("BB", 128), ("BBH", 128), ("TRI", 128), ("WB", 128),
+     ("O8K", 8), ("O8S", 8), ("O8N", 8), ("O8M", 8), ("O8C", 8), ("BSM", 128), ("IDS", 1024), ("CK", 256), ("ONE", 512), ("ZR", 256), ("CV", 1024), ("CS", 256))
+_buf("sbuf", F32, ("F1", 24), ("NMSK", 256), ("SEGM", 256), ("KR", 256), ("KAX", 256), ("BBF", 128), ("CIX", 16), ("TRX", 16), ("TRX2", 16), ("TRD", 16), ("IDF", 128), ("O16", 128),
+     ("NWN", 256), ("IOT", 1024), ("TP", 1024))
 _buf("psum", F32, ("pk", 512), ("pb", 512), ("pn", 512), ("pc", 512), ("pd", 2048))
-for _f in range(PH):
-    _buf("sbuf", B16, ("CX%d" % _f, 4096))
 for _r in range(1, ROUNDS + 1):
-    _buf("sbuf", B16, ("MO%d" % _r, 256), ("LD%d" % _r, 256))
-ALIAS = {n: ("F1", c, 1) for c, n in enumerate(("PIF", "LNF", "GRF", "LREV", "LN16", "OMP", "WTF", "KAF", "LIM", "FC", "SC", "H1", "H2", "LP0", "LP1", "LP2", "LP3"))}
+    _buf("sbuf", B16, ("MO%d" % _r, 256), ("LD%d" % _r, 1024))
+ALIAS = {n: ("F1", c, 1) for c, n in enumerate(("PIF", "LNF", "GRF", "LN16", "LNX", "WTF", "KAF", "LIM", "FC", "SC", "H1", "H2"))}
 ALIAS.update({n: ("I1", c, 1) for c, n in enumerate(("PIX", "LNI", "GRI"))})
-ALIAS.update({n: ("S16I", 16 * c, 16) for c, n in enumerate(("TA", "TB", "U", "U2", "BS", "P2", "PL", "UT0", "UT", "UT2", "BST", "PLI", "PL3"))})
-ALIAS.update({n: ("S16F", 16 * c, 16) for c, n in enumerate(("TAF", "P1", "PLF", "L1", "L2", "L3", "L4", "PZ", "PQ"))})
+ALIAS.update({n: ("S16I", 16 * c, 16) for c, n in enumerate(("TA", "TB", "U", "U2", "BS", "PL"))})
+ALIAS.update({n: ("S16F", 16 * c, 16) for c, n in enumerate(("PLF", "L1", "L2", "L3", "L4"))})
+ALIAS.update({n: ("IDS", 128 * c, 128) for c, n in enumerate(("ID", "IDN", "IDT", "IDM", "IDP", "IDQ", "ID16", "IDC"))})
+CONST = (("K16", 16.0), ("KP2", -BIG - 65536.0), ("KBG", BIG), ("KHB", BIG / 2), ("KNB", -BIG), ("K32", 32768.0), ("K37", 37.0), ("K1K", 1024.0))
+ALIAS.update({n: ("CV", 128 * c, 128) for c, (n, v) in enumerate(CONST)})
 PSUM = ("pk", "pb", "pn", "pc", "pd")
-LOADS = ["lcap", "lbr", "lres", "lwt", "lka", "lk0", "lk1"]
+LOADS = ["lcap", "lbr", "lres", "lwt", "lka", "lkr"]
 SEMAPHORES = ["sV", "sS", "sP", "sG", "sent", "oyr", "oyb"] + LOADS + ["arr%d" % r for r in range(1, ROUNDS + 1)]
 
 
@@ -174,218 +179,253 @@ def rank_program(g, core, T, topo):
         else:
             op("G", lambda: g.iota(out["ap"], pattern, base, cm, allow_small_or_imprecise_dtypes=True), [out], [])
 
-    def gcopy(a, b, n):
-        op("G", lambda: g.affine_select(a["ap"], b["ap"], [[0, n]], OP.is_gt, 0.0, 1, 0), [a], [b])
+    def select(a, b, pattern, o, base, cm):
+        op("G", lambda: g.affine_select(a["ap"], b["ap"], pattern, o, 0.0, base, cm), [a], [b])
 
-    def widen(f, k, q, h=None):
-        if h is None:
-            a, b = R("CX%d" % f, k, 4096, 16), R("CAPS", f, 1024, 4)
-        else:
-            a, b = R("CX%d" % f, 2048 * h + k, 2048 * h + 2048, 16), R("CAPS", 512 * h + f, 512 * h + 512, 4)
-        if q == "G":
-            gcopy(a, b, 256 if h is None else 128)
-        elif q == "V":
-            cp(a, b)
-        else:
-            act(a, b, AF.Copy)
+    def gcopy(a, b, n):
+        select(a, b, [[0, n]], OP.is_gt, 1, 0)
+
+    def row(name, a=0, b=None):
+        return R(name, a, b, 1, 1)
+
+    def const(out, name, start, stop):
+        mm(out, row(name), row("ONE", 0, out["r"][0][2] - out["r"][0][1]), start, stop)
 
     sc["dma"]("Y", "lbr", R("BRI")["ap"], T.br[:], [R("BRI")], [])
-    sc["dma"]("S", "lcap", R("CAPS")["ap"], T.cap[:], [R("CAPS")], [])
     x = R("RW", SH, SH + 2304)
     sc["dma"]("Y", "lres", x["ap"], T.res[:], [x], [])
+    sc["dma"]("Y", "lcap", R("CAPS")["ap"], T.cap[:], [R("CAPS")], [])
+    sc["dma"]("S", "lkr", row("KRW")["ap"], T.ka[:], [R("KRW")], [])
     sc["dma"]("S", "lwt", R("WTI")["ap"], T.wt[:], [R("WTI")], [])
     sc["dma"]("S", "lka", R("KAI")["ap"], T.ka[:], [R("KAI")], [])
-    for p in (0, 1):
-        g.scalar.dma_start(T.KRW[p:p + 1, :], T.ka[:]).then_inc(T.sem["lk%d" % p], 16)
-        sc["record"]("lk%d" % p, 16, [], [("KRW", p, p + 1, 1, 0)], "S")
 
     iota(R("PIX"), [[0, 1]], 0, 1)
     iota(R("IB15"), [[0, 16], [1, 16]], 0, 0)
-    iota(R("IB4"), [[1, 16], [0, 16]], 0, 0)
     iota(R("IB"), [[1, 256]], 0, 0)
-    for k in range(4):
-        widen(0, k, "G", 1)
+    iota(R("IB4"), [[1, 16], [0, 16]], 0, 0)
     iota(R("CIX"), [[256, 16]], 15, 0)
     iota(R("TRX"), [[16, 16]], 1024, 0)
     iota(R("TRD"), [[16, 16]], 4128, 0)
-    iota(R("NWN"), [[1, 256]], AREA0 - AREAD, 0)
     ms(R("RW", 0, SH), 0.0)
     ms(R("DD", 0, 16), 0.0)
     ms(R("DD", 4112, DDN), 0.0)
     ms(R("LIM"), 4.0)
-    ms(R("ONE"), 1.0)
     ts(R("LNI"), R("PIX"), 15, None, OP.bitwise_and)
     ts(R("GRI"), R("PIX"), 4, None, OP.arith_shift_right)
     cp(R("PIF"), R("PIX"))
+    ms(R("UZ"), 0.0)
+    ts(R("SEG", 0, 256), R("IB15"), 768.0, -256.0, OP.mult, OP.add)
     cp(R("LNF"), R("LNI"))
+    cp(R("SEG", 256, 512), R("SEG", 0, 256))
     cp(R("GRF"), R("GRI"))
-    ts(R("SEG", 0, 256), R("IB15"), 0.0, 768.0, OP.is_gt, OP.mult)
-    ts(R("SEG", 0, 256), R("SEG", 0, 256), -256.0, None, OP.add)
-
-    def halves(f):
-        ts(R("YL", f, 1024, 4), R("BRI", f, 1024, 4), 65535, None, OP.bitwise_and)
-        ts(R("KI"), R("BRI", f, 1024, 4), 4095, None, OP.bitwise_and)
-        ts(R("BC", 256 * f, 256 * f + 256), R("KI"), float(SH), None, OP.add)
-
-    def code(f, t, out, q, tiles=None):
-        a, b = (R("pn", 0, 256), R("pc", 0, 256)) if q == "V" else (R(tiles[0]), R(tiles[1]))
-        ts(a, R("BRI", f, 1024, 4), float(-65536 * (t - 1)), -8192.0, OP.is_lt, OP.mult)
-        ts(b, R("YL", f, 1024, 4), float(4096 * t), -8192.0, OP.is_lt, OP.mult)
-        bc = R("BC", 256 * f, 256 * f + 256)
-        if q == "V":
-            tt(R("DF"), bc, a, OP.add)
-            tt(out, R("DF"), b, OP.add)
-        else:
-            s = R("pd", 512 * q, 512 * q + 256)
-            mm(s, R("IDF"), bc, True, False)
-            mm(s, R("ID"), a, False, False)
-            mm(s, R("ID"), b, False, True)
-            act(out, s, AF.Copy)
-    for n in (256, 512):
-        act(R("SEG", n, 2 * n), R("SEG", 0, n), AF.Copy)
+    cp(R("SEG", 512, 1024), R("SEG", 0, 512))
     for n in (1024, 2048):
-        gcopy(R("SEG", n, 2 * n), R("SEG", 0, n), n)
-    iota(R("C37"), [[0, 128]], 37, 0)
-    iota(R("ZR"), [[0, 256]], 0, 0)
-    iota(R("W", 1024, 1280), [[0, 256]], 0, 0)
+        act(R("SEG", n, 2 * n), R("SEG", 0, n), AF.Copy)
+    ts(R("MSKD"), R("IB15"), R("LNF"), None, OP.is_equal)
+    ts(R("ID"), R("IB", 0, 128), R("PIF"), None, OP.is_equal)
+    ts(R("O8K"), R("IB", 0, 8), R("GRF"), 16.0, OP.is_equal, OP.mult)
+    ts(row("CK"), row("IB15"), -1.0, 15.0, OP.mult, OP.add)
+    ms(row("ONE"), 1.0)
+    ts(R("IDN"), R("ID"), -1.0, None, OP.mult)
+    ts(R("O8C"), R("O8K"), -1.0, None, OP.mult)
+    ts(R("SEGM"), R("IB15"), 0.0, None, OP.is_gt)
+    cp(R("LID"), R("IB", 0, 16))
+    ts(R("BB"), R("IB4", 0, 128), R("GRF"), None, OP.is_equal)
+    ts(R("MSK4"), R("IB4"), R("LNF"), None, OP.is_equal)
+    ts(R("LLN"), R("IB", 0, 16), 0.0, R("LNF"), OP.mult, OP.add)
     cp(R("WTF"), R("WTI"))
     cp(R("KAF"), R("KAI"))
-    for k in range(4, 16):
-        widen(0, k, "S", 1)
-    for k in range(11, 16):
-        widen(0, k, "S", 0)
-    halves(0)
-    code(0, 1, R("W", 0, 1024, 4), "V")
-    cp(R("OFFS"), R("W", 0, 1024, 4))
-    for k in range(11):
-        widen(0, k, "V", 0)
+    cp(row("KC"), row("KRW"))
+    gcopy(R("TABD", 0, 256), R("MSKD"), 256)
 
-    def key_constants():
-        ts(R("ID"), R("IB", 0, 128), R("PIF"), None, OP.is_equal)
-        ts(R("IDN"), R("ID"), -1.0, None, OP.mult)
-        ts(R("O8K"), R("IB", 0, 8), R("GRF"), 16.0, OP.is_equal, OP.mult)
-        ts(R("BB"), R("IB4", 0, 128), R("GRF"), None, OP.is_equal)
-        aff(R("CK"), R("IB15"), -1.0, 15.0)
+    def widen(f):
+        for s in (0, 1):
+            gcopy(R("C2", 512 * f + s, 512 * f + 512, 2), R("CAPS", f, 1024, 4), 256)
+
+    ts(R("pn", 0, 256), R("BRI", 0, 1024, 4), 4096.0, 8192.0 + SH, OP.is_ge, OP.mult)
+    ts(R("KI"), R("BRI", 0, 1024, 4), 4095, None, OP.bitwise_and)
+    tt(R("DF"), R("KI"), R("pn", 0, 256), OP.add)
+    ts(R("OFFS"), R("DF"), -8192.0, None, OP.add)
+    for n in (256, 512):
+        gcopy(R("TABD", n, 2 * n), R("TABD", 0, n), n)
+    widen(0)
+    for n in (1024, 2048):
+        gcopy(R("TABD", n, 2 * n), R("TABD", 0, n), n)
+    iota(R("W", 1024, 1280), [[0, 256]], 0, 0)
+    iota(R("ZR"), [[0, 256]], 0, 0)
 
     def late_constants():
         aff(R("IDF"), R("ID"), 1.0)
         aff(R("O8M"), R("O8K"), -0.0625)
         aff(R("LN16"), R("LNF"), 16.0)
         aff(R("CIX"), R("CIX"), 1.0, R("LN16"))
-        aff(R("LREV"), R("LNF"), -1.0, 15.0)
-        ts(R("MSKD"), R("IB15"), R("LNF"), None, OP.is_equal)
-        cp(R("LID"), R("IB", 0, 16))
-        ts(R("SEGM"), R("IB15"), 0.0, None, OP.is_gt)
-        aff(R("NEGM"), R("MSKD"), 2097152.0, -2097152.0)
-        aff(R("O16"), R("ONE"), 0.0625)
-        aff(R("NMSK"), R("MSKD"), -1.0, 1.0)
-        aff(R("KHF"), R("CK", 0, 128, 1, 2), 1024.0)
-        aff(R("OMP"), R("PIF"), -1.0, 1.0)
-        aff(R("BB4"), R("BB"), 8192.0)
-        aff(R("WB"), R("BB"), R("WTF"))
-        aff(R("O8F"), R("O8K"), 0.0625)
-        aff(R("O8W"), R("O8F"), R("WTF"))
+        aff(R("O16"), R("ID"), 0.0, 0.0625)
+        aff(R("KR"), R("MSK4"), R("KAF"))
         aff(R("BBF"), R("BB"), 1.0)
+        aff(R("BSM"), R("BB"), -16384.0)
+        aff(R("BBH"), R("BB"), 65536.0)
+        select(R("BSM"), R("BSM"), [[0, 8], [1, 16]], OP.is_ge, -MV, 0)
+        select(R("TRI"), R("BBH"), [[1, 128]], OP.is_gt, 0, -1)
+
+    def flight_constants():
+        aff(R("NEGM"), R("MSKD"), BIG, -BIG)
+        aff(R("WB"), R("BB"), R("WTF"))
         aff(R("O8S"), R("O8K"), 1024.0)
         aff(R("O8N"), R("O8K"), -1024.0)
+        aff(R("LNX"), R("LNF"), 1.0, 16.0)
+        mm(R("pd", 0, 256), R("BBF"), R("KR"), True, True)
+        aff(R("KAX"), R("pd", 0, 256), 1.0)
 
-    def score_constants():
-        ts(R("LLN"), R("IB", 0, 16), 0.0, R("LNF"), OP.mult, OP.add)
-        ts(R("BSM"), R("IB15", 0, 128), float(MV), 16384.0, OP.is_ge, OP.mult)
-        ts(R("KR"), R("IB4"), R("LNF"), R("KAF"), OP.is_equal, OP.mult)
-        mm(R("pk", 0, 256), R("BBF"), R("KR"), True, True)
-        tt(R("BSM"), R("BSM"), R("BB"), OP.mult)
-        aff(R("KAX"), R("pk", 0, 256), 1.0)
-
-    def parent_constants():
-        ts(R("KH"), R("KRW"), 768, None, OP.bitwise_and)
-        ts(R("KL"), R("KRW"), 255, None, OP.bitwise_and)
-        tt(R("KHF"), R("KHF"), R("KH"), OP.add)
-        ts(R("KLF"), R("KL"), R("PIF", 0, 1, 1, 2), None, OP.mult)
-        ts(R("KHF"), R("KHF"), R("OMP", 0, 1, 1, 2), None, OP.mult)
-        ts(R("TRIM"), R("IB15"), R("LNF"), 2097152.0, OP.is_le, OP.mult)
-        tt(R("KC", 0, 128), R("KHF"), R("KLF"), OP.add)
-        tt(R("NWN"), R("NWN"), R("NEGM"), OP.add)
-        cp(R("KC", 128, 256), R("KC", 0, 128))
+    def small_constants():
+        for n, v in CONST:
+            ms(row(n), v)
+        ms(row("ONH"), 1.0)
+        ts(row("CS"), row("IB15"), float(MV), 1008.0 * 16384, OP.is_ge, OP.mult)
+        ts(R("O8H"), R("IB", 0, 8), R("GRF"), None, OP.is_equal)
+        cp(R("IDH"), R("ID"))
 
     def list_constants():
         aff(R("TRX"), R("TRX"), 1.0, R("LNF"))
         aff(R("TRD"), R("TRD"), 1.0, R("LNF"))
-        for c in range(4):
-            aff(R("LP%d" % c), R("LNF"), 1.0, 16.0 - 4 * c)
+        aff(R("ID16"), R("ID"), 16.0)
+        aff(R("NEG2"), R("NEGM"), 16.0, R("LNX"))
 
-    def room(f, c, rooms, res):
-        o = 1024 * (c % 2)
-        for b in (0, 512):
-            if rooms:
-                mm(R("pd", o + b, o + b + 512), R("IDN" if c else "ID"), R("CX%d" % f, 1024 * c + b, 1024 * c + b + 512), True, not c)
-        for b in (0, 512):
-            if res:
-                mm(R("pd", o + b, o + b + 512), R("ID"), R("DD", 16 + 1024 * c + b, 528 + 1024 * c + b), False, True)
+    def word_constants():
+        s = R("pd", 0, 256)
+        mm(s, R("ID"), R("NEGM"), True, False)
+        mm(s, row("ONE", 0, 128), row("IB"), False, True)
+        aff(R("NWN"), s, 1.0, float(AREA0 - AREAD))
+        for n, v in (("IDM", -BIG), ("IDP", BIG), ("IDQ", BIG / 2), ("IDC", -32768.0)):
+            aff(R(n), R("ID"), v)
+        aff(R("NMSK"), R("MSKD"), -1.0, 1.0)
+        aff(R("TRX2"), R("TRX"), 1.0, R("LNX"))
 
-    word_steps = [lambda: tt(R("L1"), R("SX", 15, 256, 16), R("TRX"), OP.min),
-                  lambda: tt(R("L2"), R("L1"), R("PLF"), OP.max),
-                  lambda: cp(R("LST"), R("L2")),
-                  lambda: tt(R("TW"), IND(R("W"), R("LST")), R("NMSK"), OP.mult),
-                  lambda: tt(IND(R("W"), R("LST")), R("TW"), R("NW"), OP.add)]
+    def tests(t):
+        f, o = (t - 1) % PH, 512 * (t - 2)
+        act(R("AB", o, o + 256), R("BRE", f, 1024, 4), AF.Relu, -4096.0, -268435456.0 * t)
+        act(R("AB", o + 256, o + 512), R("YLE", f, 1024, 4), AF.Relu, -4096.0, -16777216.0 * (528 - t))
+
+    def code_sum(t, s, stop):
+        o = 512 * (t - 2)
+        const(s, "K16", True, False)
+        mm(s, R("IDN"), R("AB", o, o + 256), False, False)
+        mm(s, R("IDN"), R("AB", o + 256, o + 512), False, stop)
+
+    def code(t, s):
+        f = (t - 1) % PH
+        tt(R("W", f, 1024, 4), R("KB", f, 1024, 4), s, OP.add)
+
+    def bank(j):
+        if j in (1, 2, 7):
+            return R("pn" if j == 2 else "pb")
+        return R("pd", 512 * (j - 3), 512 * (j - 2))
+
+    def rooms(f, js):
+        for j in js:
+            mm(bank(j), R("IDN"), R("C2", 512 * f, 512 * f + 512), True, False)
+
+    def rooms2(f):
+        mm(R("pc"), R("ID"), R("C2", 512 * f, 512 * f + 512), True, True)
+        mm(R("pk", 0, 256), row("ONE", 0, 128), row("CK"), True, False)
+        for h in (0, 1):
+            for k in (0, 8):
+                mm(R("pk", 128 * h + k, 128 * h + 128, 16), R("CAPS", 512 * h + f, 512 * h + 512, 4), R("O8C"), False, False)
+
+    def row_keys(j, last=False):
+        for h in (0, 1):
+            for s in (0, 1):
+                mm(R("pk", 128 * h + j + 8 * s, 128 * h + 128, 16), R("X", 512 * j + 256 * h + s, 512 * j + 256 * h + 256, 2), R("O8K"), False, last and h + s == 2)
+
+    def key_start():
+        mm(R("pk", 0, 256), row("ONE", 0, 128), row("CS"), True, False)
+        mm(R("pk", 0, 256), row("K1K"), row("CK"), False, False)
+        for h in (0, 1):
+            mm(R("pk", 128 * h, 128 * h + 128), row("ONH"), row("KC"), False, False)
+
+    def gather(t, a, b):
+        win = R("RW", 0, AREA0 + AREAD * (t - 2) + 256 if t > 1 else SH + 2304)
+        act(R("DD", 16 + 16 * a, 16 + 16 * b), IND(win, R("OFFS", a, b)), AF.Copy)
 
     sent = 0
     for t in range(1, ROUNDS + 1):
         f = (t - 1) % PH
         f2 = t % PH
-        wf, capf = R("W", f, 1024, 4), R("CAPS", f, 1024, 4)
+        wf, capf, cap_p = R("W", f, 1024, 4), R("CAPS", f, 1024, 4), R("pc", 0, 512, 2)
+        p1, p2 = R("pd", 1536, 1792), R("pc", 0, 256)
         if t == 1:
             win = R("RW", 0, SH + 2304)
-            for c in (0, 1):
-                cp(R("DD", 16 + 1024 * c, 1040 + 1024 * c), IND(win, R("OFFS", 64 * c, 64 * c + 64)))
-            for c in (2, 3):
-                act(R("DD", 16 + 1024 * c, 1040 + 1024 * c), IND(win, R("OFFS", 64 * c, 64 * c + 64)), AF.Copy)
-            key_constants()
-            room(0, 0, True, False)
-            room(0, 1, True, False)
-        mm(R("pk", 0, 256), R("ONE", 0, 128, 1, 1), R("CK", 0, 256, 1, 1), True, False)
-        mm(R("pc", 256, 512), R("ID"), capf, True, True)
-        room(f, 1, False, True)
-        tt(R("X", 0, 1024), R("DD", 16, 1040), R("pd", 0, 1024), OP.max)
-        mm(R("pn", 0, 256), R("ID"), R("DD", 31, 4112, 16), True, True)
-        room(f, 2, True, True)
-        act(R("X", 1024, 2048), R("pd", 1024, 2048), AF.Relu)
-        room(f, 3, True, True)
-        act(R("X", 2048, 3072), R("pd", 0, 1024), AF.Relu)
-        act(R("X", 3072, 4096), R("pd", 1024, 2048), AF.Relu)
+            cp(R("DD", 16, 2064), IND(win, R("OFFS", 0, 128)))
+            act(R("DD", 2064, 4112), IND(win, R("OFFS", 128, 256)), AF.Copy)
+            rooms(0, (1, 2, 3, 4, 5, 6))
+            rooms2(0)
+
+        def add_rows(j):
+            mm(bank(j), R("ID"), R("DD", 16 + j, 4112, 8), False, True)
+
+        def relu(j, n):
+            act(R("X", 512 * j, 512 * (j + n)), bank(j) if n == 1 else R("pd", 512 * (j - 3), 512 * (j - 1)), AF.Relu)
+        tt(R("X", 0, 512), R("DD", 16, 4112, 8), R("pc"), OP.max)
+        for j in (1, 2, 3, 4):
+            add_rows(j)
+        relu(1, 1)
+        relu(2, 1)
+        relu(3, 2)
+        row_keys(0)
+        add_rows(5)
+        add_rows(6)
+        relu(5, 2)
+        row_keys(1)
+        rooms(f, (7,))
+        add_rows(7)
+        relu(7, 1)
+        for j in (2, 3, 4, 5, 6, 7):
+            row_keys(j, j == 7)
         scan(R("E1"), R("DD", 15, 4111), R("SEG"), OP.max, OP.min)
         scan(R("E2", 0, 4096, -1), R("DD", 17, 4113, -1), R("SEG"), OP.max, OP.min)
-        tt(R("TT"), R("E1", 15, 4096, 16), R("pn", 0, 256), OP.max)
-        if t > 1:
-            word_steps[0]()
-        tt(R("FL"), R("TT"), R("pc", 256, 512), OP.is_gt)
-        if t > 1:
-            word_steps[1]()
-            word_steps[2]()
-        for h in (0, 1):
-            for k in range(16):
-                mm(R("pk", 128 * h + k, 128 * h + 128, 16), R("X", 2048 * h + k, 2048 * h + 2048, 16), R("O8K"), False, h == 1 and k == 15)
-            if h == 0:
-                mm(R("pb", 0, 256), R("BB"), R("FL"), True, True)
         if t == 1:
             late_constants()
         mm(R("pn", 256, 272), R("IDF"), R("CIX"), True, False)
-        ts(R("pb", 0, 256), R("pb", 0, 256), R("LIM"), -512.0, OP.is_gt, OP.mult)
-        tt(R("MN"), R("TT"), R("pb", 0, 256), OP.add)
+        tt(R("TT"), R("E1", 15, 4096, 16), R("DD", 31, 4112, 16), OP.max)
         scan(R("KI"), R("SEGM"), R("pk", 0, 256), OP.mult, OP.max)
+        tt(R("FL"), R("TT"), cap_p, OP.is_gt)
+        mm(R("pb", 0, 256), R("BB"), R("FL"), True, True)
         ts(R("TA"), R("KI", 15, 256, 16), 15, None, OP.bitwise_and)
+        if t > 1:
+            ts(R("L1"), R("SX", 15, 256, 16), 65536.0, 4096.0, OP.is_ge, OP.mult)
         tt(R("EX"), IND(R("TA"), R("LID")), R("MSKD"), OP.mult)
-        cp(R("TAF"), R("TA"))
         for h in (0, 1):
             mm(R("pn", 256 + 8 * h, 264 + 8 * h), R("EX", 128 * h, 128 * h + 128), R("O8M"), False, h == 1)
-        act(R("EXP"), IND(R("TAF"), R("LID")), AF.Copy)
+        ts(R("pb", 0, 256), R("pb", 0, 256), R("LIM"), -512.0, OP.is_gt, OP.mult)
         cp(R("IDX"), R("pn", 256, 272))
+        tt(R("MN"), R("TT"), R("pb", 0, 256), OP.add)
+        if t > 1:
+            key_start()
+            mm(p1, R("IDF"), R("YLE", f, 1024, 4), True, False)
+            mm(R("pd", 512, 768), R("ID"), capf, True, False)
         tt(R("A1"), IND(R("E1"), R("IDX")), R("MN"), OP.max)
+        if t > 1:
+            tt(R("L2"), R("L1"), R("PLF"), OP.max)
         tt(R("A2"), IND(R("E2"), R("IDX")), R("A1"), OP.max)
-        tt(R("F2"), R("A2"), R("pc", 256, 512), OP.is_gt)
+        if t > 1:
+            tt(R("L3"), R("L2"), R("TRX"), OP.min)
+        tt(R("F2"), R("A2"), cap_p, OP.is_gt)
         mm(R("pn", 0, 256), R("BB"), R("F2"), True, True)
+        if t > 1:
+            cp(R("LST"), R("L3"))
+        if t < ROUNDS:
+            act(R("JK"), R("pb", 0, 256), AF.Copy, scale=-1.0 / 512, acc=R("FC"))
+        else:
+            act(R("JK"), R("pb", 0, 256), AF.Copy, scale=-1.0 / 512)
+        aff(R("IDT"), R("ID"), -65536.0 * (t + 4))
+        if t == 1:
+            flight_constants()
+        if t == 2:
+            word_constants()
+        if t > 1:
+            aff(R("NW"), R("NWN"), 1.0, float(AREAD * (t - 1)))
+            act(R("TW"), IND(R("W"), R("LST")), AF.Copy)
         ts(R("pn", 0, 256), R("pn", 0, 256), R("LIM"), None, OP.is_le)
-        mo, ld = R("MO%d" % t), R("LD%d" % t)
+        mo, ld, mr = R("MO%d" % t), R("LD%d" % t, 0, 256), "LD%d" % t
         tt(mo, R("A2"), R("pn", 0, 256), OP.mult)
         dst = T.cores[(rank + 1 + (t - 1) % 7) % 8]
         ne = len(topo.engines(core, dst))
@@ -394,31 +434,35 @@ def rank_program(g, core, T, topo):
         g.remote_dma(ld["ap"], mo["ap"], T.sem["arr%d" % t], T.sem["sent"], pid, rid, topo.mask(core, dst))
         sent += ne
         sc["record"]("arr%d" % t, ne, [], ld["w"], None)
-        if t < PH:
-            for k in range(16):
-                widen(t, k, "G")
         if t == 1:
-            for b in (0, 512):
-                mm(R("pd", 1024 + b, 1536 + b), R("ID"), R("CAPS", b, b + 512), True, False)
-                mm(R("pd", 1024 + b, 1536 + b), R("IDN"), R("RW", SH + b, SH + b + 512), False, True)
-            act(R("SL"), R("pd", 1024, 2048), AF.Relu)
-        for h in (0, 1):
-            mm(R("pd", 128 * h, 128 * h + 128), R("EXP", 128 * h, 128 * h + 128), R("ID"), True, True)
-        mm(R("pd", 512, 768), R("ID"), capf, True, False)
-        mm(R("pd", 512, 768), R("IDN"), mo, False, True)
-        act(R("SL", f, 1024, 4), R("pd", 512, 768), AF.Relu)
-        act(R("RW", SH + f, SH + 1024, 4), mo, AF.Copy)
-        if t == 1:
-            score_constants()
-        else:
-            word_steps[3]()
-        ts(R("EQT"), R("pd", 0, 256), R("LREV"), 128.0 * (t + 4), OP.is_equal, OP.mult)
+            iota(R("IOT"), [[1, 1024]], 0, 0)
+            iota(R("TP"), [[1, 256], [1024, 4]], 0, 0)
+        if 2 < t < ROUNDS:
+            gcopy(R("RW", AREA0 + AREAD * (t - 3), AREA0 + AREAD * (t - 3) + 256), R("ZR"), 256)
         if t > 1:
-            word_steps[4]()
-        tg, b2, sm, bf = R("pd", 1536, 1792), R("pd", 1792, 2048), R("SM"), R("BRI", f, 1024, 4)
-        tt(tg, R("EQT"), R("pb", 0, 256), OP.mult)
+            tt(IND(R("W"), R("LST")), R("TW"), R("NW"), OP.max)
+        else:
+            ts(R("BRE"), R("BRI"), -65536.0, None, OP.add)
+            ts(R("YL"), R("BRI"), 65535, None, OP.bitwise_and)
+            small_constants()
+            ts(R("YLE"), R("YL"), -65536.0 - BIG, None, OP.add)
+            ts(R("KB"), R("BRI"), 4095, None, OP.bitwise_and)
+        tt(R("TG"), IND(R("TABD"), R("IDX")), R("JK"), OP.mult)
+        sn = R("SN2" if t == 2 else "SN")
+        if t == 1:
+            act(R("RW", SH + f, SH + 1024, 4), mo, AF.Copy)
+            for b in (0, 512):
+                mm(R("pd", b, b + 512), R("ID"), R("CAPS", b, b + 512), True, False)
+                mm(R("pd", b, b + 512), R("IDN"), R("RW", SH + b, SH + b + 512), False, True)
+            act(R("SL"), R("pd", 0, 1024), AF.Relu)
+        else:
+            mm(R("pd", 512, 768), R("IDN"), mo, False, True)
+            act(R("SL", f, 1024, 4), R("pd", 512, 768), AF.Relu)
+            act(R("RW", SH + f, SH + 1024, 4), mo, AF.Copy)
+            act(sn, wf, AF.Sign, 1.0, -4095.5)
+        mm(R("pn", 0, 256), R("ID"), R("NEGM"), True, False)
+        mm(R("pn", 0, 256), row("K37"), row("IB"), False, False)
         if t < ROUNDS:
-            act(R("JK"), R("pb", 0, 256), AF.Copy, scale=-1.0 / 512, acc=R("FC"))
             mm(R("pd", 1024, 1025), R("O16"), R("FC"), True, True)
             aff(R("SC"), R("pd", 1024, 1025), 1.0)
             aff(R("H1"), R("SC"), 0.5, 8388608.0)
@@ -428,144 +472,173 @@ def rank_program(g, core, T, topo):
         else:
             y = R("RW", SH, SH + 1024)
             sc["dma"]("Y", "oyr", T.yr[:], y["ap"], [], [y])
+        if 1 < t < ROUNDS:
+            cp(R("OFFS"), R("W", f2, 1024, 4))
+        bre = R("BRE", f, 1024, 4)
         if t == 1:
-            for c, tiles in ((1, ("MN", "A1")), (2, ("FL", "F2")), (3, ("A2", "EX"))):
-                halves(c)
-                code(c, c + 1, R("W", c, 1024, 4), 1 + c % 2, tiles)
-            code(0, 5, R("OFA"), 1, ("MN", "A1"))
-            code(1, 6, R("OFB"), 2, ("FL", "F2"))
-            parent_constants()
-        yf = R("YL", f, 1024, 4)
-        if t > 1:
-            if t < ROUNDS:
-                cp(R("OFFS"), R("W", f2, 1024, 4))
-            tt(b2, yf, tg, OP.add)
-            ts(sm, wf, 4096.0, None, OP.is_ge)
-            tt(b2, bf, b2, OP.min)
-            if t == 2:
-                tt(R("EQT"), R("OFB"), tg, OP.add)
-            own = [lambda: tt(R("DF"), wf, tg, OP.add), lambda: tt(tg, R("DF"), b2, OP.subtract),
-                   lambda: tt(R("DF"), sm, tg, OP.mult), lambda: tt(bf if t == 2 else wf, R("DF"), b2, OP.add)]
-            if t == 2:
-                own += [lambda: ts(sm, sm, 2097152.0, None, OP.mult), lambda: tt(yf, yf, sm, OP.max),
-                        lambda: tt(wf, R("EQT"), sm, OP.subtract)]
+            key_start()
+            for r in (2, 5, 3, 4):
+                tests(r)
+            code_sum(2, R("pd", 512, 768), True)
+            code(2, R("pd", 512, 768))
+            cp(R("OFFS"), R("W", f2, 1024, 4))
+            mm(p1, R("IDF"), R("YLE", f, 1024, 4), True, False)
+            mm(p1, R("IDT"), R("TG"), False, False)
+            const(p1, "KBG", False, True)
+            code_sum(5, p2, False)
+            mm(p2, R("IDT"), R("TG"), False, True)
+            tt(bre, bre, p1, OP.min)
+            code(5, p2)
+            code_sum(3, R("pd", 0, 256), True)
+            code_sum(4, R("pd", 512, 768), True)
+            code(3, R("pd", 0, 256))
+            code(4, R("pd", 512, 768))
         else:
-            own = [lambda: tt(b2, yf, tg, OP.add), lambda: tt(wf, R("OFA"), tg, OP.add), lambda: tt(bf, bf, b2, OP.min)]
-        mm(R("pn", 0, 256), R("ID"), R("NEGM"), True, False)
-        mm(R("pn", 0, 256), R("C37", 0, 128, 1, 1), R("IB", 0, 256, 1, 1), False, False)
-        mm(R("pk", 0, 256), R("ONE", 0, 128, 1, 1), R("ZR", 0, 256, 1, 1), True, False)
+            if t == 2:
+                tests(6)
+            if t == 6:
+                const(p1, "KHB", False, False)
+                mm(p1, R("IDQ"), R("SN2"), False, False)
+            const(p2, "KP2", True, False)
+            mm(p2, R("IDF"), wf, False, False)
+            mm(p1, R("IDT"), R("TG"), False, False)
+            mm(p1, R("IDM"), sn, False, True)
+            mm(p2, R("IDT"), R("TG"), False, False)
+            mm(p2, R("IDP"), sn, False, True)
+            tt(R("DF"), bre, p1, OP.min)
+            tt(bre if t == 2 else wf, R("DF"), p2, OP.max)
+            if t == 2:
+                s = R("pd", 512, 768)
+                code_sum(6, s, False)
+                const(s, "KNB", False, False)
+                mm(s, R("IDT"), R("TG"), False, False)
+                mm(s, R("IDM"), sn, False, True)
+                code(6, s)
         mm(R("pn", 0, 256), R("WB"), ld, False, True)
-        for h in (0, 1):
-            mm(R("pk", 128 * h, 128 * h + 128), R("LD%d" % t, 128 * h, 128 * h + 128), R("BSM"), False, False)
-        for k in range(4):
-            act(R("MR", 256 * k, 256 * k + 256), ld, AF.Copy)
+        act(R("NN"), ld, AF.Relu, -1.0, 63.0)
+        act(R(mr, 256, 512), ld, AF.Copy)
+        act(R(mr, 512, 1024), R(mr, 0, 512), AF.Copy)
         if t < ROUNDS:
-            act(R("RW", SH + 1024 + 256 * (t - 1), SH + 1280 + 256 * (t - 1)), ld, AF.Copy)
-            act(R("RW", AREA0 + AREAD * (t - 1), AREA0 + AREAD * (t - 1) + 256), ld, AF.Copy)
-            if t > 2:
-                act(R("RW", AREA0 + AREAD * (t - 3), AREA0 + AREAD * (t - 3) + 256), R("ZR"), AF.Copy)
+            gcopy(R("RW", SH + 1024 + 256 * (t - 1), SH + 1280 + 256 * (t - 1)), ld, 256)
+            if t < ROUNDS - 1:
+                gcopy(R("RW", AREA0 + AREAD * (t - 1), AREA0 + AREAD * (t - 1) + 256), ld, 256)
+            gather(t, *PIECES[0])
+        if t < PH:
+            widen(t)
+        for h in (0, 1):
+            mm(R("pk", 128 * h, 128 * h + 128), R("NN", 128 * h, 128 * h + 128), R("BSM"), False, False)
+        for m in range(16 - MV):
+            mm(R("pd", 256 * m, 256 * m + 256), R("IDN"), R("NN"), m % 2 == 0, False)
+        if t == ROUNDS:
+            act(R("AB", 0, 1024), R("W", 0, 1024), AF.Sign, 1.0, 0.5)
+            for b, s in ((0, R("pd", 1536, 2048)), (512, R("pc"))):
+                mm(s, R("IDF"), R("W", b, b + 512), True, False)
+                const(s, "K32", False, False)
+                mm(s, R("IDC"), R("AB", b, b + 512), False, True)
         scan(R("UI"), R("SEGM"), R("pn", 0, 256), OP.mult, OP.max)
         ts(R("U"), R("UI", 15, 256, 16), 4095, None, OP.bitwise_and)
         tt(R("U2"), R("U"), R("U"), OP.mult)
         tt(R("T1"), IND(R("U"), R("LLN")), R("KAX"), OP.mult)
         ts(R("BS"), R("U2"), 5, None, OP.arith_shift_right)
+        cp(R("UZ", 1, 32, 2), R("U"))
         tt(R("PI1"), IND(R("BS"), R("LLN")), R("T1"), OP.add)
+        cp(R("pb", 257, 288, 2), R("BS"))
         ts(R("PI2"), R("PI1"), 1023, None, OP.bitwise_and)
         cp(R("POF"), R("PI2"))
-        def pieces(a, b):
-            return [(o, min(512, b - o)) for o in range(a, b, 512)]
-        for o, n in pieces(0, 256 * (16 - MV)):
-            mm(R("pd", o, o + n), R("ID"), R("MR", 0, n), True, False)
-        for h in (0, 1):
-            mm(R("pn", 256 + 8 * h, 264 + 8 * h), R("LD%d" % t, 128 * h, 128 * h + 128), R("O8W"), True, False)
-            mm(R("pn", 256 + 8 * h, 264 + 8 * h), R("IB", 128 * h, 128 * h + 128, 1, 1), R("C37", 0, 8, 1, 1), False, True)
 
-        def keys(m0, n, r):
+        def keys(m0, n, r, last=False):
             for mc in range(m0, m0 + n):
                 for h in (0, 1):
-                    mm(R("pk", 128 * h + mc, 128 * h + 128, 16), R("X", 256 * mc + 128 * h, 256 * mc + 128 * h + 128), r, False, False)
-        spl = [(m0, min(4, 16 - m0)) for m0 in range(MV, 16, 4)]
-        vpl = [(m0, min(4, MV - m0)) for m0 in range(0, MV, 4)]
-        for m0, n in spl:
+                    mm(R("pk", 128 * h + mc, 128 * h + 128, 16), R("X", 256 * mc + 128 * h, 256 * mc + 128 * h + 128), r, False, last and h == 1 and mc == m0 + n - 1)
+
+        def s_gather(m0):
             o = 256 * (m0 - MV)
-            act(R("SG", o, o + 256 * n), IND(R("SL"), R("POF", 16 * m0, 16 * (m0 + n))), AF.Copy)
-        for e, (m0, n) in enumerate(vpl):
-            tt(R("X", 256 * m0, 256 * (m0 + n)), IND(R("SL"), R("POF", 16 * m0, 16 * (m0 + n))), R("MR", 0, 256 * n), OP.min)
-            keys(m0, n, R("O8S"))
-            if e < len(spl):
-                m1, n1 = spl[e]
-                for o, w in pieces(256 * (m1 - MV), 256 * (m1 - MV + n1)):
-                    mm(R("pd", o, o + w), R("IDN"), R("SG", o, o + w), False, True)
-                act(R("X", 256 * m1, 256 * (m1 + n1)), R("pd", 256 * (m1 - MV), 256 * (m1 - MV + n1)), AF.Relu)
-        for m0, n in spl:
-            keys(m0, n, R("O8N"))
-        mm(R("pk", 0, 256), R("ONE", 0, 128, 1, 2), R("KC"), False, True)
-        act(R("NW"), R("NWN"), AF.Relu, 1.0, float(AREAD * t))
+            act(R("SG", o, o + 512), IND(R("SL"), R("POF", 16 * m0, 16 * m0 + 32)), AF.Copy)
+
+        def s_sub(m0):
+            o = 256 * (m0 - MV)
+            mm(R("pd", o, o + 512), R("IDN"), R("SG", o, o + 512), False, True)
+
+        def s_relu(m0):
+            o = 256 * (m0 - MV)
+            act(R("X", 256 * m0, 256 * m0 + 512), R("pd", o, o + 512), AF.Relu, 1.0, 63.0)
+
+        def v_score(m0, n):
+            tt(R("X", 256 * m0, 256 * (m0 + n)), IND(R("SL"), R("POF", 16 * m0, 16 * (m0 + n))), R(mr, 0, 256 * n), OP.min)
+        s_gather(10)
+        s_gather(12)
+        v_score(0, 4)
+        v_score(4, 3)
+        v_score(7, 2)
+        v_score(9, 1)
+        s_sub(10)
+        s_relu(10)
+        keys(0, 4, R("O8S"))
+        s_sub(12)
+        s_gather(14)
+        keys(10, 2, R("O8N"))
+        s_relu(12)
+        keys(4, 3, R("O8S"))
+        s_sub(14)
+        s_relu(14)
+        keys(7, 2, R("O8S"))
+        keys(12, 2, R("O8N"))
+        keys(9, 1, R("O8S"))
+        keys(14, 2, R("O8N"), True)
         if t == 1:
             list_constants()
-        def gather(c):
-            win = R("RW", 0, AREA0 + AREAD * (t - 1) + 256)
-            act(R("DD", 16 + 1024 * c, 1040 + 1024 * c), IND(win, R("OFFS", 64 * c, 64 * c + 64)), AF.Copy)
         if t < ROUNDS:
-            if t == 1:
-                cp(R("OFFS"), R("W", f2, 1024, 4))
-            gather(0)
-            room(f2, 0, True, False)
-        turned = [lambda: cp(R("UT0"), R("pn", 256, 272)), lambda: ts(R("UT"), R("UT0"), 4095, None, OP.bitwise_and),
-                  lambda: tt(R("UT2"), R("UT"), R("UT"), OP.mult), lambda: ts(R("BST"), R("UT2"), 5, None, OP.arith_shift_right)]
-        for e in range(4):
-            turned[e]()
-            if e < 3:
-                own[e]()
+            gather(t, *PIECES[1])
+            rooms(f2, (3, 4, 5, 6))
+        else:
+            act(R("W", 0, 512), R("pd", 1536, 2048), AF.Copy)
+            act(R("W", 512, 1024), R("pc"), AF.Copy)
+            act(R("NW"), R("NWN"), AF.Relu, 1.0, float(AREAD * t))
         scan(R("KI"), R("SEGM"), R("pk", 0, 256), OP.mult, OP.max)
         ts(R("TB"), R("KI", 15, 256, 16), 1023, None, OP.bitwise_and)
-        tt(R("P1"), R("UT"), R("TB"), OP.mult)
-        tt(R("P2"), R("P1"), R("BST"), OP.add)
-        ts(R("PL"), R("P2"), 1023, None, OP.bitwise_and)
-        cp(R("PLT"), R("PL"))
-        tt(R("EXD"), IND(R("PL"), R("LID")), R("MSKD"), OP.mult)
-        act(R("EXN"), IND(R("PLT"), R("LID")), AF.Copy)
-        if t < ROUNDS:
-            for c in (1, 2, 3):
-                gather(c)
+        tt(R("EXD"), IND(R("TB"), R("LID")), R("MSKD"), OP.mult)
         for h in (0, 1):
-            mm(R("pc", 8 * h, 8 * h + 8), R("EXD", 128 * h, 128 * h + 128), R("O8F"), True, True)
-        for h in (0, 1):
-            mm(R("pb", 128 * h, 128 * h + 128), R("EXN", 128 * h, 128 * h + 128), R("IDF"), True, True)
-        mm(R("pn", 0, 256), R("ID"), R("NEGM"), True, False)
-        for e in own[3:]:
-            e()
+            mm(R("pb", 256 + 16 * h, 272 + 16 * h, 2), R("EXD", 128 * h, 128 * h + 128), R("O8H"), True, True)
+        mm(R("pn", 0, 256), R("ID"), R("NEG2"), True, False)
         if t < ROUNDS:
-            room(f2, 1, True, False)
-        cp(R("PLF"), R("pc", 0, 16))
+            rooms2(f2)
+            gather(t, *PIECES[2])
+        scan(R("PR"), R("UZ"), R("pb", 256, 288), OP.mult, OP.add)
         if t < ROUNDS:
-            cp(R("PLI"), R("pc", 0, 16))
-            ts(R("PQ"), R("PLF"), 4.0, R("LP%d" % f2), OP.mult, OP.add)
-            ts(R("PL3"), R("PLI"), 3, None, OP.bitwise_and)
-        cp(R("PBU"), R("pb", 0, 256))
+            rooms(f2, (1,))
+        ts(R("PL"), R("PR", 1, 32, 2), 1023, None, OP.bitwise_and)
+        cp(R("PLU"), R("PL"))
+        cp(R("PLF"), R("PL"))
+        cp(R("PB"), IND(R("IOT"), R("PLU")))
         if t < ROUNDS:
-            ts(R("PZ"), R("PL3"), float(f2), 8192.0, OP.not_equal, OP.mult)
+            act(R("POS"), IND(R("TP"), R("PLU")), AF.Abs, 1.0, -1024.0 * f2)
+            gather(t, *PIECES[3])
+            gather(t, *PIECES[4])
         o = 0
         for q in range(15):
             n = 240 - 16 * q
-            if q == 1 and t < ROUNDS:
-                tt(R("PZ"), R("PQ"), R("PZ"), OP.add)
-            ts(R("EQ", o, o + n), R("PBU", 256 - n, 256), R("PLF", q, q + 1), None, OP.is_equal)
-            mm(R("pn", 256 - n, 256), R("BB4"), R("EQ", o, o + n), False, q == 14)
+            ts(R("EQ", o, o + n), R("PB", 256 - n, 256), R("PLF", q, q + 1), None, OP.is_equal)
+            mm(R("pn", 256 - n, 256), R("BBH"), R("EQ", o, o + n), False, q == 14)
             o += n
-            if q == 1:
-                tt(R("PBF"), R("pb", 0, 256), R("TRIM"), OP.add)
-                tt(R("EQ", 1920, 2176), IND(R("PLF"), R("LID")), R("PBF"), OP.is_equal)
-                mm(R("pn", 0, 256), R("BB4"), R("EQ", 1920, 2176), False, False)
+            if q == 2:
+                tt(R("EQ", 1920, 2176), IND(R("PLF"), R("LID")), R("PB"), OP.is_equal)
+                mm(R("pn", 0, 256), R("TRI"), R("EQ", 1920, 2176), False, False)
+            if q == 8:
+                if t < ROUNDS:
+                    mm(R("pn", 0, 256), R("ID16"), R("POS"), False, False)
+                else:
+                    mm(R("pn", 0, 256), R("IDH"), R("PB"), False, False)
         scan(R("SX"), R("SEGM"), R("pn", 0, 256), OP.mult, OP.max)
         if t < ROUNDS:
-            tt(R("L3"), R("SX", 15, 256, 16), R("PZ"), OP.max)
-            tt(R("L4"), R("L3"), R("TRD"), OP.min)
+            rooms(f2, (2,))
+            tt(R("L4"), R("SX", 15, 256, 16), R("TRD"), OP.min)
             cp(R("LSD"), R("L4"))
             out = IND(R("DD"), R("LSD"))
             op("V", lambda: g.vector.tensor_copy(out["ap"], ld["ap"]), [out], [ld])
-    for step in word_steps:
-        step()
+    tt(R("L4"), R("SX", 15, 256, 16), R("TRX2"), OP.min)
+    ts(R("LST"), R("L4"), R("LNX"), None, OP.subtract)
+    tt(R("TW"), IND(R("W"), R("LST")), R("NMSK"), OP.mult)
+    tt(IND(R("W"), R("LST")), R("TW"), R("NW"), OP.add)
     y = R("W", 0, 1024)
     sc["dma"]("Y", "oyb", T.yb[:], y["ap"], [], [y])
     g.sync.wait_ge(T.sem.oyb, 16)

@@ -22,7 +22,7 @@ def _buf(where, dtype, *names):
 
 
 _buf("sbuf", B16, ("RW", RWN), ("CAPS", 1024), ("SL", 1024), ("DD", DDN), ("E1", 4096), ("E2", 4096), ("X", 4096), ("SEG", 4096), ("TABD", 4096), ("TT", 256),
-     ("FL", 256), ("F2", 256), ("MN", 256), ("A1", 256), ("A2", 256), ("EX", 256), ("JK", 256), ("TG", 256), ("SN", 256), ("SN2", 256), ("NN", 256), ("POS", 256),
+     ("FL", 256), ("FR", 256), ("F2", 256), ("MN", 256), ("A1", 256), ("A2", 256), ("EX", 256), ("JK", 256), ("TG", 256), ("SN", 256), ("SN2", 256), ("NN", 256), ("POS", 256),
      ("SG", 2048), ("EQ", 2176), ("C2", 2048), ("AB", 2560))
 _buf("sbuf", F16, ("PB", 256), ("EXD", 256), ("O8H", 8), ("IDH", 128), ("ONH", 128), ("KC", 128))
 _buf("sbuf", F32, ("W", 1280), ("BRE", 1024), ("YLE", 1024), ("DF", 256), ("T1", 256), ("SX", 256), ("S16F", 96), ("TW", 256), ("NW", 256), ("UZ", 32))
@@ -30,17 +30,17 @@ _buf("sbuf", I32, ("BRI", 1024), ("YL", 1024), ("KB", 1024), ("KI", 256), ("S16I
      ("KRW", 128))
 _buf("sbuf", U16, ("OFFS", 256), ("IDX", 16), ("POF", 256), ("PLU", 16), ("LST", 16), ("LSD", 16), ("LID", 16), ("LLN", 16))
 _buf("sbuf", B16, ("IB", 256), ("IB15", 256), ("IB4", 256), ("MSKD", 256), ("MSK4", 256), ("NEGM", 256), ("NEG2", 256), ("BB", 128), ("BBH", 128), ("TRI", 128), ("WB", 128),
-     ("O8K", 8), ("O8S", 8), ("O8N", 8), ("O8M", 8), ("O8C", 8), ("BSM", 128), ("IDS", 1024), ("CK", 256), ("ONE", 512), ("ZR", 256), ("CV", 1024), ("CS", 256))
-_buf("sbuf", F32, ("F1", 24), ("NMSK", 256), ("SEGM", 256), ("KR", 256), ("KAX", 256), ("BBF", 128), ("CIX", 16), ("TRX", 16), ("TRX2", 16), ("TRD", 16), ("IDF", 128), ("O16", 128),
+     ("O8K", 8), ("O8S", 8), ("O8N", 8), ("O8M", 8), ("O8C", 8), ("BSM", 128), ("IDS", 1152), ("CK", 256), ("ONE", 512), ("ZR", 256), ("CV", 1024), ("CS", 256))
+_buf("sbuf", F32, ("F1", 24), ("SEGM", 256), ("KR", 256), ("KAX", 256), ("BBF", 128), ("CIX", 16), ("TRX", 16), ("TRX2", 16), ("TRD", 16), ("IDF", 128), ("O16", 128),
      ("NWN", 256), ("IOT", 1024), ("TP", 1024))
 _buf("psum", F32, ("pk", 512), ("pb", 512), ("pn", 512), ("pc", 512), ("pd", 2048))
 for _r in range(1, ROUNDS + 1):
     _buf("sbuf", B16, ("MO%d" % _r, 256), ("LD%d" % _r, 1024))
-ALIAS = {n: ("F1", c, 1) for c, n in enumerate(("PIF", "LNF", "GRF", "LN16", "LNX", "WTF", "KAF", "LIM", "FC", "SC", "H1", "H2"))}
+ALIAS = {n: ("F1", c, 1) for c, n in enumerate(("PIF", "LNF", "GRF", "LN16", "LNX", "WTF", "KAF", "LIM", "NLM", "FC", "SC", "H1", "H2"))}
 ALIAS.update({n: ("I1", c, 1) for c, n in enumerate(("PIX", "LNI", "GRI"))})
 ALIAS.update({n: ("S16I", 16 * c, 16) for c, n in enumerate(("TA", "TB", "U", "U2", "BS", "PL"))})
 ALIAS.update({n: ("S16F", 16 * c, 16) for c, n in enumerate(("PLF", "L1", "L2", "L3", "L4"))})
-ALIAS.update({n: ("IDS", 128 * c, 128) for c, n in enumerate(("ID", "IDN", "IDT", "IDM", "IDP", "IDQ", "ID16", "IDC"))})
+ALIAS.update({n: ("IDS", 128 * c, 128) for c, n in enumerate(("ID", "IDN", "IDT", "IDM", "IDP", "IDQ", "ID16", "IDC", "IDK"))})
 CONST = (("K16", 16.0), ("KP2", -BIG - 65536.0), ("KBG", BIG), ("KHB", BIG / 2), ("KNB", -BIG), ("K32", 32768.0), ("K37", 37.0), ("K1K", 1024.0))
 ALIAS.update({n: ("CV", 128 * c, 128) for c, (n, v) in enumerate(CONST)})
 PSUM = ("pk", "pb", "pn", "pc", "pd")
@@ -210,6 +210,7 @@ def rank_program(g, core, T, topo):
     ms(R("DD", 0, 16), 0.0)
     ms(R("DD", 4112, DDN), 0.0)
     ms(R("LIM"), 4.0)
+    ms(R("NLM"), -4.0)
     ts(R("LNI"), R("PIX"), 15, None, OP.bitwise_and)
     ts(R("GRI"), R("PIX"), 4, None, OP.arith_shift_right)
     cp(R("PIF"), R("PIX"))
@@ -258,7 +259,10 @@ def rank_program(g, core, T, topo):
         aff(R("IDF"), R("ID"), 1.0)
         aff(R("O8M"), R("O8K"), -0.0625)
         aff(R("LN16"), R("LNF"), 16.0)
+        aff(R("IDK"), R("ID"), -512.0)
         aff(R("CIX"), R("CIX"), 1.0, R("LN16"))
+
+    def late_constants2():
         aff(R("O16"), R("ID"), 0.0, 0.0625)
         aff(R("KR"), R("MSK4"), R("KAF"))
         aff(R("BBF"), R("BB"), 1.0)
@@ -266,6 +270,10 @@ def rank_program(g, core, T, topo):
         aff(R("BBH"), R("BB"), 65536.0)
         select(R("BSM"), R("BSM"), [[0, 8], [1, 16]], OP.is_ge, -MV, 0)
         select(R("TRI"), R("BBH"), [[1, 128]], OP.is_gt, 0, -1)
+        aff(row("CS"), row("ONE", 0, 256), 1008.0 * 16384)
+        select(row("CS"), row("CS"), [[0, 16], [1, 16]], OP.is_ge, -MV, 0)
+        for n, v in CONST:
+            aff(row(n), row("ONE", 0, 128), v)
 
     def flight_constants():
         aff(R("NEGM"), R("MSKD"), BIG, -BIG)
@@ -276,14 +284,6 @@ def rank_program(g, core, T, topo):
         mm(R("pd", 0, 256), R("BBF"), R("KR"), True, True)
         aff(R("KAX"), R("pd", 0, 256), 1.0)
 
-    def small_constants():
-        for n, v in CONST:
-            ms(row(n), v)
-        ms(row("ONH"), 1.0)
-        ts(row("CS"), row("IB15"), float(MV), 1008.0 * 16384, OP.is_ge, OP.mult)
-        ts(R("O8H"), R("IB", 0, 8), R("GRF"), None, OP.is_equal)
-        cp(R("IDH"), R("ID"))
-
     def list_constants():
         aff(R("TRX"), R("TRX"), 1.0, R("LNF"))
         aff(R("TRD"), R("TRD"), 1.0, R("LNF"))
@@ -291,13 +291,16 @@ def rank_program(g, core, T, topo):
         aff(R("NEG2"), R("NEGM"), 16.0, R("LNX"))
 
     def word_constants():
-        s = R("pd", 0, 256)
+        s = R("pd", 1024, 1280)
         mm(s, R("ID"), R("NEGM"), True, False)
         mm(s, row("ONE", 0, 128), row("IB"), False, True)
+        aff(R("IDM"), R("ID"), -BIG)
+        aff(R("IDP"), R("ID"), BIG)
         aff(R("NWN"), s, 1.0, float(AREA0 - AREAD))
-        for n, v in (("IDM", -BIG), ("IDP", BIG), ("IDQ", BIG / 2), ("IDC", -32768.0)):
-            aff(R(n), R("ID"), v)
-        aff(R("NMSK"), R("MSKD"), -1.0, 1.0)
+
+    def last_constants():
+        aff(R("IDQ"), R("ID"), BIG / 2)
+        aff(R("IDC"), R("ID"), -32768.0)
         aff(R("TRX2"), R("TRX"), 1.0, R("LNX"))
 
     def tests(t):
@@ -324,23 +327,55 @@ def rank_program(g, core, T, topo):
         for j in js:
             mm(bank(j), R("IDN"), R("C2", 512 * f, 512 * f + 512), True, False)
 
+    def first_rooms():
+        for j in range(1, 7):
+            name, a, b = bank(j)["r"][0][:3]
+            for s in (0, 1):
+                mm(R(name, a + s, b, 2), R("IDN"), R("CAPS", 0, 1024, 4), s == 0, False)
+
     def rooms2(f):
-        mm(R("pc"), R("ID"), R("C2", 512 * f, 512 * f + 512), True, True)
+        mm(R("pc", 0, 256), R("ID"), R("CAPS", f, 1024, 4), True, True)
+        mm(R("pc", 256, 512), R("IDN"), R("CAPS", f, 1024, 4), True, False)
         mm(R("pk", 0, 256), row("ONE", 0, 128), row("CK"), True, False)
         for h in (0, 1):
-            for k in (0, 8):
-                mm(R("pk", 128 * h + k, 128 * h + 128, 16), R("CAPS", 512 * h + f, 512 * h + 512, 4), R("O8C"), False, False)
+            mm(R("pk", 128 * h, 128 * h + 128, 16), R("CAPS", 512 * h + f, 512 * h + 512, 4), R("O8C"), False, False)
+
+    def add_rows(j):
+        mm(bank(j), R("ID"), R("DD", 16 + j, 4112, 8), False, True)
+
+    def relu(j, n):
+        act(R("X", 512 * j, 512 * (j + n)), bank(j) if n == 1 else R("pd", 512 * (j - 3), 512 * (j - 1)), AF.Relu)
 
     def row_keys(j, last=False):
         for h in (0, 1):
             for s in (0, 1):
                 mm(R("pk", 128 * h + j + 8 * s, 128 * h + 128, 16), R("X", 512 * j + 256 * h + s, 512 * j + 256 * h + 256, 2), R("O8K"), False, last and h + s == 2)
 
+    def suffix(a, b):
+        scan(R("E2", a, b, -1), R("DD", 17 + a, 17 + b, -1), R("SEG", 0, b - a), OP.max, OP.min)
+
     def key_start():
         mm(R("pk", 0, 256), row("ONE", 0, 128), row("CS"), True, False)
         mm(R("pk", 0, 256), row("K1K"), row("CK"), False, False)
         for h in (0, 1):
             mm(R("pk", 128 * h, 128 * h + 128), row("ONH"), row("KC"), False, False)
+
+    def keys(m0, n, r, last=False):
+        for mc in range(m0, m0 + n):
+            for h in (0, 1):
+                mm(R("pk", 128 * h + mc, 128 * h + 128, 16), R("X", 256 * mc + 128 * h, 256 * mc + 128 * h + 128), r, False, last and h == 1 and mc == m0 + n - 1)
+
+    def s_gather(m0):
+        o = 256 * (m0 - MV)
+        act(R("SG", o, o + 512), IND(R("SL"), R("POF", 16 * m0, 16 * m0 + 32)), AF.Copy)
+
+    def s_sub(m0):
+        o = 256 * (m0 - MV)
+        mm(R("pd", o, o + 512), R("IDN"), R("SG", o, o + 512), False, True)
+
+    def s_relu(m0):
+        o = 256 * (m0 - MV)
+        act(R("X", 256 * m0, 256 * m0 + 512), R("pd", o, o + 512), AF.Relu, 1.0, 63.0)
 
     def gather(t, a, b):
         win = R("RW", 0, AREA0 + AREAD * (t - 2) + 256 if t > 1 else SH + 2304)
@@ -350,27 +385,24 @@ def rank_program(g, core, T, topo):
     for t in range(1, ROUNDS + 1):
         f = (t - 1) % PH
         f2 = t % PH
-        wf, capf, cap_p = R("W", f, 1024, 4), R("CAPS", f, 1024, 4), R("pc", 0, 512, 2)
+        wf, capf, cap_p = R("W", f, 1024, 4), R("CAPS", f, 1024, 4), R("pc", 0, 256)
         p1, p2 = R("pd", 1536, 1792), R("pc", 0, 256)
         if t == 1:
             win = R("RW", 0, SH + 2304)
             cp(R("DD", 16, 2064), IND(win, R("OFFS", 0, 128)))
             act(R("DD", 2064, 4112), IND(win, R("OFFS", 128, 256)), AF.Copy)
-            rooms(0, (1, 2, 3, 4, 5, 6))
             rooms2(0)
-
-        def add_rows(j):
-            mm(bank(j), R("ID"), R("DD", 16 + j, 4112, 8), False, True)
-
-        def relu(j, n):
-            act(R("X", 512 * j, 512 * (j + n)), bank(j) if n == 1 else R("pd", 512 * (j - 3), 512 * (j - 1)), AF.Relu)
-        tt(R("X", 0, 512), R("DD", 16, 4112, 8), R("pc"), OP.max)
-        for j in (1, 2, 3, 4):
-            add_rows(j)
+            first_rooms()
+        tt(R("X", 0, 512, 2), R("DD", 16, 4112, 16), cap_p, OP.max)
+        add_rows(1)
+        add_rows(2)
+        mm(R("pc", 256, 512), R("ID"), R("DD", 24, 4112, 16), False, True)
+        add_rows(3)
+        add_rows(4)
         relu(1, 1)
         relu(2, 1)
+        act(R("X", 1, 512, 2), R("pc", 256, 512), AF.Relu)
         relu(3, 2)
-        row_keys(0)
         add_rows(5)
         add_rows(6)
         relu(5, 2)
@@ -378,52 +410,65 @@ def rank_program(g, core, T, topo):
         rooms(f, (7,))
         add_rows(7)
         relu(7, 1)
-        for j in (2, 3, 4, 5, 6, 7):
-            row_keys(j, j == 7)
         scan(R("E1"), R("DD", 15, 4111), R("SEG"), OP.max, OP.min)
-        scan(R("E2", 0, 4096, -1), R("DD", 17, 4113, -1), R("SEG"), OP.max, OP.min)
+        suffix(0, 512)
+        tt(R("TT"), R("E1", 15, 4096, 16), R("DD", 31, 4112, 16), OP.max)
+        suffix(512, 1024)
+        tt(R("FL"), R("TT"), cap_p, OP.is_gt)
+        suffix(1024, 4096)
+        for j in (0, 2, 3, 4, 5, 6, 7):
+            row_keys(j, j == 7)
         if t == 1:
             late_constants()
+        mm(R("pd", 512, 768), R("BB"), R("FL"), True, True)
+        act(R("FR"), R("pd", 512, 768), AF.Relu, 1.0, R("NLM"))
         mm(R("pn", 256, 272), R("IDF"), R("CIX"), True, False)
-        tt(R("TT"), R("E1", 15, 4096, 16), R("DD", 31, 4112, 16), OP.max)
+        mm(R("pd", 0, 256), R("ID"), R("TT"), True, False)
+        mm(R("pd", 0, 256), R("IDK"), R("FR"), False, True)
+        act(R("MN"), R("pd", 0, 256), AF.Copy)
+        act(R("JK"), R("FR"), AF.Sign, acc=R("FC") if t < ROUNDS else None)
+        if t == 1:
+            late_constants2()
+        if t == 2:
+            word_constants()
+            tests(6)
+        if t == 3:
+            last_constants()
         scan(R("KI"), R("SEGM"), R("pk", 0, 256), OP.mult, OP.max)
-        tt(R("FL"), R("TT"), cap_p, OP.is_gt)
-        mm(R("pb", 0, 256), R("BB"), R("FL"), True, True)
-        ts(R("TA"), R("KI", 15, 256, 16), 15, None, OP.bitwise_and)
         if t > 1:
             ts(R("L1"), R("SX", 15, 256, 16), 65536.0, 4096.0, OP.is_ge, OP.mult)
+        ts(R("TA"), R("KI", 15, 256, 16), 15, None, OP.bitwise_and)
+        if t > 1:
+            tt(R("L2"), R("L1"), R("PLF"), OP.max)
+        else:
+            ms(row("ONH"), 1.0)
         tt(R("EX"), IND(R("TA"), R("LID")), R("MSKD"), OP.mult)
         for h in (0, 1):
             mm(R("pn", 256 + 8 * h, 264 + 8 * h), R("EX", 128 * h, 128 * h + 128), R("O8M"), False, h == 1)
-        ts(R("pb", 0, 256), R("pb", 0, 256), R("LIM"), -512.0, OP.is_gt, OP.mult)
+        if t > 1:
+            tt(R("L3"), R("L2"), R("TRX"), OP.min)
+            cp(R("LST"), R("L3"))
+        else:
+            ts(R("O8H"), R("IB", 0, 8), R("GRF"), None, OP.is_equal)
+            cp(R("IDH"), R("ID"))
         cp(R("IDX"), R("pn", 256, 272))
-        tt(R("MN"), R("TT"), R("pb", 0, 256), OP.add)
+        aff(R("IDT"), R("ID"), -65536.0 * (t + 4))
         if t > 1:
             key_start()
             mm(p1, R("IDF"), R("YLE", f, 1024, 4), True, False)
             mm(R("pd", 512, 768), R("ID"), capf, True, False)
-        tt(R("A1"), IND(R("E1"), R("IDX")), R("MN"), OP.max)
-        if t > 1:
-            tt(R("L2"), R("L1"), R("PLF"), OP.max)
-        tt(R("A2"), IND(R("E2"), R("IDX")), R("A1"), OP.max)
-        if t > 1:
-            tt(R("L3"), R("L2"), R("TRX"), OP.min)
-        tt(R("F2"), R("A2"), cap_p, OP.is_gt)
-        mm(R("pn", 0, 256), R("BB"), R("F2"), True, True)
-        if t > 1:
-            cp(R("LST"), R("L3"))
-        if t < ROUNDS:
-            act(R("JK"), R("pb", 0, 256), AF.Copy, scale=-1.0 / 512, acc=R("FC"))
-        else:
-            act(R("JK"), R("pb", 0, 256), AF.Copy, scale=-1.0 / 512)
-        aff(R("IDT"), R("ID"), -65536.0 * (t + 4))
-        if t == 1:
-            flight_constants()
-        if t == 2:
-            word_constants()
-        if t > 1:
             aff(R("NW"), R("NWN"), 1.0, float(AREAD * (t - 1)))
             act(R("TW"), IND(R("W"), R("LST")), AF.Copy)
+        else:
+            flight_constants()
+        if t < ROUNDS:
+            mm(R("pd", 1024, 1025), R("O16"), R("FC"), True, True)
+            aff(R("SC"), R("pd", 1024, 1025), 1.0)
+        tt(R("A1"), IND(R("E1"), R("IDX")), R("MN"), OP.max)
+        tt(R("A2"), IND(R("E2"), R("IDX")), R("A1"), OP.max)
+        tt(R("F2"), R("A2"), cap_p, OP.is_gt)
+        mm(R("pn", 0, 256), R("BB"), R("F2"), True, True)
+        tt(R("TG"), IND(R("TABD"), R("IDX")), R("JK"), OP.mult)
         ts(R("pn", 0, 256), R("pn", 0, 256), R("LIM"), None, OP.is_le)
         mo, ld, mr = R("MO%d" % t), R("LD%d" % t, 0, 256), "LD%d" % t
         tt(mo, R("A2"), R("pn", 0, 256), OP.mult)
@@ -442,12 +487,10 @@ def rank_program(g, core, T, topo):
         if t > 1:
             tt(IND(R("W"), R("LST")), R("TW"), R("NW"), OP.max)
         else:
-            ts(R("BRE"), R("BRI"), -65536.0, None, OP.add)
             ts(R("YL"), R("BRI"), 65535, None, OP.bitwise_and)
-            small_constants()
+            ts(R("BRE"), R("BRI"), -65536.0, None, OP.add)
             ts(R("YLE"), R("YL"), -65536.0 - BIG, None, OP.add)
             ts(R("KB"), R("BRI"), 4095, None, OP.bitwise_and)
-        tt(R("TG"), IND(R("TABD"), R("IDX")), R("JK"), OP.mult)
         sn = R("SN2" if t == 2 else "SN")
         if t == 1:
             act(R("RW", SH + f, SH + 1024, 4), mo, AF.Copy)
@@ -462,67 +505,66 @@ def rank_program(g, core, T, topo):
             act(sn, wf, AF.Sign, 1.0, -4095.5)
         mm(R("pn", 0, 256), R("ID"), R("NEGM"), True, False)
         mm(R("pn", 0, 256), row("K37"), row("IB"), False, False)
-        if t < ROUNDS:
-            mm(R("pd", 1024, 1025), R("O16"), R("FC"), True, True)
-            aff(R("SC"), R("pd", 1024, 1025), 1.0)
-            aff(R("H1"), R("SC"), 0.5, 8388608.0)
-            aff(R("H2"), R("H1"), -2.0, 16777216.0)
-            act(R("H1"), R("SC"), AF.Abs, 1.0, R("H2"))
-            aff(R("LIM"), R("H1"), 1.0, 4.0)
-        else:
+        limit = [lambda: aff(R("H1"), R("SC"), 0.5, 8388608.0), lambda: aff(R("H2"), R("H1"), -2.0, 16777216.0), lambda: act(R("H1"), R("SC"), AF.Abs, 1.0, R("H2")),
+                 lambda: aff(R("LIM"), R("H1"), 1.0, 4.0), lambda: aff(R("NLM"), R("H1"), -1.0, -4.0)] if t < ROUNDS else [lambda: None] * 5
+        if t == ROUNDS:
             y = R("RW", SH, SH + 1024)
             sc["dma"]("Y", "oyr", T.yr[:], y["ap"], [], [y])
         if 1 < t < ROUNDS:
             cp(R("OFFS"), R("W", f2, 1024, 4))
-        bre = R("BRE", f, 1024, 4)
         if t == 1:
-            key_start()
             for r in (2, 5, 3, 4):
                 tests(r)
+            key_start()
             code_sum(2, R("pd", 512, 768), True)
             code(2, R("pd", 512, 768))
             cp(R("OFFS"), R("W", f2, 1024, 4))
-            mm(p1, R("IDF"), R("YLE", f, 1024, 4), True, False)
-            mm(p1, R("IDT"), R("TG"), False, False)
-            const(p1, "KBG", False, True)
-            code_sum(5, p2, False)
-            mm(p2, R("IDT"), R("TG"), False, True)
-            tt(bre, bre, p1, OP.min)
-            code(5, p2)
-            code_sum(3, R("pd", 0, 256), True)
-            code_sum(4, R("pd", 512, 768), True)
-            code(3, R("pd", 0, 256))
-            code(4, R("pd", 512, 768))
-        else:
-            if t == 2:
-                tests(6)
+        bre, p3, p4 = R("BRE", f, 1024, 4), R("pb", 0, 256), R("pc", 256, 512)
+
+        def word_sums():
+            if t == 1:
+                mm(p1, R("IDF"), R("YLE", f, 1024, 4), True, False)
+                mm(p1, R("IDT"), R("TG"), False, False)
+                const(p1, "KBG", False, True)
+                code_sum(5, p2, False)
+                mm(p2, R("IDT"), R("TG"), False, True)
+                code_sum(3, p3, True)
+                code_sum(4, p4, True)
+                return [lambda: tt(bre, bre, p1, OP.min), lambda: code(5, p2), lambda: code(3, p3), lambda: code(4, p4)]
             if t == 6:
                 const(p1, "KHB", False, False)
                 mm(p1, R("IDQ"), R("SN2"), False, False)
-            const(p2, "KP2", True, False)
-            mm(p2, R("IDF"), wf, False, False)
             mm(p1, R("IDT"), R("TG"), False, False)
             mm(p1, R("IDM"), sn, False, True)
+            const(p2, "KP2", True, False)
+            mm(p2, R("IDF"), wf, False, False)
             mm(p2, R("IDT"), R("TG"), False, False)
             mm(p2, R("IDP"), sn, False, True)
-            tt(R("DF"), bre, p1, OP.min)
-            tt(bre if t == 2 else wf, R("DF"), p2, OP.max)
+            steps = [lambda: tt(R("DF"), bre, p1, OP.min), lambda: tt(bre if t == 2 else wf, R("DF"), p2, OP.max)]
             if t == 2:
-                s = R("pd", 512, 768)
-                code_sum(6, s, False)
-                const(s, "KNB", False, False)
-                mm(s, R("IDT"), R("TG"), False, False)
-                mm(s, R("IDM"), sn, False, True)
-                code(6, s)
+                code_sum(6, p3, False)
+                const(p3, "KNB", False, False)
+                mm(p3, R("IDT"), R("TG"), False, False)
+                mm(p3, R("IDM"), sn, False, True)
+                steps.append(lambda: code(6, p3))
+            return steps
+        if t == ROUNDS:
+            for step in word_sums():
+                step()
         mm(R("pn", 0, 256), R("WB"), ld, False, True)
         act(R("NN"), ld, AF.Relu, -1.0, 63.0)
+        limit[0]()
         act(R(mr, 256, 512), ld, AF.Copy)
+        limit[1]()
         act(R(mr, 512, 1024), R(mr, 0, 512), AF.Copy)
+        limit[2]()
         if t < ROUNDS:
             gcopy(R("RW", SH + 1024 + 256 * (t - 1), SH + 1280 + 256 * (t - 1)), ld, 256)
             if t < ROUNDS - 1:
                 gcopy(R("RW", AREA0 + AREAD * (t - 1), AREA0 + AREAD * (t - 1) + 256), ld, 256)
             gather(t, *PIECES[0])
+        limit[3]()
+        limit[4]()
         if t < PH:
             widen(t)
         for h in (0, 1):
@@ -534,6 +576,7 @@ def rank_program(g, core, T, topo):
             for b, s in ((0, R("pd", 1536, 2048)), (512, R("pc"))):
                 mm(s, R("IDF"), R("W", b, b + 512), True, False)
                 const(s, "K32", False, False)
+            for b, s in ((0, R("pd", 1536, 2048)), (512, R("pc"))):
                 mm(s, R("IDC"), R("AB", b, b + 512), False, True)
         scan(R("UI"), R("SEGM"), R("pn", 0, 256), OP.mult, OP.max)
         ts(R("U"), R("UI", 15, 256, 16), 4095, None, OP.bitwise_and)
@@ -543,69 +586,53 @@ def rank_program(g, core, T, topo):
         cp(R("UZ", 1, 32, 2), R("U"))
         tt(R("PI1"), IND(R("BS"), R("LLN")), R("T1"), OP.add)
         cp(R("pb", 257, 288, 2), R("BS"))
-        ts(R("PI2"), R("PI1"), 1023, None, OP.bitwise_and)
-        cp(R("POF"), R("PI2"))
-
-        def keys(m0, n, r, last=False):
-            for mc in range(m0, m0 + n):
-                for h in (0, 1):
-                    mm(R("pk", 128 * h + mc, 128 * h + 128, 16), R("X", 256 * mc + 128 * h, 256 * mc + 128 * h + 128), r, False, last and h == 1 and mc == m0 + n - 1)
-
-        def s_gather(m0):
-            o = 256 * (m0 - MV)
-            act(R("SG", o, o + 512), IND(R("SL"), R("POF", 16 * m0, 16 * m0 + 32)), AF.Copy)
-
-        def s_sub(m0):
-            o = 256 * (m0 - MV)
-            mm(R("pd", o, o + 512), R("IDN"), R("SG", o, o + 512), False, True)
-
-        def s_relu(m0):
-            o = 256 * (m0 - MV)
-            act(R("X", 256 * m0, 256 * m0 + 512), R("pd", o, o + 512), AF.Relu, 1.0, 63.0)
-
-        def v_score(m0, n):
+        words = word_sums() if t < ROUNDS else []
+        for a, b in ((16 * MV, 256), (0, 16 * MV)):
+            ts(R("PI2", a, b), R("PI1", a, b), 1023, None, OP.bitwise_and)
+        for a, b in ((16 * MV, 256), (0, 16 * MV)):
+            cp(R("POF", a, b), R("PI2", a, b))
+        for m0 in (10, 12, 14):
+            s_gather(m0)
+        for m0, n in ((0, 4), (4, 3), (7, 2), (9, 1)):
             tt(R("X", 256 * m0, 256 * (m0 + n)), IND(R("SL"), R("POF", 16 * m0, 16 * (m0 + n))), R(mr, 0, 256 * n), OP.min)
-        s_gather(10)
-        s_gather(12)
-        v_score(0, 4)
-        v_score(4, 3)
-        v_score(7, 2)
-        v_score(9, 1)
         s_sub(10)
-        s_relu(10)
-        keys(0, 4, R("O8S"))
         s_sub(12)
-        s_gather(14)
-        keys(10, 2, R("O8N"))
-        s_relu(12)
-        keys(4, 3, R("O8S"))
+        keys(0, 4, R("O8S"))
         s_sub(14)
-        s_relu(14)
-        keys(7, 2, R("O8S"))
+        for m0 in (10, 12, 14):
+            s_relu(m0)
+        keys(4, 3, R("O8S"))
+        keys(10, 2, R("O8N"))
         keys(12, 2, R("O8N"))
+        keys(7, 2, R("O8S"))
         keys(9, 1, R("O8S"))
         keys(14, 2, R("O8N"), True)
+        for step in words[:2]:
+            step()
         if t == 1:
             list_constants()
         if t < ROUNDS:
             gather(t, *PIECES[1])
-            rooms(f2, (3, 4, 5, 6))
+            rooms(f2, (3, 4))
         else:
             act(R("W", 0, 512), R("pd", 1536, 2048), AF.Copy)
             act(R("W", 512, 1024), R("pc"), AF.Copy)
-            act(R("NW"), R("NWN"), AF.Relu, 1.0, float(AREAD * t))
+            act(R("NW"), R("NWN"), AF.Relu, 1.0, AREAD * t + BIG / 2)
+            aff(R("NW"), R("NW"), 1.0, -BIG / 2)
         scan(R("KI"), R("SEGM"), R("pk", 0, 256), OP.mult, OP.max)
         ts(R("TB"), R("KI", 15, 256, 16), 1023, None, OP.bitwise_and)
+        for step in words[2:3]:
+            step()
         tt(R("EXD"), IND(R("TB"), R("LID")), R("MSKD"), OP.mult)
         for h in (0, 1):
             mm(R("pb", 256 + 16 * h, 272 + 16 * h, 2), R("EXD", 128 * h, 128 * h + 128), R("O8H"), True, True)
+        for step in words[3:]:
+            step()
         mm(R("pn", 0, 256), R("ID"), R("NEG2"), True, False)
         if t < ROUNDS:
             rooms2(f2)
             gather(t, *PIECES[2])
         scan(R("PR"), R("UZ"), R("pb", 256, 288), OP.mult, OP.add)
-        if t < ROUNDS:
-            rooms(f2, (1,))
         ts(R("PL"), R("PR", 1, 32, 2), 1023, None, OP.bitwise_and)
         cp(R("PLU"), R("PL"))
         cp(R("PLF"), R("PL"))
@@ -614,6 +641,8 @@ def rank_program(g, core, T, topo):
             act(R("POS"), IND(R("TP"), R("PLU")), AF.Abs, 1.0, -1024.0 * f2)
             gather(t, *PIECES[3])
             gather(t, *PIECES[4])
+        else:
+            act(R("DF"), IND(R("W"), R("PLU")), AF.Identity, 1.0, BIG / 2)
         o = 0
         for q in range(15):
             n = 240 - 16 * q
@@ -628,16 +657,21 @@ def rank_program(g, core, T, topo):
                     mm(R("pn", 0, 256), R("ID16"), R("POS"), False, False)
                 else:
                     mm(R("pn", 0, 256), R("IDH"), R("PB"), False, False)
+        if t < ROUNDS:
+            rooms(f2, (1,))
+        else:
+            mm(R("pd", 0, 256), R("IDM"), R("MSKD"), True, False)
+            mm(R("pd", 0, 256), R("IDF"), R("DF"), False, True)
+            act(R("TW"), R("pd", 0, 256), AF.Relu)
         scan(R("SX"), R("SEGM"), R("pn", 0, 256), OP.mult, OP.max)
         if t < ROUNDS:
-            rooms(f2, (2,))
+            rooms(f2, (2, 5, 6))
             tt(R("L4"), R("SX", 15, 256, 16), R("TRD"), OP.min)
             cp(R("LSD"), R("L4"))
             out = IND(R("DD"), R("LSD"))
             op("V", lambda: g.vector.tensor_copy(out["ap"], ld["ap"]), [out], [ld])
     tt(R("L4"), R("SX", 15, 256, 16), R("TRX2"), OP.min)
     ts(R("LST"), R("L4"), R("LNX"), None, OP.subtract)
-    tt(R("TW"), IND(R("W"), R("LST")), R("NMSK"), OP.mult)
     tt(IND(R("W"), R("LST")), R("TW"), R("NW"), OP.add)
     y = R("W", 0, 1024)
     sc["dma"]("Y", "oyb", T.yb[:], y["ap"], [], [y])

@@ -1,3 +1,4 @@
+from concourse.bass import DstId, RemoteDMATransfer
 from concourse.mybir import AluOpType, ActivationFunctionType
 import comms_topo
 
@@ -9,8 +10,12 @@ MV = 10
 SH = 16
 AREA0, AREAD = 13312, 4352
 RWN = AREA0 + AREAD * 3 + 256
-DDN = 4384
-PIECES = ((0, 40), (40, 104), (104, 152), (152, 204), (204, 256))
+DDR = 4132
+SPARE = 4 * DDR + 16
+DDN = SPARE + 384
+VROWS = (0, 8, 1)
+SUFFIX = ((0, 16), (16, 152), (152, 168), (168, 184), (184, 240), (240, 256))
+PIECES = ((0, 40), (40, 112), (112, 182), (182, 256))
 BIG = 2097152.0
 
 SCRATCH = {}
@@ -23,25 +28,25 @@ def _buf(where, dtype, *names):
 
 _buf("sbuf", B16, ("RW", RWN), ("CAPS", 1024), ("SL", 1024), ("DD", DDN), ("E1", 4096), ("E2", 4096), ("X", 4096), ("SEG", 4096), ("TABD", 4096), ("TT", 256),
      ("FL", 256), ("FR", 256), ("F2", 256), ("MN", 256), ("A1", 256), ("A2", 256), ("EX", 256), ("JK", 256), ("TG", 256), ("SN", 256), ("SN2", 256), ("NN", 256), ("POS", 256),
-     ("SG", 2048), ("EQ", 2176), ("C2", 2048), ("AB", 2560))
-_buf("sbuf", F16, ("PB", 256), ("EXD", 256), ("O8H", 8), ("IDH", 128), ("ONH", 128), ("KC", 128))
-_buf("sbuf", F32, ("W", 1280), ("BRE", 1024), ("YLE", 1024), ("DF", 256), ("T1", 256), ("SX", 256), ("S16F", 96), ("TW", 256), ("NW", 256), ("UZ", 32))
-_buf("sbuf", I32, ("BRI", 1024), ("YL", 1024), ("KB", 1024), ("KI", 256), ("S16I", 112), ("UI", 256), ("PI1", 256), ("PI2", 256), ("PR", 32), ("WTI", 1), ("KAI", 1), ("I1", 8),
+     ("SG", 2048), ("EQ", 2176), ("C2", 2048), ("AB", 2560), ("TP", 1024))
+_buf("sbuf", F16, ("PB", 256), ("EXD", 256), ("EXN", 256), ("O8H", 8), ("IDH", 128), ("ID4", 128), ("ONH", 128), ("KC", 128))
+_buf("sbuf", F32, ("W", 1408), ("BRE", 1024), ("YLE", 1024), ("DF", 256), ("T1", 256), ("SX", 256), ("S16F", 96), ("TW", 256), ("NW", 256), ("UZ", 32))
+_buf("sbuf", I32, ("BRI", 1024), ("YL", 1024), ("KB", 1024), ("KI", 256), ("S16I", 112), ("UI", 256), ("PI1", 256), ("PI2", 256), ("PR", 32), ("TI", 32), ("WTI", 1), ("KAI", 1), ("I1", 8),
      ("KRW", 128))
 _buf("sbuf", U16, ("OFFS", 256), ("IDX", 16), ("POF", 256), ("PLU", 16), ("LST", 16), ("LSD", 16), ("LID", 16), ("LLN", 16))
 _buf("sbuf", B16, ("IB", 256), ("IB15", 256), ("IB4", 256), ("MSKD", 256), ("MSK4", 256), ("NEGM", 256), ("NEG2", 256), ("BB", 128), ("BBH", 128), ("TRI", 128), ("WB", 128),
-     ("O8K", 8), ("O8S", 8), ("O8N", 8), ("O8M", 8), ("O8C", 8), ("BSM", 128), ("IDS", 1152), ("CK", 256), ("ONE", 512), ("ZR", 256), ("CV", 1024), ("CS", 256))
-_buf("sbuf", F32, ("F1", 24), ("SEGM", 256), ("KR", 256), ("KAX", 256), ("BBF", 128), ("CIX", 16), ("TRX", 16), ("TRX2", 16), ("TRD", 16), ("IDF", 128), ("O16", 128),
-     ("NWN", 256), ("IOT", 1024), ("TP", 1024))
+     ("O8K", 8), ("O8S", 8), ("O8N", 8), ("O8M", 8), ("O8C", 8), ("O8W", 8), ("BSM", 128), ("IDS", 1152), ("CK", 256), ("ONE", 512), ("ZR", 256), ("CV", 1024), ("CS", 256))
+_buf("sbuf", F32, ("F1", 24), ("SEGM", 256), ("KR", 256), ("KAX", 256), ("BBF", 128), ("CIX", 16), ("TRX", 16), ("TRD", 256), ("IDF", 128), ("O16", 128),
+     ("NWN", 256))
 _buf("psum", F32, ("pk", 512), ("pb", 512), ("pn", 512), ("pc", 512), ("pd", 2048))
 for _r in range(1, ROUNDS + 1):
-    _buf("sbuf", B16, ("MO%d" % _r, 256), ("LD%d" % _r, 1024))
-ALIAS = {n: ("F1", c, 1) for c, n in enumerate(("PIF", "LNF", "GRF", "LN16", "LNX", "WTF", "KAF", "LIM", "NLM", "FC", "SC", "H1", "H2"))}
+    _buf("sbuf", B16, ("MO%d" % _r, 512), ("LD%d" % _r, 1024))
+ALIAS = {n: ("F1", c, 1) for c, n in enumerate(("PIF", "LNF", "GRF", "LN16", "LNX", "WTF", "W16", "KAF", "LIM", "NLM", "FC", "SC", "H1", "H2"))}
 ALIAS.update({n: ("I1", c, 1) for c, n in enumerate(("PIX", "LNI", "GRI"))})
-ALIAS.update({n: ("S16I", 16 * c, 16) for c, n in enumerate(("TA", "TB", "U", "U2", "BS", "PL"))})
+ALIAS.update({n: ("S16I", 16 * c, 16) for c, n in enumerate(("TA", "UT0", "U", "U2", "BS", "PL", "UT"))})
 ALIAS.update({n: ("S16F", 16 * c, 16) for c, n in enumerate(("PLF", "L1", "L2", "L3", "L4"))})
-ALIAS.update({n: ("IDS", 128 * c, 128) for c, n in enumerate(("ID", "IDN", "IDT", "IDM", "IDP", "IDQ", "ID16", "IDC", "IDK"))})
-CONST = (("K16", 16.0), ("KP2", -BIG - 65536.0), ("KBG", BIG), ("KHB", BIG / 2), ("KNB", -BIG), ("K32", 32768.0), ("K37", 37.0), ("K1K", 1024.0))
+ALIAS.update({n: ("IDS", 128 * c, 128) for c, n in enumerate(("ID", "IDN", "IDT", "IDM", "IDP", "IDQ", "IDR", "IDC", "IDK"))})
+CONST = (("K16", 16.0), ("KP2", -BIG - 65536.0), ("KBG", BIG), ("KHB", BIG / 2), ("KNB", -BIG), ("K37", 37.0), ("K1K", 1024.0))
 ALIAS.update({n: ("CV", 128 * c, 128) for c, (n, v) in enumerate(CONST)})
 PSUM = ("pk", "pb", "pn", "pc", "pd")
 LOADS = ["lcap", "lbr", "lres", "lwt", "lka", "lkr"]
@@ -204,13 +209,13 @@ def rank_program(g, core, T, topo):
     iota(R("IB"), [[1, 256]], 0, 0)
     iota(R("IB4"), [[1, 16], [0, 16]], 0, 0)
     iota(R("CIX"), [[256, 16]], 15, 0)
-    iota(R("TRX"), [[16, 16]], 1024, 0)
-    iota(R("TRD"), [[16, 16]], 4128, 0)
+    iota(R("TRX"), [[16, 16]], 1024, 1)
     ms(R("RW", 0, SH), 0.0)
     ms(R("DD", 0, 16), 0.0)
-    ms(R("DD", 4112, DDN), 0.0)
+    for f in range(PH):
+        ms(R("DD", DDR * f + 4112, DDR * f + DDR + 16), 0.0)
     ms(R("LIM"), 4.0)
-    ms(R("NLM"), -4.0)
+    ms(R("NLM"), 8.0)
     ts(R("LNI"), R("PIX"), 15, None, OP.bitwise_and)
     ts(R("GRI"), R("PIX"), 4, None, OP.arith_shift_right)
     cp(R("PIF"), R("PIX"))
@@ -235,6 +240,7 @@ def rank_program(g, core, T, topo):
     ts(R("MSK4"), R("IB4"), R("LNF"), None, OP.is_equal)
     ts(R("LLN"), R("IB", 0, 16), 0.0, R("LNF"), OP.mult, OP.add)
     cp(R("WTF"), R("WTI"))
+    ts(R("W16"), R("WTI"), 0.0625, None, OP.mult)
     cp(R("KAF"), R("KAI"))
     cp(row("KC"), row("KRW"))
     gcopy(R("TABD", 0, 256), R("MSKD"), 256)
@@ -242,6 +248,10 @@ def rank_program(g, core, T, topo):
     def widen(f):
         for s in (0, 1):
             gcopy(R("C2", 512 * f + s, 512 * f + 512, 2), R("CAPS", f, 1024, 4), 256)
+
+    def spare_columns(base):
+        iota(R("TRD"), [[1, 256]], base, 1)
+        select(R("TRD"), R("TRD"), [[0, 16], [1, 16]], OP.is_equal, 0, 0)
 
     ts(R("pn", 0, 256), R("BRI", 0, 1024, 4), 4096.0, 8192.0 + SH, OP.is_ge, OP.mult)
     ts(R("KI"), R("BRI", 0, 1024, 4), 4095, None, OP.bitwise_and)
@@ -252,8 +262,8 @@ def rank_program(g, core, T, topo):
     widen(0)
     for n in (1024, 2048):
         gcopy(R("TABD", n, 2 * n), R("TABD", 0, n), n)
-    iota(R("W", 1024, 1280), [[0, 256]], 0, 0)
-    iota(R("ZR"), [[0, 256]], 0, 0)
+    for n, v in CONST:
+        iota(row(n), [[0, 128]], int(v), 0)
 
     def late_constants():
         aff(R("IDF"), R("ID"), 1.0)
@@ -268,16 +278,18 @@ def rank_program(g, core, T, topo):
         aff(R("BBF"), R("BB"), 1.0)
         aff(R("BSM"), R("BB"), -16384.0)
         aff(R("BBH"), R("BB"), 65536.0)
+        aff(row("CS"), row("ONE", 0, 256), 1008.0 * 16384)
+
+    def cut_constants():
+        select(row("CS"), row("CS"), [[0, 16], [1, 16]], OP.is_ge, -MV, 0)
         select(R("BSM"), R("BSM"), [[0, 8], [1, 16]], OP.is_ge, -MV, 0)
         select(R("TRI"), R("BBH"), [[1, 128]], OP.is_gt, 0, -1)
-        aff(row("CS"), row("ONE", 0, 256), 1008.0 * 16384)
-        select(row("CS"), row("CS"), [[0, 16], [1, 16]], OP.is_ge, -MV, 0)
-        for n, v in CONST:
-            aff(row(n), row("ONE", 0, 128), v)
+        iota(R("TP"), [[0, 256], [1, 4]], 0, 0)
 
     def flight_constants():
         aff(R("NEGM"), R("MSKD"), BIG, -BIG)
         aff(R("WB"), R("BB"), R("WTF"))
+        aff(R("O8W"), R("O8K"), R("W16"))
         aff(R("O8S"), R("O8K"), 1024.0)
         aff(R("O8N"), R("O8K"), -1024.0)
         aff(R("LNX"), R("LNF"), 1.0, 16.0)
@@ -285,10 +297,8 @@ def rank_program(g, core, T, topo):
         aff(R("KAX"), R("pd", 0, 256), 1.0)
 
     def list_constants():
-        aff(R("TRX"), R("TRX"), 1.0, R("LNF"))
-        aff(R("TRD"), R("TRD"), 1.0, R("LNF"))
-        aff(R("ID16"), R("ID"), 16.0)
-        aff(R("NEG2"), R("NEGM"), 16.0, R("LNX"))
+        aff(R("IDR"), R("ID"), DDR - 4.0)
+        aff(R("NEG2"), R("NEGM"), -16.0, R("LNX"))
 
     def word_constants():
         s = R("pd", 1024, 1280)
@@ -301,11 +311,13 @@ def rank_program(g, core, T, topo):
     def last_constants():
         aff(R("IDQ"), R("ID"), BIG / 2)
         aff(R("IDC"), R("ID"), -32768.0)
-        aff(R("TRX2"), R("TRX"), 1.0, R("LNX"))
 
-    def tests(t):
+    def barred(t):
         f, o = (t - 1) % PH, 512 * (t - 2)
         act(R("AB", o, o + 256), R("BRE", f, 1024, 4), AF.Relu, -4096.0, -268435456.0 * t)
+
+    def over(t):
+        f, o = (t - 1) % PH, 512 * (t - 2)
         act(R("AB", o + 256, o + 512), R("YLE", f, 1024, 4), AF.Relu, -4096.0, -16777216.0 * (528 - t))
 
     def code_sum(t, s, stop):
@@ -319,16 +331,16 @@ def rank_program(g, core, T, topo):
         tt(R("W", f, 1024, 4), R("KB", f, 1024, 4), s, OP.add)
 
     def bank(j):
-        if j in (1, 2, 7):
-            return R("pn" if j == 2 else "pb")
-        return R("pd", 512 * (j - 3), 512 * (j - 2))
+        if j < 4:
+            return R("pb" if j == 2 else "pn")
+        return R("pd", 512 * (j - 4), 512 * (j - 3))
 
     def rooms(f, js):
         for j in js:
             mm(bank(j), R("IDN"), R("C2", 512 * f, 512 * f + 512), True, False)
 
     def first_rooms():
-        for j in range(1, 7):
+        for j in range(2, 8):
             name, a, b = bank(j)["r"][0][:3]
             for s in (0, 1):
                 mm(R(name, a + s, b, 2), R("IDN"), R("CAPS", 0, 1024, 4), s == 0, False)
@@ -338,21 +350,26 @@ def rank_program(g, core, T, topo):
         mm(R("pc", 256, 512), R("IDN"), R("CAPS", f, 1024, 4), True, False)
         mm(R("pk", 0, 256), row("ONE", 0, 128), row("CK"), True, False)
         for h in (0, 1):
-            mm(R("pk", 128 * h, 128 * h + 128, 16), R("CAPS", 512 * h + f, 512 * h + 512, 4), R("O8C"), False, False)
+            for k in VROWS:
+                mm(R("pk", 128 * h + k, 128 * h + 128, 16), R("CAPS", 512 * h + f, 512 * h + 512, 4), R("O8C"), False, False)
 
-    def add_rows(j):
-        mm(bank(j), R("ID"), R("DD", 16 + j, 4112, 8), False, True)
+    def cols(f, k, step):
+        return R("DD", DDR * f + 16 + k, DDR * f + 4112, step)
+
+    def add_rows(f, j):
+        mm(bank(j), R("ID"), cols(f, j, 8), False, True)
 
     def relu(j, n):
-        act(R("X", 512 * j, 512 * (j + n)), bank(j) if n == 1 else R("pd", 512 * (j - 3), 512 * (j - 1)), AF.Relu)
+        act(R("X", 512 * j, 512 * (j + n)), bank(j) if n == 1 else R("pd", 512 * (j - 4), 512 * (j - 2)), AF.Relu)
 
     def row_keys(j, last=False):
         for h in (0, 1):
             for s in (0, 1):
                 mm(R("pk", 128 * h + j + 8 * s, 128 * h + 128, 16), R("X", 512 * j + 256 * h + s, 512 * j + 256 * h + 256, 2), R("O8K"), False, last and h + s == 2)
 
-    def suffix(a, b):
-        scan(R("E2", a, b, -1), R("DD", 17 + a, 17 + b, -1), R("SEG", 0, b - a), OP.max, OP.min)
+    def suffix(f, a, b):
+        if a < b:
+            scan(R("E2", 16 * a, 16 * b, -1), R("DD", DDR * f + 17 + 16 * a, DDR * f + 17 + 16 * b, -1), R("SEG", 0, 16 * (b - a)), OP.max, OP.min)
 
     def key_start():
         mm(R("pk", 0, 256), row("ONE", 0, 128), row("CS"), True, False)
@@ -379,7 +396,8 @@ def rank_program(g, core, T, topo):
 
     def gather(t, a, b):
         win = R("RW", 0, AREA0 + AREAD * (t - 2) + 256 if t > 1 else SH + 2304)
-        act(R("DD", 16 + 16 * a, 16 + 16 * b), IND(win, R("OFFS", a, b)), AF.Copy)
+        o = DDR * (t % PH) + 16
+        act(R("DD", o + 16 * a, o + 16 * b), IND(win, R("OFFS", a, b)), AF.Copy)
 
     sent = 0
     for t in range(1, ROUNDS + 1):
@@ -393,30 +411,33 @@ def rank_program(g, core, T, topo):
             act(R("DD", 2064, 4112), IND(win, R("OFFS", 128, 256)), AF.Copy)
             rooms2(0)
             first_rooms()
-        tt(R("X", 0, 512, 2), R("DD", 16, 4112, 16), cap_p, OP.max)
-        add_rows(1)
-        add_rows(2)
-        mm(R("pc", 256, 512), R("ID"), R("DD", 24, 4112, 16), False, True)
-        add_rows(3)
-        add_rows(4)
-        relu(1, 1)
+        for k in VROWS:
+            tt(R("X", 512 * (k % 8) + k // 8, 512 * (k % 8) + 512, 2), cols(f, k, 16), cap_p, OP.max)
+        add_rows(f, 2)
+        add_rows(f, 3)
+        add_rows(f, 4)
+        add_rows(f, 5)
+        mm(R("pc", 256, 512), R("ID"), cols(f, 9, 16), False, True)
         relu(2, 1)
-        act(R("X", 1, 512, 2), R("pc", 256, 512), AF.Relu)
-        relu(3, 2)
-        add_rows(5)
-        add_rows(6)
-        relu(5, 2)
-        row_keys(1)
-        rooms(f, (7,))
-        add_rows(7)
+        relu(3, 1)
+        relu(4, 2)
+        act(R("X", 513, 1024, 2), R("pc", 256, 512), AF.Relu)
+        add_rows(f, 6)
+        add_rows(f, 7)
+        relu(6, 1)
         relu(7, 1)
-        scan(R("E1"), R("DD", 15, 4111), R("SEG"), OP.max, OP.min)
-        suffix(0, 512)
-        tt(R("TT"), R("E1", 15, 4096, 16), R("DD", 31, 4112, 16), OP.max)
-        suffix(512, 1024)
-        tt(R("FL"), R("TT"), cap_p, OP.is_gt)
-        suffix(1024, 4096)
-        for j in (0, 2, 3, 4, 5, 6, 7):
+        mm(R("pn", 0, 256), R("ID"), cols(f, 15, 16), True, True)
+        scan(R("E1"), R("DD", DDR * f + 15, DDR * f + 4111), R("SEG"), OP.max, OP.min)
+        pieces = iter(SUFFIX)
+        suffix(f, *next(pieces))
+        tt(R("TT"), R("E1", 15, 4096, 16), R("pn", 0, 256), OP.max)
+        suffix(f, *next(pieces))
+        for j in (0, 2, 3, 4, 5, 1):
+            row_keys(j)
+        mm(R("pd", 0, 256), R("IDN"), capf, True, False)
+        mm(R("pd", 0, 256), R("ID"), R("TT"), False, True)
+        act(R("FL"), R("pd", 0, 256), AF.Sign, 1.0, -0.5)
+        for j in (6, 7):
             row_keys(j, j == 7)
         if t == 1:
             late_constants()
@@ -431,64 +452,68 @@ def rank_program(g, core, T, topo):
             late_constants2()
         if t == 2:
             word_constants()
-            tests(6)
+            barred(6)
+            over(6)
         if t == 3:
             last_constants()
         scan(R("KI"), R("SEGM"), R("pk", 0, 256), OP.mult, OP.max)
-        if t > 1:
-            ts(R("L1"), R("SX", 15, 256, 16), 65536.0, 4096.0, OP.is_ge, OP.mult)
+        suffix(f, *next(pieces))
         ts(R("TA"), R("KI", 15, 256, 16), 15, None, OP.bitwise_and)
-        if t > 1:
-            tt(R("L2"), R("L1"), R("PLF"), OP.max)
-        else:
-            ms(row("ONH"), 1.0)
+        suffix(f, *next(pieces))
         tt(R("EX"), IND(R("TA"), R("LID")), R("MSKD"), OP.mult)
         for h in (0, 1):
             mm(R("pn", 256 + 8 * h, 264 + 8 * h), R("EX", 128 * h, 128 * h + 128), R("O8M"), False, h == 1)
-        if t > 1:
-            tt(R("L3"), R("L2"), R("TRX"), OP.min)
-            cp(R("LST"), R("L3"))
-        else:
-            ts(R("O8H"), R("IB", 0, 8), R("GRF"), None, OP.is_equal)
-            cp(R("IDH"), R("ID"))
+        suffix(f, *next(pieces))
         cp(R("IDX"), R("pn", 256, 272))
+        suffix(f, *next(pieces))
         aff(R("IDT"), R("ID"), -65536.0 * (t + 4))
         if t > 1:
             key_start()
             mm(p1, R("IDF"), R("YLE", f, 1024, 4), True, False)
             mm(R("pd", 512, 768), R("ID"), capf, True, False)
             aff(R("NW"), R("NWN"), 1.0, float(AREAD * (t - 1)))
-            act(R("TW"), IND(R("W"), R("LST")), AF.Copy)
+            act(R("TW"), IND(R("W"), R("PLU")), AF.Copy)
         else:
             flight_constants()
         if t < ROUNDS:
             mm(R("pd", 1024, 1025), R("O16"), R("FC"), True, True)
             aff(R("SC"), R("pd", 1024, 1025), 1.0)
+        a2, keep, mo, ld, mr = R("MO%d" % t, 0, 256), R("MO%d" % t, 256, 512), R("A2"), R("LD%d" % t, 0, 256), "LD%d" % t
         tt(R("A1"), IND(R("E1"), R("IDX")), R("MN"), OP.max)
-        tt(R("A2"), IND(R("E2"), R("IDX")), R("A1"), OP.max)
-        tt(R("F2"), R("A2"), cap_p, OP.is_gt)
+        if t == 1:
+            ms(row("ONH"), 1.0)
+        tt(a2, IND(R("E2"), R("IDX")), R("A1"), OP.max)
+        if t > 1:
+            tt(R("L3"), R("L2"), R("TRX"), OP.min)
+        else:
+            ts(R("O8H"), R("IB", 0, 8), R("GRF"), None, OP.is_equal)
+        tt(R("F2"), a2, cap_p, OP.is_gt)
         mm(R("pn", 0, 256), R("BB"), R("F2"), True, True)
         tt(R("TG"), IND(R("TABD"), R("IDX")), R("JK"), OP.mult)
-        ts(R("pn", 0, 256), R("pn", 0, 256), R("LIM"), None, OP.is_le)
-        mo, ld, mr = R("MO%d" % t), R("LD%d" % t, 0, 256), "LD%d" % t
-        tt(mo, R("A2"), R("pn", 0, 256), OP.mult)
+        ts(keep, R("pn", 0, 256), R("LIM"), 256.0, OP.is_le, OP.mult)
         dst = T.cores[(rank + 1 + (t - 1) % 7) % 8]
         ne = len(topo.engines(core, dst))
         rid, pid, _se = topo.addr(dst)
-        sc["deps"]("G", mo["r"], [])
-        g.remote_dma(ld["ap"], mo["ap"], T.sem["arr%d" % t], T.sem["sent"], pid, rid, topo.mask(core, dst))
+        sc["deps"]("G", a2["r"] + keep["r"], [])
+        g.remote_dma_fused([RemoteDMATransfer(dst_ids=[DstId(rid=rid, pnc=pid)], dma_engine_mask=topo.mask(core, dst), remote_sem=T.sem["arr%d" % t],
+                                              srcs=[a2["ap"], keep["ap"]], dsts=[ld["ap"]], alu_op=3)], local_sem=T.sem["sent"])
         sent += ne
+        if t > 1:
+            cp(R("LST"), R("L3"))
+        else:
+            cp(R("IDH"), R("ID"))
+            ts(R("ID4"), R("ID"), 4.0, None, OP.mult)
+        tt(mo, a2, keep, OP.min)
         sc["record"]("arr%d" % t, ne, [], ld["w"], None)
         if t == 1:
-            iota(R("IOT"), [[1, 1024]], 0, 0)
-            iota(R("TP"), [[1, 256], [1024, 4]], 0, 0)
+            cut_constants()
         if 2 < t < ROUNDS:
             gcopy(R("RW", AREA0 + AREAD * (t - 3), AREA0 + AREAD * (t - 3) + 256), R("ZR"), 256)
         if t > 1:
             tt(IND(R("W"), R("LST")), R("TW"), R("NW"), OP.max)
         else:
-            ts(R("YL"), R("BRI"), 65535, None, OP.bitwise_and)
             ts(R("BRE"), R("BRI"), -65536.0, None, OP.add)
+            ts(R("YL"), R("BRI"), 65535, None, OP.bitwise_and)
             ts(R("YLE"), R("YL"), -65536.0 - BIG, None, OP.add)
             ts(R("KB"), R("BRI"), 4095, None, OP.bitwise_and)
         sn = R("SN2" if t == 2 else "SN")
@@ -497,6 +522,8 @@ def rank_program(g, core, T, topo):
             for b in (0, 512):
                 mm(R("pd", b, b + 512), R("ID"), R("CAPS", b, b + 512), True, False)
                 mm(R("pd", b, b + 512), R("IDN"), R("RW", SH + b, SH + b + 512), False, True)
+            for r in (2, 5, 3, 4):
+                barred(r)
             act(R("SL"), R("pd", 0, 1024), AF.Relu)
         else:
             mm(R("pd", 512, 768), R("IDN"), mo, False, True)
@@ -505,8 +532,10 @@ def rank_program(g, core, T, topo):
             act(sn, wf, AF.Sign, 1.0, -4095.5)
         mm(R("pn", 0, 256), R("ID"), R("NEGM"), True, False)
         mm(R("pn", 0, 256), row("K37"), row("IB"), False, False)
+        for h in (0, 1):
+            mm(R("pb", 256 + 8 * h, 264 + 8 * h), row("IB", 128 * h, 128 * h + 128), row("K37", 0, 8), h == 0, False)
         limit = [lambda: aff(R("H1"), R("SC"), 0.5, 8388608.0), lambda: aff(R("H2"), R("H1"), -2.0, 16777216.0), lambda: act(R("H1"), R("SC"), AF.Abs, 1.0, R("H2")),
-                 lambda: aff(R("LIM"), R("H1"), 1.0, 4.0), lambda: aff(R("NLM"), R("H1"), -1.0, -4.0)] if t < ROUNDS else [lambda: None] * 5
+                 lambda: aff(R("LIM"), R("H1"), 1.0, 4.0), lambda: aff(R("NLM"), R("H1"), -2.0, 8.0)] if t < ROUNDS else [lambda: None] * 5
         if t == ROUNDS:
             y = R("RW", SH, SH + 1024)
             sc["dma"]("Y", "oyr", T.yr[:], y["ap"], [], [y])
@@ -514,12 +543,12 @@ def rank_program(g, core, T, topo):
             cp(R("OFFS"), R("W", f2, 1024, 4))
         if t == 1:
             for r in (2, 5, 3, 4):
-                tests(r)
+                over(r)
             key_start()
             code_sum(2, R("pd", 512, 768), True)
             code(2, R("pd", 512, 768))
             cp(R("OFFS"), R("W", f2, 1024, 4))
-        bre, p3, p4 = R("BRE", f, 1024, 4), R("pb", 0, 256), R("pc", 256, 512)
+        bre, p3, p4 = R("BRE", f, 1024, 4), R("pb", 0, 256), R("pd", 1792, 2048)
 
         def word_sums():
             if t == 1:
@@ -548,10 +577,9 @@ def rank_program(g, core, T, topo):
                 mm(p3, R("IDM"), sn, False, True)
                 steps.append(lambda: code(6, p3))
             return steps
-        if t == ROUNDS:
-            for step in word_sums():
-                step()
         mm(R("pn", 0, 256), R("WB"), ld, False, True)
+        for h in (0, 1):
+            mm(R("pb", 256 + 8 * h, 264 + 8 * h), R(mr, 128 * h, 128 * h + 128), R("O8W"), False, h == 1)
         act(R("NN"), ld, AF.Relu, -1.0, 63.0)
         limit[0]()
         act(R(mr, 256, 512), ld, AF.Copy)
@@ -563,30 +591,32 @@ def rank_program(g, core, T, topo):
             if t < ROUNDS - 1:
                 gcopy(R("RW", AREA0 + AREAD * (t - 1), AREA0 + AREAD * (t - 1) + 256), ld, 256)
             gather(t, *PIECES[0])
+        else:
+            aff(R("NW"), R("NWN"), 1.0, float(AREAD * t))
+            aff(R("NEG2"), R("NEGM"), -16.0)
         limit[3]()
         limit[4]()
         if t < PH:
             widen(t)
+        if t == 1:
+            spare_columns(SPARE)
+            iota(R("ZR"), [[0, 256]], 0, 0)
         for h in (0, 1):
             mm(R("pk", 128 * h, 128 * h + 128), R("NN", 128 * h, 128 * h + 128), R("BSM"), False, False)
         for m in range(16 - MV):
             mm(R("pd", 256 * m, 256 * m + 256), R("IDN"), R("NN"), m % 2 == 0, False)
-        if t == ROUNDS:
-            act(R("AB", 0, 1024), R("W", 0, 1024), AF.Sign, 1.0, 0.5)
-            for b, s in ((0, R("pd", 1536, 2048)), (512, R("pc"))):
-                mm(s, R("IDF"), R("W", b, b + 512), True, False)
-                const(s, "K32", False, False)
-            for b, s in ((0, R("pd", 1536, 2048)), (512, R("pc"))):
-                mm(s, R("IDC"), R("AB", b, b + 512), False, True)
         scan(R("UI"), R("SEGM"), R("pn", 0, 256), OP.mult, OP.max)
+        cp(R("UT0"), R("pb", 256, 272))
         ts(R("U"), R("UI", 15, 256, 16), 4095, None, OP.bitwise_and)
+        ts(R("UT"), R("UT0"), 4095, None, OP.bitwise_and)
         tt(R("U2"), R("U"), R("U"), OP.mult)
         tt(R("T1"), IND(R("U"), R("LLN")), R("KAX"), OP.mult)
         ts(R("BS"), R("U2"), 5, None, OP.arith_shift_right)
-        cp(R("UZ", 1, 32, 2), R("U"))
+        tt(R("UT0"), R("UT"), R("UT"), OP.mult)
         tt(R("PI1"), IND(R("BS"), R("LLN")), R("T1"), OP.add)
-        cp(R("pb", 257, 288, 2), R("BS"))
-        words = word_sums() if t < ROUNDS else []
+        ts(R("TI", 1, 32, 2), R("UT0"), 5, None, OP.arith_shift_right)
+        words = word_sums() + [lambda: cp(R("UZ", 1, 32, 2), R("UT"))]
+        words = words[:1] + words[-1:] + words[1:-1]
         for a, b in ((16 * MV, 256), (0, 16 * MV)):
             ts(R("PI2", a, b), R("PI1", a, b), 1023, None, OP.bitwise_and)
         for a, b in ((16 * MV, 256), (0, 16 * MV)):
@@ -607,72 +637,82 @@ def rank_program(g, core, T, topo):
         keys(7, 2, R("O8S"))
         keys(9, 1, R("O8S"))
         keys(14, 2, R("O8N"), True)
-        for step in words[:2]:
+        for step in words[:3]:
             step()
+        words = words[1:]
         if t == 1:
             list_constants()
         if t < ROUNDS:
             gather(t, *PIECES[1])
-            rooms(f2, (3, 4))
+            rooms(f2, (4, 5))
         else:
-            act(R("W", 0, 512), R("pd", 1536, 2048), AF.Copy)
-            act(R("W", 512, 1024), R("pc"), AF.Copy)
-            act(R("NW"), R("NWN"), AF.Relu, 1.0, AREAD * t + BIG / 2)
-            aff(R("NW"), R("NW"), 1.0, -BIG / 2)
+            spare_columns(1024)
+            act(R("AB", 0, 1024), R("W", 0, 1024), AF.Sign, 1.0, 0.5)
+            mm(R("pn", 0, 256), R("ID"), R("NEG2"), True, False)
+            mm(R("pd", 0, 512), R("IDF"), R("W", 0, 512), True, False)
+            mm(R("pd", 512, 768), R("IDF"), R("W", 512, 768), True, False)
         scan(R("KI"), R("SEGM"), R("pk", 0, 256), OP.mult, OP.max)
-        ts(R("TB"), R("KI", 15, 256, 16), 1023, None, OP.bitwise_and)
+        ts(R("TI", 0, 32, 2), R("KI", 15, 256, 16), 1023, None, OP.bitwise_and)
         for step in words[2:3]:
             step()
-        tt(R("EXD"), IND(R("TB"), R("LID")), R("MSKD"), OP.mult)
-        for h in (0, 1):
-            mm(R("pb", 256 + 16 * h, 272 + 16 * h, 2), R("EXD", 128 * h, 128 * h + 128), R("O8H"), True, True)
+        scan(R("PR"), R("UZ"), R("TI"), OP.mult, OP.add)
         for step in words[3:]:
             step()
-        mm(R("pn", 0, 256), R("ID"), R("NEG2"), True, False)
+        ts(R("PL"), R("PR", 1, 32, 2), 1023, None, OP.bitwise_and)
         if t < ROUNDS:
+            mm(R("pn", 0, 256), R("ID"), R("NEG2"), True, False)
             rooms2(f2)
             gather(t, *PIECES[2])
-        scan(R("PR"), R("UZ"), R("pb", 256, 288), OP.mult, OP.add)
-        ts(R("PL"), R("PR", 1, 32, 2), 1023, None, OP.bitwise_and)
-        cp(R("PLU"), R("PL"))
-        cp(R("PLF"), R("PL"))
-        cp(R("PB"), IND(R("IOT"), R("PLU")))
+        pl = R("pd", 1792, 1808)
+        cp(R("EXN"), IND(R("PL"), R("LID")))
+        tt(R("EXD"), IND(R("PL"), R("LID")), R("MSKD"), OP.mult)
+        for h in (0, 1):
+            mm(R("pb", 128 * h, 128 * h + 128), R("EXN", 128 * h, 128 * h + 128), R("IDH"), True, True)
+        for h in (0, 1):
+            mm(R("pd", 1792 + 8 * h, 1800 + 8 * h), R("EXD", 128 * h, 128 * h + 128), R("O8H"), True, True)
+        cp(R("PB"), R("pb", 0, 256))
+        cp(R("PLU"), pl)
+        if t == ROUNDS:
+            mm(R("pd", 0, 512), R("IDC"), R("AB", 0, 512), False, True)
+            mm(R("pd", 768, 1024), R("IDF"), R("W", 768, 1024), False, False)
+            mm(R("pd", 512, 1024), R("IDC"), R("AB", 512, 1024), False, True)
+            mm(R("pd", 1024, 1280), R("IDM"), R("MSKD"), True, False)
+            for b in (0, 512):
+                aff(R("W", b, b + 512), R("pd", b, b + 512), 1.0, 32768.0)
         if t < ROUNDS:
-            act(R("POS"), IND(R("TP"), R("PLU")), AF.Abs, 1.0, -1024.0 * f2)
+            act(R("POS"), IND(R("TP"), R("PLU")), AF.Copy)
             gather(t, *PIECES[3])
-            gather(t, *PIECES[4])
+            mm(R("pn", 0, 256), R("ID4"), R("PB"), False, False)
         else:
-            act(R("DF"), IND(R("W"), R("PLU")), AF.Identity, 1.0, BIG / 2)
+            act(R("DF"), IND(R("W"), R("PLU")), AF.Copy)
+            mm(R("pn", 0, 256), R("IDH"), R("PB"), False, False)
         o = 0
         for q in range(15):
             n = 240 - 16 * q
-            ts(R("EQ", o, o + n), R("PB", 256 - n, 256), R("PLF", q, q + 1), None, OP.is_equal)
+            ts(R("EQ", o, o + n), R("PB", 256 - n, 256), R("PLF", q, q + 1) if q > 1 else R("pd", 1792 + q, 1793 + q), None, OP.is_equal)
             mm(R("pn", 256 - n, 256), R("BBH"), R("EQ", o, o + n), False, q == 14)
             o += n
+            if q == 0:
+                cp(R("PLF"), pl)
             if q == 2:
                 tt(R("EQ", 1920, 2176), IND(R("PLF"), R("LID")), R("PB"), OP.is_equal)
-                mm(R("pn", 0, 256), R("TRI"), R("EQ", 1920, 2176), False, False)
-            if q == 8:
                 if t < ROUNDS:
-                    mm(R("pn", 0, 256), R("ID16"), R("POS"), False, False)
-                else:
-                    mm(R("pn", 0, 256), R("IDH"), R("PB"), False, False)
+                    mm(R("pn", 0, 256), R("IDR"), R("POS"), False, False)
+                mm(R("pn", 0, 256), R("TRI"), R("EQ", 1920, 2176), False, False)
         if t < ROUNDS:
-            rooms(f2, (1,))
+            rooms(f2, (2,))
         else:
-            mm(R("pd", 0, 256), R("IDM"), R("MSKD"), True, False)
-            mm(R("pd", 0, 256), R("IDF"), R("DF"), False, True)
-            act(R("TW"), R("pd", 0, 256), AF.Relu)
-        scan(R("SX"), R("SEGM"), R("pn", 0, 256), OP.mult, OP.max)
+            mm(R("pd", 1024, 1280), R("IDF"), R("DF"), False, True)
+            act(R("TW"), R("pd", 1024, 1280), AF.Copy)
+        scan(R("SX"), R("TRD"), R("pn", 0, 256), OP.max, OP.min)
         if t < ROUNDS:
-            rooms(f2, (2, 5, 6))
-            tt(R("L4"), R("SX", 15, 256, 16), R("TRD"), OP.min)
-            cp(R("LSD"), R("L4"))
-            out = IND(R("DD"), R("LSD"))
-            op("V", lambda: g.vector.tensor_copy(out["ap"], ld["ap"]), [out], [ld])
-    tt(R("L4"), R("SX", 15, 256, 16), R("TRX2"), OP.min)
-    ts(R("LST"), R("L4"), R("LNX"), None, OP.subtract)
-    tt(IND(R("W"), R("LST")), R("TW"), R("NW"), OP.add)
+            rooms(f2, (3, 6, 7))
+            cp(R("LSD"), R("SX", 15, 256, 16))
+            ts(R("L1"), R("SX", 15, 256, 16), float(SPARE), 4096.0, OP.is_ge, OP.mult)
+            cp(IND(R("DD"), R("LSD")), ld)
+            tt(R("L2"), R("L1"), R("PLF"), OP.max)
+    cp(R("LST"), R("SX", 15, 256, 16))
+    tt(IND(R("W"), R("LST")), R("TW"), R("NW"), OP.max)
     y = R("W", 0, 1024)
     sc["dma"]("Y", "oyb", T.yb[:], y["ap"], [], [y])
     g.sync.wait_ge(T.sem.oyb, 16)

from concourse.bass import DstId, RemoteDMATransfer
from concourse.mybir import AluOpType, ActivationFunctionType
import comms_topo

OP = AluOpType
AF = ActivationFunctionType
B16, F16, F32, I32, U16 = "bfloat16", "float16", "float32", "int32", "uint16"
ROUNDS, PH = 6, 4
MV = 10
SH = 16
AREA0, AREAD = 13312, 4352
RWN = AREA0 + AREAD * 3 + 256
DDR = 4132
SPARE = 4 * DDR + 16
DDN = SPARE + 384
VROWS = (0, 8, 1)
SUFFIX = ((0, 16), (16, 152), (152, 168), (168, 184), (184, 240), (240, 256))
PIECES = ((0, 40), (40, 112), (112, 182), (182, 256))
BIG = 2097152.0

SCRATCH = {}


def _buf(where, dtype, *names):
    for n in names:
        SCRATCH[n[0]] = (where, [128, n[1]], dtype)


_buf("sbuf", B16, ("RW", RWN), ("CAPS", 1024), ("SL", 1024), ("DD", DDN), ("E1", 4096), ("E2", 4096), ("X", 4096), ("SEG", 4096), ("TABD", 4096), ("TT", 256),
     ("FL", 256), ("FR", 256), ("F2", 256), ("MN", 256), ("A1", 256), ("A2", 256), ("EX", 256), ("JK", 256), ("TG", 256), ("SN", 256), ("SN2", 256), ("NN", 256), ("POS", 256),
     ("SG", 2048), ("EQ", 2176), ("C2", 2048), ("AB", 2560), ("TP", 1024))
_buf("sbuf", F16, ("PB", 256), ("EXD", 256), ("EXN", 256), ("O8H", 8), ("IDH", 128), ("ID4", 128), ("ONH", 128), ("KC", 128))
_buf("sbuf", F32, ("W", 1408), ("BRE", 1024), ("YLE", 1024), ("DF", 256), ("T1", 256), ("SX", 256), ("S16F", 96), ("TW", 256), ("NW", 256), ("UZ", 32))
_buf("sbuf", I32, ("BRI", 1024), ("YL", 1024), ("KB", 1024), ("KI", 256), ("S16I", 112), ("UI", 256), ("PI1", 256), ("PI2", 256), ("PR", 32), ("TI", 32), ("WTI", 1), ("KAI", 1), ("I1", 8),
     ("KRW", 128))
_buf("sbuf", U16, ("OFFS", 256), ("IDX", 16), ("POF", 256), ("PLU", 16), ("LST", 16), ("LSD", 16), ("LID", 16), ("LLN", 16))
_buf("sbuf", B16, ("IB", 256), ("IB15", 256), ("IB4", 256), ("MSKD", 256), ("MSK4", 256), ("NEGM", 256), ("NEG2", 256), ("BB", 128), ("BBH", 128), ("TRI", 128), ("WB", 128),
     ("O8K", 8), ("O8S", 8), ("O8N", 8), ("O8M", 8), ("O8C", 8), ("O8W", 8), ("BSM", 128), ("IDS", 1152), ("CK", 256), ("ONE", 512), ("ZR", 256), ("CV", 1024), ("CS", 256))
_buf("sbuf", F32, ("F1", 24), ("SEGM", 256), ("KR", 256), ("KAX", 256), ("BBF", 128), ("CIX", 16), ("TRX", 16), ("TRD", 256), ("IDF", 128), ("O16", 128),
     ("NWN", 256))
_buf("psum", F32, ("pk", 512), ("pb", 512), ("pn", 512), ("pc", 512), ("pd", 2048))
for _r in range(1, ROUNDS + 1):
    _buf("sbuf", B16, ("MO%d" % _r, 512), ("LD%d" % _r, 1024))
ALIAS = {n: ("F1", c, 1) for c, n in enumerate(("PIF", "LNF", "GRF", "LN16", "LNX", "WTF", "W16", "KAF", "LIM", "NLM", "FC", "SC", "H1", "H2"))}
ALIAS.update({n: ("I1", c, 1) for c, n in enumerate(("PIX", "LNI", "GRI"))})
ALIAS.update({n: ("S16I", 16 * c, 16) for c, n in enumerate(("TA", "UT0", "U", "U2", "BS", "PL", "UT"))})
ALIAS.update({n: ("S16F", 16 * c, 16) for c, n in enumerate(("PLF", "L1", "L2", "L3", "L4"))})
ALIAS.update({n: ("IDS", 128 * c, 128) for c, n in enumerate(("ID", "IDN", "IDT", "IDM", "IDP", "IDQ", "IDR", "IDC", "IDK"))})
CONST = (("K16", 16.0), ("KP2", -BIG - 65536.0), ("KBG", BIG), ("KHB", BIG / 2), ("KNB", -BIG), ("K37", 37.0), ("K1K", 1024.0))
ALIAS.update({n: ("CV", 128 * c, 128) for c, (n, v) in enumerate(CONST)})
PSUM = ("pk", "pb", "pn", "pc", "pd")
LOADS = ["lcap", "lbr", "lres", "lwt", "lka", "lkr"]
SEMAPHORES = ["sV", "sS", "sP", "sG", "sent", "oyr", "oyb"] + LOADS + ["arr%d" % r for r in range(1, ROUNDS + 1)]


def scheduler(g, T):
    eng = {"V": g.vector, "S": g.scalar, "P": g.tensor, "G": g, "Y": g.sync}
    cnt, rec, snap = {}, {}, {}
    clk = {q: {} for q in eng}

    def ref(name, a=None, b=None, s=1, p=None):
        if name in ALIAS:
            name, o, w = ALIAS[name]
            a, b = o + (a or 0), o + (w if b is None else b)
        a = 0 if a is None else a
        b = SCRATCH[name][1][1] if b is None else b
        if s > 0:
            sl = slice(a, b, s)
        else:
            sl = slice(b - 1, a - 1 if a else None, -1)
        rows = slice(0, p) if p else slice(0, SCRATCH[name][1][0])
        x = (name, a, b, max(s, 1), a % max(s, 1))
        return {"ap": T[name][rows, sl], "r": [x], "w": [x]}

    def ind(win, off):
        return {"ap": win["ap"].indirect(off["ap"]), "r": win["r"] + off["r"], "w": win["w"], "x": off["r"]}

    def overlap(q, x, y):
        if x[0] in PSUM and q:
            return x[1] // 512 <= (y[2] - 1) // 512 and y[1] // 512 <= (x[2] - 1) // 512
        if x[3] == y[3] and x[4] != y[4]:
            return False
        return x[1] < y[2] and y[1] < x[2]

    def deps(q, reads, writes):
        need = {}
        for isw, rs in ((False, reads), (True, writes)):
            for x in rs:
                for (y, w, q2, n) in rec.get(x[0], []):
                    same = q2 == q
                    if not overlap(not same, x, y) or (same and q == "P"):
                        continue
                    if not (w or isw or (x[0] in PSUM and not same)):
                        continue
                    if need.get(q2, 0) < n:
                        need[q2] = n
        for q2 in sorted(need):
            n = need[q2]
            if clk[q].get(q2, 0) >= n:
                continue
            if any(q3 != q2 and snap.get((q3, m), {}).get(q2, 0) >= n for q3, m in need.items() if clk[q].get(q3, 0) < m):
                continue
            eng[q].wait_ge(T.sem["s" + q2] if q2 in eng else T.sem[q2], n)
        for q2, n in need.items():
            if clk[q].get(q2, 0) < n:
                clk[q][q2] = n
                for q3, m in snap.get((q2, n), {}).items():
                    if clk[q].get(q3, 0) < m:
                        clk[q][q3] = m

    def record(q, n, reads, writes, by):
        s = dict(clk[by]) if by else {}
        if q in eng:
            s[q] = max(s.get(q, 0), n - 1)
        snap[(q, n)] = s
        for x in writes:
            rec[x[0]] = [e for e in rec.get(x[0], []) if not (x[1] <= e[0][1] and e[0][2] <= x[2] and (x[3] == 1 or x[3:] == e[0][3:]))]
        for w, rs in ((False, reads), (True, writes)):
            for x in rs:
                rec.setdefault(x[0], []).append((x, w, q, n))

    def op(q, fn, outs, ins):
        reads = [x for i in ins for x in i["r"]] + [x for o in outs for x in o.get("x", [])]
        writes = [x for o in outs for x in o["w"]]
        deps(q, reads, writes)
        cnt[q] = cnt.get(q, 0) + 1
        fn().then_inc(T.sem["s" + q], 1)
        record(q, cnt[q], reads, writes, q)

    def dma(q, sem, out, in_, outs, ins):
        reads, writes = [x for i in ins for x in i["r"]], [x for o in outs for x in o["w"]]
        deps(q, reads, writes)
        eng[q].dma_start(out, in_).then_inc(T.sem[sem], 16)
        record(sem, 16, reads, writes, q)

    return {"ref": ref, "ind": ind, "op": op, "dma": dma, "deps": deps, "record": record, "cnt": cnt}


def rank_program(g, core, T, topo):
    rank = T.rank_of(core)
    if rank is None:
        return
    sc = scheduler(g, T)
    R, IND, op = sc["ref"], sc["ind"], sc["op"]

    def val(x):
        return x["ap"] if isinstance(x, dict) else x

    def tt(out, a, b, o):
        op("V", lambda: g.vector.tensor_tensor(out["ap"], a["ap"], b["ap"], o), [out], [a, b])

    def ts(out, a, s1, s2, o0, o1=None):
        ins = [a] + [s for s in (s1, s2) if isinstance(s, dict)]
        if o1 is None:
            op("V", lambda: g.vector.tensor_scalar(out["ap"], a["ap"], val(s1), None, o0), [out], ins)
        else:
            op("V", lambda: g.vector.tensor_scalar(out["ap"], a["ap"], val(s1), val(s2), o0, o1), [out], ins)

    def cp(out, a):
        op("V", lambda: g.vector.tensor_copy(out["ap"], a["ap"]), [out], [a])

    def scan(out, d0, d1, o0, o1):
        op("V", lambda: g.vector.tensor_tensor_scan(out["ap"], d0["ap"], d1["ap"], 0.0, o0, o1), [out], [d0, d1])

    def ms(out, v):
        op("V", lambda: g.vector.memset(out["ap"], v), [out], [])

    def act(out, a, f, scale=1.0, bias=0.0, acc=None):
        ins = [a] + [v for v in (scale, bias) if isinstance(v, dict)]
        if acc:
            op("S", lambda: g.scalar.activation(out["ap"], a["ap"], f, bias=val(bias), scale=val(scale), accum_out=acc["ap"]), [out, acc], ins)
        else:
            op("S", lambda: g.scalar.activation(out["ap"], a["ap"], f, bias=val(bias), scale=val(scale)), [out], ins)

    def aff(out, a, scale, bias=0.0):
        act(out, a, AF.Identity, scale, bias)

    def mm(out, l, r, start, stop):
        op("P", lambda: g.tensor.matmul(out["ap"], l["ap"], r["ap"], start, stop), [out], [l, r])

    def iota(out, pattern, base, cm):
        if SCRATCH[out["r"][0][0]][2] == I32:
            op("G", lambda: g.iota(out["ap"], pattern, base, cm), [out], [])
        else:
            op("G", lambda: g.iota(out["ap"], pattern, base, cm, allow_small_or_imprecise_dtypes=True), [out], [])

    def select(a, b, pattern, o, base, cm):
        op("G", lambda: g.affine_select(a["ap"], b["ap"], pattern, o, 0.0, base, cm), [a], [b])

    def gcopy(a, b, n):
        select(a, b, [[0, n]], OP.is_gt, 1, 0)

    def row(name, a=0, b=None):
        return R(name, a, b, 1, 1)

    def const(out, name, start, stop):
        mm(out, row(name), row("ONE", 0, out["r"][0][2] - out["r"][0][1]), start, stop)

    sc["dma"]("Y", "lbr", R("BRI")["ap"], T.br[:], [R("BRI")], [])
    x = R("RW", SH, SH + 2304)
    sc["dma"]("Y", "lres", x["ap"], T.res[:], [x], [])
    sc["dma"]("Y", "lcap", R("CAPS")["ap"], T.cap[:], [R("CAPS")], [])
    sc["dma"]("S", "lkr", row("KRW")["ap"], T.ka[:], [R("KRW")], [])
    sc["dma"]("S", "lwt", R("WTI")["ap"], T.wt[:], [R("WTI")], [])
    sc["dma"]("S", "lka", R("KAI")["ap"], T.ka[:], [R("KAI")], [])

    iota(R("PIX"), [[0, 1]], 0, 1)
    iota(R("IB15"), [[0, 16], [1, 16]], 0, 0)
    iota(R("IB"), [[1, 256]], 0, 0)
    iota(R("IB4"), [[1, 16], [0, 16]], 0, 0)
    iota(R("CIX"), [[256, 16]], 15, 0)
    iota(R("TRX"), [[16, 16]], 1024, 1)
    ms(R("RW", 0, SH), 0.0)
    ms(R("DD", 0, 16), 0.0)
    for f in range(PH):
        ms(R("DD", DDR * f + 4112, DDR * f + DDR + 16), 0.0)
    ms(R("LIM"), 4.0)
    ms(R("NLM"), 8.0)
    ts(R("LNI"), R("PIX"), 15, None, OP.bitwise_and)
    ts(R("GRI"), R("PIX"), 4, None, OP.arith_shift_right)
    cp(R("PIF"), R("PIX"))
    ms(R("UZ"), 0.0)
    ts(R("SEG", 0, 256), R("IB15"), 768.0, -256.0, OP.mult, OP.add)
    cp(R("LNF"), R("LNI"))
    cp(R("SEG", 256, 512), R("SEG", 0, 256))
    cp(R("GRF"), R("GRI"))
    cp(R("SEG", 512, 1024), R("SEG", 0, 512))
    for n in (1024, 2048):
        act(R("SEG", n, 2 * n), R("SEG", 0, n), AF.Copy)
    ts(R("MSKD"), R("IB15"), R("LNF"), None, OP.is_equal)
    ts(R("ID"), R("IB", 0, 128), R("PIF"), None, OP.is_equal)
    ts(R("O8K"), R("IB", 0, 8), R("GRF"), 16.0, OP.is_equal, OP.mult)
    ts(row("CK"), row("IB15"), -1.0, 15.0, OP.mult, OP.add)
    ms(row("ONE"), 1.0)
    ts(R("IDN"), R("ID"), -1.0, None, OP.mult)
    ts(R("O8C"), R("O8K"), -1.0, None, OP.mult)
    ts(R("SEGM"), R("IB15"), 0.0, None, OP.is_gt)
    cp(R("LID"), R("IB", 0, 16))
    ts(R("BB"), R("IB4", 0, 128), R("GRF"), None, OP.is_equal)
    ts(R("MSK4"), R("IB4"), R("LNF"), None, OP.is_equal)
    ts(R("LLN"), R("IB", 0, 16), 0.0, R("LNF"), OP.mult, OP.add)
    cp(R("WTF"), R("WTI"))
    ts(R("W16"), R("WTI"), 0.0625, None, OP.mult)
    cp(R("KAF"), R("KAI"))
    cp(row("KC"), row("KRW"))
    gcopy(R("TABD", 0, 256), R("MSKD"), 256)

    def widen(f):
        for s in (0, 1):
            gcopy(R("C2", 512 * f + s, 512 * f + 512, 2), R("CAPS", f, 1024, 4), 256)

    def spare_columns(base):
        iota(R("TRD"), [[1, 256]], base, 1)
        select(R("TRD"), R("TRD"), [[0, 16], [1, 16]], OP.is_equal, 0, 0)

    ts(R("pn", 0, 256), R("BRI", 0, 1024, 4), 4096.0, 8192.0 + SH, OP.is_ge, OP.mult)
    ts(R("KI"), R("BRI", 0, 1024, 4), 4095, None, OP.bitwise_and)
    tt(R("DF"), R("KI"), R("pn", 0, 256), OP.add)
    ts(R("OFFS"), R("DF"), -8192.0, None, OP.add)
    for n in (256, 512):
        gcopy(R("TABD", n, 2 * n), R("TABD", 0, n), n)
    widen(0)
    for n in (1024, 2048):
        gcopy(R("TABD", n, 2 * n), R("TABD", 0, n), n)
    for n, v in CONST:
        iota(row(n), [[0, 128]], int(v), 0)

    def late_constants():
        aff(R("IDF"), R("ID"), 1.0)
        aff(R("O8M"), R("O8K"), -0.0625)
        aff(R("LN16"), R("LNF"), 16.0)
        aff(R("IDK"), R("ID"), -512.0)
        aff(R("CIX"), R("CIX"), 1.0, R("LN16"))

    def late_constants2():
        aff(R("O16"), R("ID"), 0.0, 0.0625)
        aff(R("KR"), R("MSK4"), R("KAF"))
        aff(R("BBF"), R("BB"), 1.0)
        aff(R("BSM"), R("BB"), -16384.0)
        aff(R("BBH"), R("BB"), 65536.0)
        aff(row("CS"), row("ONE", 0, 256), 1008.0 * 16384)

    def cut_constants():
        select(row("CS"), row("CS"), [[0, 16], [1, 16]], OP.is_ge, -MV, 0)
        select(R("BSM"), R("BSM"), [[0, 8], [1, 16]], OP.is_ge, -MV, 0)
        select(R("TRI"), R("BBH"), [[1, 128]], OP.is_gt, 0, -1)
        iota(R("TP"), [[0, 256], [1, 4]], 0, 0)

    def flight_constants():
        aff(R("NEGM"), R("MSKD"), BIG, -BIG)
        aff(R("WB"), R("BB"), R("WTF"))
        aff(R("O8W"), R("O8K"), R("W16"))
        aff(R("O8S"), R("O8K"), 1024.0)
        aff(R("O8N"), R("O8K"), -1024.0)
        aff(R("LNX"), R("LNF"), 1.0, 16.0)
        mm(R("pd", 0, 256), R("BBF"), R("KR"), True, True)
        aff(R("KAX"), R("pd", 0, 256), 1.0)

    def list_constants():
        aff(R("IDR"), R("ID"), DDR - 4.0)
        aff(R("NEG2"), R("NEGM"), -16.0, R("LNX"))

    def word_constants():
        s = R("pd", 1024, 1280)
        mm(s, R("ID"), R("NEGM"), True, False)
        mm(s, row("ONE", 0, 128), row("IB"), False, True)
        aff(R("IDM"), R("ID"), -BIG)
        aff(R("IDP"), R("ID"), BIG)
        aff(R("NWN"), s, 1.0, float(AREA0 - AREAD))

    def last_constants():
        aff(R("IDQ"), R("ID"), BIG / 2)
        aff(R("IDC"), R("ID"), -32768.0)

    def barred(t):
        f, o = (t - 1) % PH, 512 * (t - 2)
        act(R("AB", o, o + 256), R("BRE", f, 1024, 4), AF.Relu, -4096.0, -268435456.0 * t)

    def over(t):
        f, o = (t - 1) % PH, 512 * (t - 2)
        act(R("AB", o + 256, o + 512), R("YLE", f, 1024, 4), AF.Relu, -4096.0, -16777216.0 * (528 - t))

    def code_sum(t, s, stop):
        o = 512 * (t - 2)
        const(s, "K16", True, False)
        mm(s, R("IDN"), R("AB", o, o + 256), False, False)
        mm(s, R("IDN"), R("AB", o + 256, o + 512), False, stop)

    def code(t, s):
        f = (t - 1) % PH
        tt(R("W", f, 1024, 4), R("KB", f, 1024, 4), s, OP.add)

    def bank(j):
        if j < 4:
            return R("pb" if j == 2 else "pn")
        return R("pd", 512 * (j - 4), 512 * (j - 3))

    def rooms(f, js):
        for j in js:
            mm(bank(j), R("IDN"), R("C2", 512 * f, 512 * f + 512), True, False)

    def first_rooms():
        for j in range(2, 8):
            name, a, b = bank(j)["r"][0][:3]
            for s in (0, 1):
                mm(R(name, a + s, b, 2), R("IDN"), R("CAPS", 0, 1024, 4), s == 0, False)

    def rooms2(f):
        mm(R("pc", 0, 256), R("ID"), R("CAPS", f, 1024, 4), True, True)
        mm(R("pc", 256, 512), R("IDN"), R("CAPS", f, 1024, 4), True, False)
        mm(R("pk", 0, 256), row("ONE", 0, 128), row("CK"), True, False)
        for h in (0, 1):
            for k in VROWS:
                mm(R("pk", 128 * h + k, 128 * h + 128, 16), R("CAPS", 512 * h + f, 512 * h + 512, 4), R("O8C"), False, False)

    def cols(f, k, step):
        return R("DD", DDR * f + 16 + k, DDR * f + 4112, step)

    def add_rows(f, j):
        mm(bank(j), R("ID"), cols(f, j, 8), False, True)

    def relu(j, n):
        act(R("X", 512 * j, 512 * (j + n)), bank(j) if n == 1 else R("pd", 512 * (j - 4), 512 * (j - 2)), AF.Relu)

    def row_keys(j, last=False):
        for h in (0, 1):
            for s in (0, 1):
                mm(R("pk", 128 * h + j + 8 * s, 128 * h + 128, 16), R("X", 512 * j + 256 * h + s, 512 * j + 256 * h + 256, 2), R("O8K"), False, last and h + s == 2)

    def suffix(f, a, b):
        if a < b:
            scan(R("E2", 16 * a, 16 * b, -1), R("DD", DDR * f + 17 + 16 * a, DDR * f + 17 + 16 * b, -1), R("SEG", 0, 16 * (b - a)), OP.max, OP.min)

    def key_start():
        mm(R("pk", 0, 256), row("ONE", 0, 128), row("CS"), True, False)
        mm(R("pk", 0, 256), row("K1K"), row("CK"), False, False)
        for h in (0, 1):
            mm(R("pk", 128 * h, 128 * h + 128), row("ONH"), row("KC"), False, False)

    def keys(m0, n, r, last=False):
        for mc in range(m0, m0 + n):
            for h in (0, 1):
                mm(R("pk", 128 * h + mc, 128 * h + 128, 16), R("X", 256 * mc + 128 * h, 256 * mc + 128 * h + 128), r, False, last and h == 1 and mc == m0 + n - 1)

    def s_gather(m0):
        o = 256 * (m0 - MV)
        act(R("SG", o, o + 512), IND(R("SL"), R("POF", 16 * m0, 16 * m0 + 32)), AF.Copy)

    def s_sub(m0):
        o = 256 * (m0 - MV)
        mm(R("pd", o, o + 512), R("IDN"), R("SG", o, o + 512), False, True)

    def s_relu(m0):
        o = 256 * (m0 - MV)
        act(R("X", 256 * m0, 256 * m0 + 512), R("pd", o, o + 512), AF.Relu, 1.0, 63.0)

    def gather(t, a, b):
        win = R("RW", 0, AREA0 + AREAD * (t - 2) + 256 if t > 1 else SH + 2304)
        o = DDR * (t % PH) + 16
        act(R("DD", o + 16 * a, o + 16 * b), IND(win, R("OFFS", a, b)), AF.Copy)

    sent = 0
    for t in range(1, ROUNDS + 1):
        f = (t - 1) % PH
        f2 = t % PH
        wf, capf, cap_p = R("W", f, 1024, 4), R("CAPS", f, 1024, 4), R("pc", 0, 256)
        p1, p2 = R("pd", 1536, 1792), R("pc", 0, 256)
        if t == 1:
            win = R("RW", 0, SH + 2304)
            cp(R("DD", 16, 2064), IND(win, R("OFFS", 0, 128)))
            act(R("DD", 2064, 4112), IND(win, R("OFFS", 128, 256)), AF.Copy)
            rooms2(0)
            first_rooms()
        for k in VROWS:
            tt(R("X", 512 * (k % 8) + k // 8, 512 * (k % 8) + 512, 2), cols(f, k, 16), cap_p, OP.max)
        add_rows(f, 2)
        add_rows(f, 3)
        add_rows(f, 4)
        add_rows(f, 5)
        mm(R("pc", 256, 512), R("ID"), cols(f, 9, 16), False, True)
        relu(2, 1)
        relu(3, 1)
        relu(4, 2)
        act(R("X", 513, 1024, 2), R("pc", 256, 512), AF.Relu)
        add_rows(f, 6)
        add_rows(f, 7)
        relu(6, 1)
        relu(7, 1)
        mm(R("pn", 0, 256), R("ID"), cols(f, 15, 16), True, True)
        scan(R("E1"), R("DD", DDR * f + 15, DDR * f + 4111), R("SEG"), OP.max, OP.min)
        pieces = iter(SUFFIX)
        suffix(f, *next(pieces))
        tt(R("TT"), R("E1", 15, 4096, 16), R("pn", 0, 256), OP.max)
        suffix(f, *next(pieces))
        for j in (0, 2, 3, 4, 5, 1):
            row_keys(j)
        mm(R("pd", 0, 256), R("IDN"), capf, True, False)
        mm(R("pd", 0, 256), R("ID"), R("TT"), False, True)
        act(R("FL"), R("pd", 0, 256), AF.Sign, 1.0, -0.5)
        for j in (6, 7):
            row_keys(j, j == 7)
        if t == 1:
            late_constants()
        mm(R("pd", 512, 768), R("BB"), R("FL"), True, True)
        act(R("FR"), R("pd", 512, 768), AF.Relu, 1.0, R("NLM"))
        mm(R("pn", 256, 272), R("IDF"), R("CIX"), True, False)
        mm(R("pd", 0, 256), R("ID"), R("TT"), True, False)
        mm(R("pd", 0, 256), R("IDK"), R("FR"), False, True)
        act(R("MN"), R("pd", 0, 256), AF.Copy)
        act(R("JK"), R("FR"), AF.Sign, acc=R("FC") if t < ROUNDS else None)
        if t == 1:
            late_constants2()
        if t == 2:
            word_constants()
            barred(6)
            over(6)
        if t == 3:
            last_constants()
        scan(R("KI"), R("SEGM"), R("pk", 0, 256), OP.mult, OP.max)
        suffix(f, *next(pieces))
        ts(R("TA"), R("KI", 15, 256, 16), 15, None, OP.bitwise_and)
        suffix(f, *next(pieces))
        tt(R("EX"), IND(R("TA"), R("LID")), R("MSKD"), OP.mult)
        for h in (0, 1):
            mm(R("pn", 256 + 8 * h, 264 + 8 * h), R("EX", 128 * h, 128 * h + 128), R("O8M"), False, h == 1)
        suffix(f, *next(pieces))
        cp(R("IDX"), R("pn", 256, 272))
        suffix(f, *next(pieces))
        aff(R("IDT"), R("ID"), -65536.0 * (t + 4))
        if t > 1:
            key_start()
            mm(p1, R("IDF"), R("YLE", f, 1024, 4), True, False)
            mm(R("pd", 512, 768), R("ID"), capf, True, False)
            aff(R("NW"), R("NWN"), 1.0, float(AREAD * (t - 1)))
            act(R("TW"), IND(R("W"), R("PLU")), AF.Copy)
        else:
            flight_constants()
        if t < ROUNDS:
            mm(R("pd", 1024, 1025), R("O16"), R("FC"), True, True)
            aff(R("SC"), R("pd", 1024, 1025), 1.0)
        a2, keep, mo, ld, mr = R("MO%d" % t, 0, 256), R("MO%d" % t, 256, 512), R("A2"), R("LD%d" % t, 0, 256), "LD%d" % t
        tt(R("A1"), IND(R("E1"), R("IDX")), R("MN"), OP.max)
        if t == 1:
            ms(row("ONH"), 1.0)
        tt(a2, IND(R("E2"), R("IDX")), R("A1"), OP.max)
        if t > 1:
            tt(R("L3"), R("L2"), R("TRX"), OP.min)
        else:
            ts(R("O8H"), R("IB", 0, 8), R("GRF"), None, OP.is_equal)
        tt(R("F2"), a2, cap_p, OP.is_gt)
        mm(R("pn", 0, 256), R("BB"), R("F2"), True, True)
        tt(R("TG"), IND(R("TABD"), R("IDX")), R("JK"), OP.mult)
        ts(keep, R("pn", 0, 256), R("LIM"), 256.0, OP.is_le, OP.mult)
        dst = T.cores[(rank + 1 + (t - 1) % 7) % 8]
        ne = len(topo.engines(core, dst))
        rid, pid, _se = topo.addr(dst)
        sc["deps"]("G", a2["r"] + keep["r"], [])
        g.remote_dma_fused([RemoteDMATransfer(dst_ids=[DstId(rid=rid, pnc=pid)], dma_engine_mask=topo.mask(core, dst), remote_sem=T.sem["arr%d" % t],
                                              srcs=[a2["ap"], keep["ap"]], dsts=[ld["ap"]], alu_op=3)], local_sem=T.sem["sent"])
        sent += ne
        if t > 1:
            cp(R("LST"), R("L3"))
        else:
            cp(R("IDH"), R("ID"))
            ts(R("ID4"), R("ID"), 4.0, None, OP.mult)
        tt(mo, a2, keep, OP.min)
        sc["record"]("arr%d" % t, ne, [], ld["w"], None)
        if t == 1:
            cut_constants()
        if 2 < t < ROUNDS:
            gcopy(R("RW", AREA0 + AREAD * (t - 3), AREA0 + AREAD * (t - 3) + 256), R("ZR"), 256)
        if t > 1:
            tt(IND(R("W"), R("LST")), R("TW"), R("NW"), OP.max)
        else:
            ts(R("BRE"), R("BRI"), -65536.0, None, OP.add)
            ts(R("YL"), R("BRI"), 65535, None, OP.bitwise_and)
            ts(R("YLE"), R("YL"), -65536.0 - BIG, None, OP.add)
            ts(R("KB"), R("BRI"), 4095, None, OP.bitwise_and)
        sn = R("SN2" if t == 2 else "SN")
        if t == 1:
            act(R("RW", SH + f, SH + 1024, 4), mo, AF.Copy)
            for b in (0, 512):
                mm(R("pd", b, b + 512), R("ID"), R("CAPS", b, b + 512), True, False)
                mm(R("pd", b, b + 512), R("IDN"), R("RW", SH + b, SH + b + 512), False, True)
            for r in (2, 5, 3, 4):
                barred(r)
            act(R("SL"), R("pd", 0, 1024), AF.Relu)
        else:
            mm(R("pd", 512, 768), R("IDN"), mo, False, True)
            act(R("SL", f, 1024, 4), R("pd", 512, 768), AF.Relu)
            act(R("RW", SH + f, SH + 1024, 4), mo, AF.Copy)
            act(sn, wf, AF.Sign, 1.0, -4095.5)
        mm(R("pn", 0, 256), R("ID"), R("NEGM"), True, False)
        mm(R("pn", 0, 256), row("K37"), row("IB"), False, False)
        for h in (0, 1):
            mm(R("pb", 256 + 8 * h, 264 + 8 * h), row("IB", 128 * h, 128 * h + 128), row("K37", 0, 8), h == 0, False)
        limit = [lambda: aff(R("H1"), R("SC"), 0.5, 8388608.0), lambda: aff(R("H2"), R("H1"), -2.0, 16777216.0), lambda: act(R("H1"), R("SC"), AF.Abs, 1.0, R("H2")),
                 lambda: aff(R("LIM"), R("H1"), 1.0, 4.0), lambda: aff(R("NLM"), R("H1"), -2.0, 8.0)] if t < ROUNDS else [lambda: None] * 5
        if t == ROUNDS:
            y = R("RW", SH, SH + 1024)
            sc["dma"]("Y", "oyr", T.yr[:], y["ap"], [], [y])
        if 1 < t < ROUNDS:
            cp(R("OFFS"), R("W", f2, 1024, 4))
        if t == 1:
            for r in (2, 5, 3, 4):
                over(r)
            key_start()
            code_sum(2, R("pd", 512, 768), True)
            code(2, R("pd", 512, 768))
            cp(R("OFFS"), R("W", f2, 1024, 4))
        bre, p3, p4 = R("BRE", f, 1024, 4), R("pb", 0, 256), R("pd", 1792, 2048)

        def word_sums():
            if t == 1:
                mm(p1, R("IDF"), R("YLE", f, 1024, 4), True, False)
                mm(p1, R("IDT"), R("TG"), False, False)
                const(p1, "KBG", False, True)
                code_sum(5, p2, False)
                mm(p2, R("IDT"), R("TG"), False, True)
                code_sum(3, p3, True)
                code_sum(4, p4, True)
                return [lambda: tt(bre, bre, p1, OP.min), lambda: code(5, p2), lambda: code(3, p3), lambda: code(4, p4)]
            if t == 6:
                const(p1, "KHB", False, False)
                mm(p1, R("IDQ"), R("SN2"), False, False)
            mm(p1, R("IDT"), R("TG"), False, False)
            mm(p1, R("IDM"), sn, False, True)
            const(p2, "KP2", True, False)
            mm(p2, R("IDF"), wf, False, False)
            mm(p2, R("IDT"), R("TG"), False, False)
            mm(p2, R("IDP"), sn, False, True)
            steps = [lambda: tt(R("DF"), bre, p1, OP.min), lambda: tt(bre if t == 2 else wf, R("DF"), p2, OP.max)]
            if t == 2:
                code_sum(6, p3, False)
                const(p3, "KNB", False, False)
                mm(p3, R("IDT"), R("TG"), False, False)
                mm(p3, R("IDM"), sn, False, True)
                steps.append(lambda: code(6, p3))
            return steps
        mm(R("pn", 0, 256), R("WB"), ld, False, True)
        for h in (0, 1):
            mm(R("pb", 256 + 8 * h, 264 + 8 * h), R(mr, 128 * h, 128 * h + 128), R("O8W"), False, h == 1)
        act(R("NN"), ld, AF.Relu, -1.0, 63.0)
        limit[0]()
        act(R(mr, 256, 512), ld, AF.Copy)
        limit[1]()
        act(R(mr, 512, 1024), R(mr, 0, 512), AF.Copy)
        limit[2]()
        if t < ROUNDS:
            gcopy(R("RW", SH + 1024 + 256 * (t - 1), SH + 1280 + 256 * (t - 1)), ld, 256)
            if t < ROUNDS - 1:
                gcopy(R("RW", AREA0 + AREAD * (t - 1), AREA0 + AREAD * (t - 1) + 256), ld, 256)
            gather(t, *PIECES[0])
        else:
            aff(R("NW"), R("NWN"), 1.0, float(AREAD * t))
            aff(R("NEG2"), R("NEGM"), -16.0)
        limit[3]()
        limit[4]()
        if t < PH:
            widen(t)
        if t == 1:
            spare_columns(SPARE)
            iota(R("ZR"), [[0, 256]], 0, 0)
        for h in (0, 1):
            mm(R("pk", 128 * h, 128 * h + 128), R("NN", 128 * h, 128 * h + 128), R("BSM"), False, False)
        for m in range(16 - MV):
            mm(R("pd", 256 * m, 256 * m + 256), R("IDN"), R("NN"), m % 2 == 0, False)
        scan(R("UI"), R("SEGM"), R("pn", 0, 256), OP.mult, OP.max)
        cp(R("UT0"), R("pb", 256, 272))
        ts(R("U"), R("UI", 15, 256, 16), 4095, None, OP.bitwise_and)
        ts(R("UT"), R("UT0"), 4095, None, OP.bitwise_and)
        tt(R("U2"), R("U"), R("U"), OP.mult)
        tt(R("T1"), IND(R("U"), R("LLN")), R("KAX"), OP.mult)
        ts(R("BS"), R("U2"), 5, None, OP.arith_shift_right)
        tt(R("UT0"), R("UT"), R("UT"), OP.mult)
        tt(R("PI1"), IND(R("BS"), R("LLN")), R("T1"), OP.add)
        ts(R("TI", 1, 32, 2), R("UT0"), 5, None, OP.arith_shift_right)
        words = word_sums() + [lambda: cp(R("UZ", 1, 32, 2), R("UT"))]
        words = words[:1] + words[-1:] + words[1:-1]
        for a, b in ((16 * MV, 256), (0, 16 * MV)):
            ts(R("PI2", a, b), R("PI1", a, b), 1023, None, OP.bitwise_and)
        for a, b in ((16 * MV, 256), (0, 16 * MV)):
            cp(R("POF", a, b), R("PI2", a, b))
        for m0 in (10, 12, 14):
            s_gather(m0)
        for m0, n in ((0, 4), (4, 3), (7, 2), (9, 1)):
            tt(R("X", 256 * m0, 256 * (m0 + n)), IND(R("SL"), R("POF", 16 * m0, 16 * (m0 + n))), R(mr, 0, 256 * n), OP.min)
        s_sub(10)
        s_sub(12)
        keys(0, 4, R("O8S"))
        s_sub(14)
        for m0 in (10, 12, 14):
            s_relu(m0)
        keys(4, 3, R("O8S"))
        keys(10, 2, R("O8N"))
        keys(12, 2, R("O8N"))
        keys(7, 2, R("O8S"))
        keys(9, 1, R("O8S"))
        keys(14, 2, R("O8N"), True)
        for step in words[:3]:
            step()
        words = words[1:]
        if t == 1:
            list_constants()
        if t < ROUNDS:
            gather(t, *PIECES[1])
            rooms(f2, (4, 5))
        else:
            spare_columns(1024)
            act(R("AB", 0, 1024), R("W", 0, 1024), AF.Sign, 1.0, 0.5)
            mm(R("pn", 0, 256), R("ID"), R("NEG2"), True, False)
            mm(R("pd", 0, 512), R("IDF"), R("W", 0, 512), True, False)
            mm(R("pd", 512, 768), R("IDF"), R("W", 512, 768), True, False)
        scan(R("KI"), R("SEGM"), R("pk", 0, 256), OP.mult, OP.max)
        ts(R("TI", 0, 32, 2), R("KI", 15, 256, 16), 1023, None, OP.bitwise_and)
        for step in words[2:3]:
            step()
        scan(R("PR"), R("UZ"), R("TI"), OP.mult, OP.add)
        for step in words[3:]:
            step()
        ts(R("PL"), R("PR", 1, 32, 2), 1023, None, OP.bitwise_and)
        if t < ROUNDS:
            mm(R("pn", 0, 256), R("ID"), R("NEG2"), True, False)
            rooms2(f2)
            gather(t, *PIECES[2])
        pl = R("pd", 1792, 1808)
        cp(R("EXN"), IND(R("PL"), R("LID")))
        tt(R("EXD"), IND(R("PL"), R("LID")), R("MSKD"), OP.mult)
        for h in (0, 1):
            mm(R("pb", 128 * h, 128 * h + 128), R("EXN", 128 * h, 128 * h + 128), R("IDH"), True, True)
        for h in (0, 1):
            mm(R("pd", 1792 + 8 * h, 1800 + 8 * h), R("EXD", 128 * h, 128 * h + 128), R("O8H"), True, True)
        cp(R("PB"), R("pb", 0, 256))
        cp(R("PLU"), pl)
        if t == ROUNDS:
            mm(R("pd", 0, 512), R("IDC"), R("AB", 0, 512), False, True)
            mm(R("pd", 768, 1024), R("IDF"), R("W", 768, 1024), False, False)
            mm(R("pd", 512, 1024), R("IDC"), R("AB", 512, 1024), False, True)
            mm(R("pd", 1024, 1280), R("IDM"), R("MSKD"), True, False)
            for b in (0, 512):
                aff(R("W", b, b + 512), R("pd", b, b + 512), 1.0, 32768.0)
        if t < ROUNDS:
            act(R("POS"), IND(R("TP"), R("PLU")), AF.Copy)
            gather(t, *PIECES[3])
            mm(R("pn", 0, 256), R("ID4"), R("PB"), False, False)
        else:
            act(R("DF"), IND(R("W"), R("PLU")), AF.Copy)
            mm(R("pn", 0, 256), R("IDH"), R("PB"), False, False)
        o = 0
        for q in range(15):
            n = 240 - 16 * q
            ts(R("EQ", o, o + n), R("PB", 256 - n, 256), R("PLF", q, q + 1) if q > 1 else R("pd", 1792 + q, 1793 + q), None, OP.is_equal)
            mm(R("pn", 256 - n, 256), R("BBH"), R("EQ", o, o + n), False, q == 14)
            o += n
            if q == 0:
                cp(R("PLF"), pl)
            if q == 2:
                tt(R("EQ", 1920, 2176), IND(R("PLF"), R("LID")), R("PB"), OP.is_equal)
                if t < ROUNDS:
                    mm(R("pn", 0, 256), R("IDR"), R("POS"), False, False)
                mm(R("pn", 0, 256), R("TRI"), R("EQ", 1920, 2176), False, False)
        if t < ROUNDS:
            rooms(f2, (2,))
        else:
            mm(R("pd", 1024, 1280), R("IDF"), R("DF"), False, True)
            act(R("TW"), R("pd", 1024, 1280), AF.Copy)
        scan(R("SX"), R("TRD"), R("pn", 0, 256), OP.max, OP.min)
        if t < ROUNDS:
            rooms(f2, (3, 6, 7))
            cp(R("LSD"), R("SX", 15, 256, 16))
            ts(R("L1"), R("SX", 15, 256, 16), float(SPARE), 4096.0, OP.is_ge, OP.mult)
            cp(IND(R("DD"), R("LSD")), ld)
            tt(R("L2"), R("L1"), R("PLF"), OP.max)
    cp(R("LST"), R("SX", 15, 256, 16))
    tt(IND(R("W"), R("LST")), R("TW"), R("NW"), OP.max)
    y = R("W", 0, 1024)
    sc["dma"]("Y", "oyb", T.yb[:], y["ap"], [], [y])
    g.sync.wait_ge(T.sem.oyb, 16)
    g.sync.wait_ge(T.sem.oyr, 16)
    for q in ("V", "S", "P", "G"):
        g.wait_ge(T.sem["s" + q], sc["cnt"][q])
    g.wait_ge(T.sem.sent, sent)
    for s in LOADS:
        g.wait_ge(T.sem[s], 16)
